import numpy as np
import ml_dtypes


def mxq(x, axis, fmt="e4m3"):
    dtype, down = {"e4m3": (ml_dtypes.float8_e4m3fn, 7), "e5m2": (ml_dtypes.float8_e5m2, 14)}[fmt]
    v = np.moveaxis(np.asarray(x, np.float32).astype(ml_dtypes.bfloat16).astype(np.float64), axis, -1)
    blocks = v.reshape(v.shape[:-1] + (-1, 32))
    amax = np.abs(blocks).max(-1, keepdims=True)
    byte = np.maximum(np.where(amax > 0, np.frexp(amax)[1] - 1 + 127, 0) - down, 1)
    scale = np.exp2(byte - 127.0)
    codes = (blocks / scale).astype(np.float32).astype(dtype).astype(np.float64)
    return np.moveaxis((codes * scale).reshape(v.shape), -1, axis)


WIDE = False


def mx_kscale(k):
    if not WIDE:
        return np.ones(k)
    levels = np.array([10, -10, 5, -5, 0])
    if k % 512:
        return np.exp2(np.random.permutation(np.resize(levels, k // 32))).repeat(32)
    a = np.empty((k // 512, 16))
    for p in range(k // 512):
        a[p, :8] = np.random.permutation(np.resize(levels, 8))
        for g in range(8):
            far = levels[np.abs(levels - a[p, g]) >= 10]
            a[p, g + 8] = far[np.random.randint(len(far))]
    return np.exp2(a.ravel()).repeat(32)


def f64(x):
    return np.asarray(x).astype(np.float64)


def striped(idx):
    return np.tile(idx.reshape(-1, 16).T, (8, 1)).astype(np.uint16)


def unstriped(offs):
    return offs[:16].T.reshape(-1).astype(np.int64)


def silu(v):
    return v / (1.0 + np.exp(-np.maximum(v, -700.0)))


K, T, E, C, H, N = 512, 2048, 4, 256, 512, 256


def by_expert(wq, xq):
    return np.concatenate([wq[e].T @ xq[:, e * C:(e + 1) * C] for e in range(E)], axis=1)


def setup_inputs():
    n = np.random.standard_normal
    s = mx_kscale(K)[:, None]
    u = mx_kscale(H)
    return {
        "xT": (n((K, T)) * s).astype(np.float32),
        "w1": (n((E, K, H)) / np.sqrt(K) / s[None]).astype(np.float32),
        "w3": (n((E, K, H)) / np.sqrt(K) / s[None] * u[None, None, :]).astype(np.float32),
        "w2": (n((E, H, N)) / np.sqrt(H) / u[None, :, None]).astype(np.float32),
        "gate": np.tile(np.random.uniform(0.2, 1.0, E * C), (N, 1)).astype(np.float32),
        "offs": striped(np.random.permutation(T)[:E * C]),
        "dst": striped(np.random.permutation(T)[:E * C]),
    }


def reference(xT, w1, w3, w2, gate, offs, dst):
    idx = unstriped(offs)
    xq = mxq(f64(xT)[:, idx], 0, "e4m3")
    h = silu(by_expert(mxq(f64(w1), 1, "e4m3"), xq))
    h = h * by_expert(mxq(f64(w3), 1, "e4m3"), xq)
    y = by_expert(mxq(f64(w2), 1, "e4m3"), mxq(h, 0, "e4m3"))
    out = np.zeros((N, T))
    out[:, unstriped(dst)] = f64(gate) * y
    return out

@@ -1,0 +1,226 @@
+from contextlib import ExitStack
+
+import concourse.mybir as mybir
+
+K, T, E, C, H, N = 512, 2048, 4, 256, 512, 256
+FLOPS = 2 * E * C * (2 * K * H + H * N)
+
+F32 = mybir.dt.float32
+BF16 = mybir.dt.bfloat16
+U32 = mybir.dt.uint32
+I32 = mybir.dt.int32
+U16 = mybir.dt.uint16
+U8 = mybir.dt.uint8
+FP8X4 = mybir.dt.float8_e4m3fn_x4
+COPY = mybir.ActivationFunctionType.Copy
+SILU = mybir.ActivationFunctionType.Silu
+MULT = mybir.AluOpType.mult
+
+P = 128
+PACK = 4
+RUN = 4
+X_CHUNKS = (256, 512, 512, 512, 256)
+W1_VECTOR = (0, 0, 0, H)
+W3_VECTOR = (0, 0, 0, 0)
+HALF = 128
+LIST_COLS = C // 16
+
+
+def split(nc, out, in_, at, total):
+    if at > 0:
+        nc.vector.tensor_copy(out=out(0, at), in_=in_(0, at))
+    if at < total:
+        nc.scalar.activation(out=out(at, total), in_=in_(at, total), func=COPY)
+
+
+def tile_moe_two_glu_silu_kernel(tc, xT, w1, w3, w2, gate, offs, dst, out):
+    nc = tc.nc
+    with ExitStack() as ctx:
+        keep = ctx.enter_context(tc.tile_pool(name="keep", bufs=1))
+        load = ctx.enter_context(tc.tile_pool(name="load", bufs=2))
+        cast = ctx.enter_context(tc.tile_pool(name="cast", bufs=2))
+        codes = ctx.enter_context(tc.tile_pool(name="codes", bufs=4))
+        hid = ctx.enter_context(tc.tile_pool(name="hid", bufs=3))
+        psum = ctx.enter_context(tc.psum_pool(name="psum", bufs=3))
+        psum_y = ctx.enter_context(tc.psum_pool(name="psum_y", bufs=2))
+
+        offs_sb = keep.tile([P, E * LIST_COLS], U16, name="offs_sb")
+        dst_sb = keep.tile([P, E * LIST_COLS], U16, name="dst_sb")
+        warm = keep.tile([P, 1], F32, name="warm")
+        windows = [keep.tile([P, T], F32, name=f"window{b}") for b in range(N // P)]
+        x_codes = keep.tile([P, T], U32, name="x_codes", align_bytes=64)
+        x_scales = keep.tile([P, T], U8, name="x_scales", align_bytes=64)
+        gates = [keep.tile([P, N // P, 2 * C], F32, name=f"gates{g}") for g in range(E // 2)]
+
+        def load_gate(g):
+            cols = slice(g * 2 * C, (g + 1) * 2 * C)
+            nc.sync.dma_start(out=gates[g][:], in_=gate[:, cols].rearrange("(b p) s -> p b s", p=P))
+
+        x_cols = [slice(sum(X_CHUNKS[:c]), sum(X_CHUNKS[:c + 1])) for c in range(len(X_CHUNKS))]
+        x_raw = []
+        for c, cols in enumerate(x_cols):
+            raw = keep.tile([P, PACK, X_CHUNKS[c]], F32, name=f"x_raw{c}")
+            nc.sync.dma_start(out=raw[:], in_=xT[:, cols].rearrange("(p j) t -> p j t", j=PACK))
+            x_raw.append(raw)
+            if c == 0:
+                nc.sync.dma_start(offs_sb[:], offs)
+
+        def load_weights(e):
+            tiles = {}
+            for name, w, width in (("w1", w1, H), ("w3", w3, H), ("w2", w2, N)):
+                if name == "w2" and e == E - 1:
+                    load_gate(E // 2 - 1)
+                tiles[name] = load.tile([P, PACK, width], F32, name=f"{name}_raw")
+                nc.sync.dma_start(out=tiles[name][:], in_=w[e].rearrange("(p j) n -> p j n", j=PACK))
+            if e == 0:
+                nc.sync.dma_start(dst_sb[:], dst)
+                load_gate(0)
+            return tiles
+
+        raws = [load_weights(0), load_weights(1)]
+
+        nc.vector.memset(warm[:], 0.0)
+        nc.scalar.activation(out=warm[:], in_=warm[:], func=SILU)
+        nc.gpsimd.memset(x_scales[:].bitcast(I32), 0)
+        nc.vector.memset(windows[0][:], 0.0)
+        nc.gpsimd.memset(windows[1][:], 0.0)
+
+        for c, cols in enumerate(x_cols):
+            x_bf = keep.tile([P, X_CHUNKS[c] * PACK], BF16, name=f"x_bf{c}", align_bytes=64)
+
+            def dst_view(a, b):
+                return x_bf[:, a * PACK:b * PACK].rearrange("p (c i j) -> p c j i", i=RUN, j=PACK)
+
+            def src_view(a, b):
+                return x_raw[c][:, :, a:b].rearrange("p j (c i) -> p c j i", i=RUN)
+
+            split(nc, dst_view, src_view, X_CHUNKS[c] // 2, X_CHUNKS[c])
+            nc.vector.quantize_mx(out=x_codes[:, cols].bitcast(FP8X4), scales=x_scales[:, cols], in_=x_bf[:])
+
+        def gather(e0, e1):
+            at = slice(e0 * LIST_COLS, e1 * LIST_COLS)
+            words = keep.tile([P, (e1 - e0) * C], U32, name=f"slot_codes{e0}", align_bytes=64)
+            planes = keep.tile([P, (e1 - e0) * C], U8, name=f"slot_scales{e0}", align_bytes=64)
+            nc.vector.tensor_copy(out=words[:], in_=x_codes[:].indirect(offs_sb[:, at]))
+            nc.vector.tensor_copy(out=planes[:], in_=x_scales[:].indirect(offs_sb[:, at]))
+            for e in range(e0, e1):
+                slots[e] = (words, planes, (e - e0) * C)
+
+        def quantize_first(name, raw, at):
+            bf = cast.tile([P, PACK, H // PACK, PACK], BF16, name=f"{name}_bf", align_bytes=64)
+            out_codes = codes.tile([P, H], U32, name=f"{name}_codes", align_bytes=64)
+            out_scales = codes.tile([P, H], U8, name=f"{name}_scales", align_bytes=64)
+
+            def dst_view(a, b):
+                return bf[:, :, a // PACK:b // PACK, :].rearrange("p t m j -> p m j t")
+
+            def src_view(a, b):
+                return raw[:, :, a:b].rearrange("p j (m t) -> p m j t", t=PACK)
+
+            split(nc, dst_view, src_view, at, H)
+            nc.vector.quantize_mx(out=out_codes[:].bitcast(FP8X4), scales=out_scales[:], in_=bf[:].rearrange("p t m j -> p (t m j)"))
+            return out_codes, out_scales
+
+        def first_product(bank_name, slots, weights):
+            banks = []
+            for s in range(C // HALF):
+                cols = slice(slots[2] + s * HALF, slots[2] + (s + 1) * HALF)
+                bank = psum.tile([P, PACK, HALF], F32, name=bank_name)
+                for t in range(PACK):
+                    w_cols = slice(t * P, (t + 1) * P)
+                    nc.tensor.matmul_mx(
+                        out=bank[:, t, :],
+                        lhsT=weights[0][:, w_cols].bitcast(FP8X4),
+                        lhsT_scale=weights[1][:, w_cols],
+                        rhs=slots[0][:, cols].bitcast(FP8X4),
+                        rhs_scale=slots[1][:, cols],
+                        start=True,
+                        stop=True,
+                    )
+                banks.append(bank)
+            return banks
+
+        def activate(a_banks):
+            acts = []
+            for bank in a_banks:
+                act = hid.tile([P, HALF, PACK], F32, name="act", bufs=4)
+                nc.scalar.activation(out=act[:], in_=bank[:].rearrange("p t c -> p c t"), func=SILU)
+                acts.append(act)
+            return acts
+
+        def second_operands(acts, b_banks, w2_raw):
+            bf = hid.tile([P, N + C, PACK], BF16, name="second_bf", align_bytes=64)
+            out_codes = hid.tile([P, N + C], U32, name="second_codes", align_bytes=64)
+            out_scales = hid.tile([P, N + C], U8, name="second_scales", align_bytes=64)
+            nc.scalar.activation(
+                out=bf[:, :N, :].rearrange("p (c i) j -> p c j i", i=RUN),
+                in_=w2_raw[:].rearrange("p j (c i) -> p c j i", i=RUN),
+                func=COPY,
+            )
+            for s, bank in enumerate(b_banks):
+                cols = slice(N + s * HALF, N + (s + 1) * HALF)
+                nc.vector.tensor_tensor(out=bf[:, cols, :], in0=acts[s][:], in1=bank[:].rearrange("p t c -> p c t"), op=MULT)
+            nc.vector.quantize_mx(out=out_codes[:].bitcast(FP8X4), scales=out_scales[:], in_=bf[:].rearrange("p c t -> p (c t)"))
+            return out_codes, out_scales
+
+        def project(second):
+            y_bank = psum_y.tile([P, N // P, C], F32, name="y_bank")
+            for b in range(N // P):
+                w_cols = slice(b * P, (b + 1) * P)
+                nc.tensor.matmul_mx(
+                    out=y_bank[:, b, :],
+                    lhsT=second[0][:, w_cols].bitcast(FP8X4),
+                    lhsT_scale=second[1][:, w_cols],
+                    rhs=second[0][:, N:].bitcast(FP8X4),
+                    rhs_scale=second[1][:, N:],
+                    start=True,
+                    stop=True,
+                )
+            return y_bank
+
+        def copy_out(y_bank, last):
+            y = hid.tile([P, N // P, C], F32, name="y")
+            if last:
+                for b in reversed(range(N // P)):
+                    nc.scalar.activation(out=y[:, b, :], in_=y_bank[:, b, :], func=COPY)
+            else:
+                nc.scalar.activation(out=y[:], in_=y_bank[:], func=COPY)
+            return y
+
+        def scatter(e, y, b):
+            at = slice(e * LIST_COLS, (e + 1) * LIST_COLS)
+            gate_cols = slice((e % 2) * C, (e % 2 + 1) * C)
+            nc.vector.tensor_tensor(
+                out=windows[b][:].indirect(dst_sb[:, at]),
+                in0=y[:, b, :],
+                in1=gates[e // 2][:, b, gate_cols],
+                op=MULT,
+            )
+
+        slots = {}
+        gather(0, 1)
+        for e in range(E):
+            first = quantize_first("w1", raws[e]["w1"], W1_VECTOR[e])
+            a_banks = first_product("a_bank", slots[e], first)
+            if e == 0:
+                gather(1, 2)
+            else:
+                y = copy_out(y_bank, False)
+            third = quantize_first("w3", raws[e]["w3"], W3_VECTOR[e])
+            b_banks = first_product("b_bank", slots[e], third)
+            acts = activate(a_banks)
+            if e == 0:
+                gather(2, 3)
+            else:
+                scatter(e - 1, y, 0)
+            y_bank = project(second_operands(acts, b_banks, raws[e]["w2"]))
+            if e == 0:
+                gather(3, 4)
+            else:
+                scatter(e - 1, y, 1)
+            if e + 2 < E:
+                raws.append(load_weights(e + 2))
+        y = copy_out(y_bank, True)
+        for b, queue in ((1, nc.scalar), (0, nc.sync)):
+            scatter(E - 1, y, b)
+            queue.dma_start(out=out[b * P:(b + 1) * P, :], in_=windows[b][:])

@@ -19,27 +19,20 @@ MULT = mybir.AluOpType.mult
 P = 128
 PACK = 4
 RUN = 4
-X_CHUNKS = (256, 512, 512, 512, 256)
-W1_VECTOR = (0, 0, 0, H)
-W3_VECTOR = (0, 0, 0, 0)
+X_CHUNKS = (512, 512, 512, 256, 256)
+W1_VECTOR = (0, 2, 0, 0)
+W3_VECTOR = (2, 0, 0, 0)
+W2_VECTOR = (True, True, True, False)
 HALF = 128
 LIST_COLS = C // 16
-
-
-def split(nc, out, in_, at, total):
-    if at > 0:
-        nc.vector.tensor_copy(out=out(0, at), in_=in_(0, at))
-    if at < total:
-        nc.scalar.activation(out=out(at, total), in_=in_(at, total), func=COPY)
 
 
 def tile_moe_two_glu_silu_kernel(tc, xT, w1, w3, w2, gate, offs, dst, out):
     nc = tc.nc
     with ExitStack() as ctx:
         keep = ctx.enter_context(tc.tile_pool(name="keep", bufs=1))
-        load = ctx.enter_context(tc.tile_pool(name="load", bufs=2))
         cast = ctx.enter_context(tc.tile_pool(name="cast", bufs=2))
-        codes = ctx.enter_context(tc.tile_pool(name="codes", bufs=4))
+        codes = ctx.enter_context(tc.tile_pool(name="codes", bufs=3))
         hid = ctx.enter_context(tc.tile_pool(name="hid", bufs=3))
         psum = ctx.enter_context(tc.psum_pool(name="psum", bufs=3))
         psum_y = ctx.enter_context(tc.psum_pool(name="psum_y", bufs=2))
@@ -50,11 +43,7 @@ def tile_moe_two_glu_silu_kernel(tc, xT, w1, w3, w2, gate, offs, dst, out):
         windows = [keep.tile([P, T], F32, name=f"window{b}") for b in range(N // P)]
         x_codes = keep.tile([P, T], U32, name="x_codes", align_bytes=64)
         x_scales = keep.tile([P, T], U8, name="x_scales", align_bytes=64)
-        gates = [keep.tile([P, N // P, 2 * C], F32, name=f"gates{g}") for g in range(E // 2)]
-
-        def load_gate(g):
-            cols = slice(g * 2 * C, (g + 1) * 2 * C)
-            nc.sync.dma_start(out=gates[g][:], in_=gate[:, cols].rearrange("(b p) s -> p b s", p=P))
+        gates = [keep.tile([P, 2 * C], F32, name=f"gates{g}") for g in range(E // 2)]
 
         x_cols = [slice(sum(X_CHUNKS[:c]), sum(X_CHUNKS[:c + 1])) for c in range(len(X_CHUNKS))]
         x_raw = []
@@ -65,19 +54,17 @@ def tile_moe_two_glu_silu_kernel(tc, xT, w1, w3, w2, gate, offs, dst, out):
             if c == 0:
                 nc.sync.dma_start(offs_sb[:], offs)
 
-        def load_weights(e):
+        raws = []
+        for e in range(E):
             tiles = {}
             for name, w, width in (("w1", w1, H), ("w3", w3, H), ("w2", w2, N)):
-                if name == "w2" and e == E - 1:
-                    load_gate(E // 2 - 1)
-                tiles[name] = load.tile([P, PACK, width], F32, name=f"{name}_raw")
+                tiles[name] = keep.tile([P, PACK, width], F32, name=f"{name}_raw{e}")
                 nc.sync.dma_start(out=tiles[name][:], in_=w[e].rearrange("(p j) n -> p j n", j=PACK))
             if e == 0:
                 nc.sync.dma_start(dst_sb[:], dst)
-                load_gate(0)
-            return tiles
-
-        raws = [load_weights(0), load_weights(1)]
+            if e % 2 == 0:
+                nc.sync.dma_start(out=gates[e // 2][:], in_=gate[:P, e * C:(e + 2) * C])
+            raws.append(tiles)
 
         nc.vector.memset(warm[:], 0.0)
         nc.scalar.activation(out=warm[:], in_=warm[:], func=SILU)
@@ -87,44 +74,39 @@ def tile_moe_two_glu_silu_kernel(tc, xT, w1, w3, w2, gate, offs, dst, out):
 
         for c, cols in enumerate(x_cols):
             x_bf = keep.tile([P, X_CHUNKS[c] * PACK], BF16, name=f"x_bf{c}", align_bytes=64)
-
-            def dst_view(a, b):
-                return x_bf[:, a * PACK:b * PACK].rearrange("p (c i j) -> p c j i", i=RUN, j=PACK)
-
-            def src_view(a, b):
-                return x_raw[c][:, :, a:b].rearrange("p j (c i) -> p c j i", i=RUN)
-
-            split(nc, dst_view, src_view, X_CHUNKS[c] // 2, X_CHUNKS[c])
+            at = X_CHUNKS[c] // 2
+            for a, b, copy in ((0, at, nc.vector.tensor_copy), (at, X_CHUNKS[c], nc.scalar.copy)):
+                copy(
+                    out=x_bf[:, a * PACK:b * PACK].rearrange("p (c i j) -> p c j i", i=RUN, j=PACK),
+                    in_=x_raw[c][:, :, a:b].rearrange("p j (c i) -> p c j i", i=RUN),
+                )
             nc.vector.quantize_mx(out=x_codes[:, cols].bitcast(FP8X4), scales=x_scales[:, cols], in_=x_bf[:])
 
-        def gather(e0, e1):
-            at = slice(e0 * LIST_COLS, e1 * LIST_COLS)
-            words = keep.tile([P, (e1 - e0) * C], U32, name=f"slot_codes{e0}", align_bytes=64)
-            planes = keep.tile([P, (e1 - e0) * C], U8, name=f"slot_scales{e0}", align_bytes=64)
+        def gather(e):
+            at = slice(e * LIST_COLS, (e + 1) * LIST_COLS)
+            words = codes.tile([P, C], U32, name="slot_codes", align_bytes=64)
+            planes = codes.tile([P, C], U8, name="slot_scales", align_bytes=64)
             nc.vector.tensor_copy(out=words[:], in_=x_codes[:].indirect(offs_sb[:, at]))
             nc.vector.tensor_copy(out=planes[:], in_=x_scales[:].indirect(offs_sb[:, at]))
-            for e in range(e0, e1):
-                slots[e] = (words, planes, (e - e0) * C)
+            return words, planes
 
         def quantize_first(name, raw, at):
             bf = cast.tile([P, PACK, H // PACK, PACK], BF16, name=f"{name}_bf", align_bytes=64)
             out_codes = codes.tile([P, H], U32, name=f"{name}_codes", align_bytes=64)
             out_scales = codes.tile([P, H], U8, name=f"{name}_scales", align_bytes=64)
-
-            def dst_view(a, b):
-                return bf[:, :, a // PACK:b // PACK, :].rearrange("p t m j -> p m j t")
-
-            def src_view(a, b):
-                return raw[:, :, a:b].rearrange("p j (m t) -> p m j t", t=PACK)
-
-            split(nc, dst_view, src_view, at, H)
+            for a, b, copy in ((0, at, nc.vector.tensor_copy), (at, PACK, nc.scalar.copy)):
+                if a < b:
+                    copy(
+                        out=bf[:, a:b, :, :].rearrange("p t m j -> p m j t"),
+                        in_=raw[:].rearrange("p j (m t) -> p m j t", t=PACK)[:, :, :, a:b],
+                    )
             nc.vector.quantize_mx(out=out_codes[:].bitcast(FP8X4), scales=out_scales[:], in_=bf[:].rearrange("p t m j -> p (t m j)"))
             return out_codes, out_scales
 
         def first_product(bank_name, slots, weights):
             banks = []
             for s in range(C // HALF):
-                cols = slice(slots[2] + s * HALF, slots[2] + (s + 1) * HALF)
+                cols = slice(s * HALF, (s + 1) * HALF)
                 bank = psum.tile([P, PACK, HALF], F32, name=bank_name)
                 for t in range(PACK):
                     w_cols = slice(t * P, (t + 1) * P)
@@ -140,87 +122,81 @@ def tile_moe_two_glu_silu_kernel(tc, xT, w1, w3, w2, gate, offs, dst, out):
                 banks.append(bank)
             return banks
 
-        def activate(a_banks):
-            acts = []
-            for bank in a_banks:
-                act = hid.tile([P, HALF, PACK], F32, name="act", bufs=4)
-                nc.scalar.activation(out=act[:], in_=bank[:].rearrange("p t c -> p c t"), func=SILU)
-                acts.append(act)
-            return acts
+        def activate(a_banks, acts):
+            for bank, act in zip(a_banks, acts):
+                nc.scalar.activation(out=act.rearrange("p (c t) -> p c t", t=PACK), in_=bank[:].rearrange("p t c -> p c t"), func=SILU)
 
-        def second_operands(acts, b_banks, w2_raw):
-            bf = hid.tile([P, N + C, PACK], BF16, name="second_bf", align_bytes=64)
-            out_codes = hid.tile([P, N + C], U32, name="second_codes", align_bytes=64)
-            out_scales = hid.tile([P, N + C], U8, name="second_scales", align_bytes=64)
-            nc.scalar.activation(
-                out=bf[:, :N, :].rearrange("p (c i) j -> p c j i", i=RUN),
+        def quantize_second(w2_raw, on_vector):
+            bf = cast.tile([P, N, PACK], BF16, name="w2_bf", align_bytes=64)
+            out_codes = codes.tile([P, N], U32, name="w2_codes", align_bytes=64)
+            out_scales = codes.tile([P, N], U8, name="w2_scales", align_bytes=64)
+            copy = nc.vector.tensor_copy if on_vector else nc.scalar.copy
+            copy(
+                out=bf[:].rearrange("p (c i) j -> p c j i", i=RUN),
                 in_=w2_raw[:].rearrange("p j (c i) -> p c j i", i=RUN),
-                func=COPY,
             )
-            for s, bank in enumerate(b_banks):
-                cols = slice(N + s * HALF, N + (s + 1) * HALF)
-                nc.vector.tensor_tensor(out=bf[:, cols, :], in0=acts[s][:], in1=bank[:].rearrange("p t c -> p c t"), op=MULT)
             nc.vector.quantize_mx(out=out_codes[:].bitcast(FP8X4), scales=out_scales[:], in_=bf[:].rearrange("p c t -> p (c t)"))
             return out_codes, out_scales
 
-        def project(second):
+        def second_product(weights, acts, b_banks):
+            bf = hid.tile([P, C, PACK], BF16, name="h_bf", align_bytes=64)
+            h_codes = hid.tile([P, C], U32, name="h_codes", align_bytes=64)
+            h_scales = hid.tile([P, C], U8, name="h_scales", align_bytes=64)
+            for s, bank in enumerate(b_banks):
+                nc.vector.tensor_tensor(
+                    out=bf[:, s * HALF:(s + 1) * HALF, :],
+                    in0=acts[s].rearrange("p (c t) -> p c t", t=PACK),
+                    in1=bank[:].rearrange("p t c -> p c t"),
+                    op=MULT,
+                )
+            nc.vector.quantize_mx(out=h_codes[:].bitcast(FP8X4), scales=h_scales[:], in_=bf[:].rearrange("p c t -> p (c t)"))
             y_bank = psum_y.tile([P, N // P, C], F32, name="y_bank")
             for b in range(N // P):
                 w_cols = slice(b * P, (b + 1) * P)
                 nc.tensor.matmul_mx(
                     out=y_bank[:, b, :],
-                    lhsT=second[0][:, w_cols].bitcast(FP8X4),
-                    lhsT_scale=second[1][:, w_cols],
-                    rhs=second[0][:, N:].bitcast(FP8X4),
-                    rhs_scale=second[1][:, N:],
+                    lhsT=weights[0][:, w_cols].bitcast(FP8X4),
+                    lhsT_scale=weights[1][:, w_cols],
+                    rhs=h_codes[:].bitcast(FP8X4),
+                    rhs_scale=h_scales[:],
                     start=True,
                     stop=True,
                 )
             return y_bank
 
-        def copy_out(y_bank, last):
-            y = hid.tile([P, N // P, C], F32, name="y")
-            if last:
-                for b in reversed(range(N // P)):
-                    nc.scalar.activation(out=y[:, b, :], in_=y_bank[:, b, :], func=COPY)
-            else:
-                nc.scalar.activation(out=y[:], in_=y_bank[:], func=COPY)
-            return y
-
-        def scatter(e, y, b):
+        def scatter(e, y_bank, b, y):
+            nc.scalar.copy(out=y, in_=y_bank[:, b, :])
             at = slice(e * LIST_COLS, (e + 1) * LIST_COLS)
             gate_cols = slice((e % 2) * C, (e % 2 + 1) * C)
             nc.vector.tensor_tensor(
                 out=windows[b][:].indirect(dst_sb[:, at]),
-                in0=y[:, b, :],
-                in1=gates[e // 2][:, b, gate_cols],
+                in0=y,
+                in1=gates[e // 2][:, gate_cols],
                 op=MULT,
             )
 
-        slots = {}
-        gather(0, 1)
+        spare = keep.tile([P, PACK, H], F32, name="spare")
+        slots = [gather(e) for e in range(E - 1)]
+        a_banks = first_product("a_bank", slots[0], quantize_first("w1", raws[0]["w1"], W1_VECTOR[0]))
+        b_banks = first_product("b_bank", slots[0], quantize_first("w3", raws[0]["w3"], W3_VECTOR[0]))
+        y_banks = []
         for e in range(E):
-            first = quantize_first("w1", raws[e]["w1"], W1_VECTOR[e])
-            a_banks = first_product("a_bank", slots[e], first)
+            home = spare if e == 0 else raws[e]["w3"]
+            acts = [home[:, 1 + s, :] for s in range(C // HALF)]
+            activate(a_banks, acts)
+            y_banks.append(second_product(quantize_second(raws[e]["w2"], W2_VECTOR[e]), acts, b_banks))
             if e == 0:
-                gather(1, 2)
-            else:
-                y = copy_out(y_bank, False)
-            third = quantize_first("w3", raws[e]["w3"], W3_VECTOR[e])
-            b_banks = first_product("b_bank", slots[e], third)
-            acts = activate(a_banks)
+                slots.append(gather(E - 1))
+            if e + 1 < E:
+                a_banks = first_product("a_bank", slots[e + 1], quantize_first("w1", raws[e + 1]["w1"], W1_VECTOR[e + 1]))
+            if e > 0:
+                scatter(e - 1, y_banks[e - 1], 1, raws[e + 1]["w1"][:, 0, :C] if e + 1 < E else acts[-1][:, :C])
             if e == 0:
-                gather(2, 3)
-            else:
-                scatter(e - 1, y, 0)
-            y_bank = project(second_operands(acts, b_banks, raws[e]["w2"]))
-            if e == 0:
-                gather(3, 4)
-            else:
-                scatter(e - 1, y, 1)
-            if e + 2 < E:
-                raws.append(load_weights(e + 2))
-        y = copy_out(y_bank, True)
-        for b, queue in ((1, nc.scalar), (0, nc.sync)):
-            scatter(E - 1, y, b)
-            queue.dma_start(out=out[b * P:(b + 1) * P, :], in_=windows[b][:])
+                scatter(e, y_banks[e], 0, spare[:, 0, :C])
+            if e + 1 < E:
+                b_banks = first_product("b_bank", slots[e + 1], quantize_first("w3", raws[e + 1]["w3"], W3_VECTOR[e + 1]))
+            if e > 0:
+                scatter(e, y_banks[e], 0, raws[e + 1]["w3"][:, 0, :C] if e + 1 < E else spare[:, 3, :C])
+        nc.sync.dma_start(out=out[:P, :], in_=windows[0][:])
+        scatter(E - 1, y_banks[E - 1], 1, spare[:, 3, C:])
+        nc.scalar.dma_start(out=out[P:, :], in_=windows[1][:])

@@ -8,7 +8,6 @@ FLOPS = 2 * E * C * (2 * K * H + H * N)
 F32 = mybir.dt.float32
 BF16 = mybir.dt.bfloat16
 U32 = mybir.dt.uint32
-I32 = mybir.dt.int32
 U16 = mybir.dt.uint16
 U8 = mybir.dt.uint8
 FP8X4 = mybir.dt.float8_e4m3fn_x4
@@ -19,9 +18,8 @@ MULT = mybir.AluOpType.mult
 P = 128
 PACK = 4
 RUN = 4
-X_CHUNKS = (512, 512, 512, 256, 256)
-W1_VECTOR = (0, 2, 0, 0)
-W3_VECTOR = (2, 0, 0, 0)
+W1_VECTOR = (4, 0, 0, 0)
+W3_VECTOR = (2, 2, 0, 0)
 W2_VECTOR = (True, True, True, False)
 HALF = 128
 LIST_COLS = C // 16
@@ -41,18 +39,26 @@ def tile_moe_two_glu_silu_kernel(tc, xT, w1, w3, w2, gate, offs, dst, out):
         dst_sb = keep.tile([P, E * LIST_COLS], U16, name="dst_sb")
         warm = keep.tile([P, 1], F32, name="warm")
         windows = [keep.tile([P, T], F32, name=f"window{b}") for b in range(N // P)]
-        x_codes = keep.tile([P, T], U32, name="x_codes", align_bytes=64)
-        x_scales = keep.tile([P, T], U8, name="x_scales", align_bytes=64)
         gates = [keep.tile([P, 2 * C], F32, name=f"gates{g}") for g in range(E // 2)]
 
-        x_cols = [slice(sum(X_CHUNKS[:c]), sum(X_CHUNKS[:c + 1])) for c in range(len(X_CHUNKS))]
-        x_raw = []
-        for c, cols in enumerate(x_cols):
-            raw = keep.tile([P, PACK, X_CHUNKS[c]], F32, name=f"x_raw{c}")
-            nc.sync.dma_start(out=raw[:], in_=xT[:, cols].rearrange("(p j) t -> p j t", j=PACK))
-            x_raw.append(raw)
-            if c == 0:
-                nc.sync.dma_start(offs_sb[:], offs)
+        x_rows = xT.rearrange("(p j) t -> p j t", j=PACK)
+        halves = [slice(0, T // 2), slice(T // 2, T)]
+
+        def load_halves(j):
+            tiles = [keep.tile([P, T // 2], F32, name=f"x_half{j}_{h}") for h in range(2)]
+            for tile, cols in zip(tiles, halves):
+                nc.sync.dma_start(out=tile[:], in_=x_rows[:, j, cols])
+            return tiles
+
+        def load_plane(j):
+            tile = keep.tile([P, T], F32, name=f"x_plane{j}")
+            nc.sync.dma_start(out=tile[:], in_=x_rows[:, j, :])
+            return tile
+
+        x_first = load_halves(0)
+        nc.sync.dma_start(offs_sb[:], offs)
+        x_mid = [load_plane(2), load_plane(3)]
+        x_last = load_halves(1)
 
         raws = []
         for e in range(E):
@@ -68,26 +74,31 @@ def tile_moe_two_glu_silu_kernel(tc, xT, w1, w3, w2, gate, offs, dst, out):
 
         nc.vector.memset(warm[:], 0.0)
         nc.scalar.activation(out=warm[:], in_=warm[:], func=SILU)
-        nc.gpsimd.memset(x_scales[:].bitcast(I32), 0)
         nc.vector.memset(windows[0][:], 0.0)
         nc.gpsimd.memset(windows[1][:], 0.0)
 
-        for c, cols in enumerate(x_cols):
-            x_bf = keep.tile([P, X_CHUNKS[c] * PACK], BF16, name=f"x_bf{c}", align_bytes=64)
-            at = X_CHUNKS[c] // 2
-            for a, b, copy in ((0, at, nc.vector.tensor_copy), (at, X_CHUNKS[c], nc.scalar.copy)):
-                copy(
-                    out=x_bf[:, a * PACK:b * PACK].rearrange("p (c i j) -> p c j i", i=RUN, j=PACK),
-                    in_=x_raw[c][:, :, a:b].rearrange("p j (c i) -> p c j i", i=RUN),
-                )
-            nc.vector.quantize_mx(out=x_codes[:, cols].bitcast(FP8X4), scales=x_scales[:, cols], in_=x_bf[:])
+        slot_bf = [keep.tile([P, C, PACK], BF16, name=f"slot_bf{e}", align_bytes=64) for e in range(E)]
 
-        def gather(e):
-            at = slice(e * LIST_COLS, (e + 1) * LIST_COLS)
-            words = codes.tile([P, C], U32, name="slot_codes", align_bytes=64)
-            planes = codes.tile([P, C], U8, name="slot_scales", align_bytes=64)
-            nc.vector.tensor_copy(out=words[:], in_=x_codes[:].indirect(offs_sb[:, at]))
-            nc.vector.tensor_copy(out=planes[:], in_=x_scales[:].indirect(offs_sb[:, at]))
+        def offsets(e):
+            return offs_sb[:, e * LIST_COLS:(e + 1) * LIST_COLS]
+
+        def gather_on_scalar(j, tiles):
+            plane = keep.tile([P, T], BF16, name=f"x_bf{j}")
+            for tile, cols in zip(tiles, halves):
+                nc.scalar.copy(out=plane[:, cols], in_=tile[:])
+            for e in range(E):
+                nc.scalar.activation(out=slot_bf[e][:, :, j], in_=plane[:].indirect(offsets(e)), func=COPY)
+
+        gather_on_scalar(0, x_first)
+        for j, plane in zip((2, 3), x_mid):
+            for e in range(E):
+                nc.vector.tensor_copy(out=slot_bf[e][:, :, j], in_=plane[:].indirect(offsets(e)))
+        gather_on_scalar(1, x_last)
+
+        def quantize_slots(e):
+            words = keep.tile([P, C], U32, name="slot_codes", align_bytes=64)
+            planes = keep.tile([P, C], U8, name="slot_scales", align_bytes=64)
+            nc.vector.quantize_mx(out=words[:].bitcast(FP8X4), scales=planes[:], in_=slot_bf[e][:].rearrange("p c j -> p (c j)"))
             return words, planes
 
         def quantize_first(name, raw, at):
@@ -175,28 +186,27 @@ def tile_moe_two_glu_silu_kernel(tc, xT, w1, w3, w2, gate, offs, dst, out):
                 op=MULT,
             )
 
-        spare = keep.tile([P, PACK, H], F32, name="spare")
-        slots = [gather(e) for e in range(E - 1)]
+        spare = keep.tile([P, 3, C], F32, name="spare")
+        slots = [quantize_slots(0)]
         a_banks = first_product("a_bank", slots[0], quantize_first("w1", raws[0]["w1"], W1_VECTOR[0]))
         b_banks = first_product("b_bank", slots[0], quantize_first("w3", raws[0]["w3"], W3_VECTOR[0]))
         y_banks = []
         for e in range(E):
-            home = spare if e == 0 else raws[e]["w3"]
+            home = raws[e]["w3"]
             acts = [home[:, 1 + s, :] for s in range(C // HALF)]
             activate(a_banks, acts)
             y_banks.append(second_product(quantize_second(raws[e]["w2"], W2_VECTOR[e]), acts, b_banks))
-            if e == 0:
-                slots.append(gather(E - 1))
             if e + 1 < E:
+                slots.append(quantize_slots(e + 1))
                 a_banks = first_product("a_bank", slots[e + 1], quantize_first("w1", raws[e + 1]["w1"], W1_VECTOR[e + 1]))
             if e > 0:
                 scatter(e - 1, y_banks[e - 1], 1, raws[e + 1]["w1"][:, 0, :C] if e + 1 < E else acts[-1][:, :C])
             if e == 0:
-                scatter(e, y_banks[e], 0, spare[:, 0, :C])
+                scatter(e, y_banks[e], 0, spare[:, 0, :])
             if e + 1 < E:
                 b_banks = first_product("b_bank", slots[e + 1], quantize_first("w3", raws[e + 1]["w3"], W3_VECTOR[e + 1]))
             if e > 0:
-                scatter(e, y_banks[e], 0, raws[e + 1]["w3"][:, 0, :C] if e + 1 < E else spare[:, 3, :C])
+                scatter(e, y_banks[e], 0, raws[e + 1]["w3"][:, 0, :C] if e + 1 < E else spare[:, 1, :])
         nc.sync.dma_start(out=out[:P, :], in_=windows[0][:])
-        scatter(E - 1, y_banks[E - 1], 1, spare[:, 3, C:])
+        scatter(E - 1, y_banks[E - 1], 1, spare[:, 2, :])
         nc.scalar.dma_start(out=out[P:, :], in_=windows[1][:])

@@ -17,10 +17,10 @@ MULT = mybir.AluOpType.mult
 
 P = 128
 PACK = 4
-RUN = 4
-W1_VECTOR = (4, 0, 0, 0)
-W3_VECTOR = (2, 2, 0, 0)
-W2_VECTOR = (True, True, True, False)
+RUN = 2
+W1_VECTOR = (4, 2, 0, 0)
+W3_VECTOR = (3, 2, 0, 0)
+W2_VECTOR = (False, True, True, False)
 HALF = 128
 LIST_COLS = C // 16
 
@@ -65,7 +65,12 @@ def tile_moe_two_glu_silu_kernel(tc, xT, w1, w3, w2, gate, offs, dst, out):
             tiles = {}
             for name, w, width in (("w1", w1, H), ("w3", w3, H), ("w2", w2, N)):
                 tiles[name] = keep.tile([P, PACK, width], F32, name=f"{name}_raw{e}")
-                nc.sync.dma_start(out=tiles[name][:], in_=w[e].rearrange("(p j) n -> p j n", j=PACK))
+                if name == "w2":
+                    rows = w[e].rearrange("(a t i) n -> i a t n", t=PACK, i=RUN)
+                    for i in range(RUN):
+                        nc.sync.dma_start(out=tiles[name][i:P:RUN, :, :], in_=rows[i])
+                else:
+                    nc.sync.dma_start(out=tiles[name][:], in_=w[e].rearrange("(p j) n -> p j n", j=PACK))
             if e == 0:
                 nc.sync.dma_start(dst_sb[:], dst)
             if e % 2 == 0:
@@ -108,8 +113,8 @@ def tile_moe_two_glu_silu_kernel(tc, xT, w1, w3, w2, gate, offs, dst, out):
             for a, b, copy in ((0, at, nc.vector.tensor_copy), (at, PACK, nc.scalar.copy)):
                 if a < b:
                     copy(
-                        out=bf[:, a:b, :, :].rearrange("p t m j -> p m j t"),
-                        in_=raw[:].rearrange("p j (m t) -> p m j t", t=PACK)[:, :, :, a:b],
+                        out=bf[:, a:b, :, :].rearrange("p t (a i) j -> p a t j i", i=RUN),
+                        in_=raw[:].rearrange("p j (a t i) -> p a t j i", t=PACK, i=RUN)[:, :, a:b],
                     )
             nc.vector.quantize_mx(out=out_codes[:].bitcast(FP8X4), scales=out_scales[:], in_=bf[:].rearrange("p t m j -> p (t m j)"))
             return out_codes, out_scales
@@ -186,7 +191,7 @@ def tile_moe_two_glu_silu_kernel(tc, xT, w1, w3, w2, gate, offs, dst, out):
                 op=MULT,
             )
 
-        spare = keep.tile([P, 3, C], F32, name="spare")
+        spare = keep.tile([P, 2, C], F32, name="spare")
         slots = [quantize_slots(0)]
         a_banks = first_product("a_bank", slots[0], quantize_first("w1", raws[0]["w1"], W1_VECTOR[0]))
         b_banks = first_product("b_bank", slots[0], quantize_first("w3", raws[0]["w3"], W3_VECTOR[0]))
@@ -199,14 +204,16 @@ def tile_moe_two_glu_silu_kernel(tc, xT, w1, w3, w2, gate, offs, dst, out):
             if e + 1 < E:
                 slots.append(quantize_slots(e + 1))
                 a_banks = first_product("a_bank", slots[e + 1], quantize_first("w1", raws[e + 1]["w1"], W1_VECTOR[e + 1]))
-            if e > 0:
-                scatter(e - 1, y_banks[e - 1], 1, raws[e + 1]["w1"][:, 0, :C] if e + 1 < E else acts[-1][:, :C])
-            if e == 0:
-                scatter(e, y_banks[e], 0, spare[:, 0, :])
-            if e + 1 < E:
+                if e == 0:
+                    scatter(e, y_banks[e], 0, raws[1]["w1"][:, 0, :C])
                 b_banks = first_product("b_bank", slots[e + 1], quantize_first("w3", raws[e + 1]["w3"], W3_VECTOR[e + 1]))
-            if e > 0:
-                scatter(e, y_banks[e], 0, raws[e + 1]["w3"][:, 0, :C] if e + 1 < E else spare[:, 1, :])
+                spent = raws[e + 1]["w3"]
+                if e > 0:
+                    scatter(e, y_banks[e], 0, spent[:, 0, :C])
+                if e + 2 < E:
+                    scatter(e, y_banks[e], 1, spent[:, 0, C:])
+        scatter(E - 2, y_banks[E - 2], 1, acts[-1][:, :C])
+        scatter(E - 1, y_banks[E - 1], 0, spare[:, 0, :])
         nc.sync.dma_start(out=out[:P, :], in_=windows[0][:])
-        scatter(E - 1, y_banks[E - 1], 1, spare[:, 2, :])
+        scatter(E - 1, y_banks[E - 1], 1, spare[:, 1, :])
         nc.scalar.dma_start(out=out[P:, :], in_=windows[1][:])

@@ -19,7 +19,7 @@ P = 128
 PACK = 4
 RUN = 2
 W1_VECTOR = (4, 2, 0, 0)
-W3_VECTOR = (3, 2, 0, 0)
+W3_VECTOR = (4, 2, 0, 0)
 W2_VECTOR = (False, True, True, False)
 HALF = 128
 LIST_COLS = C // 16
@@ -32,14 +32,14 @@ def tile_moe_two_glu_silu_kernel(tc, xT, w1, w3, w2, gate, offs, dst, out):
         cast = ctx.enter_context(tc.tile_pool(name="cast", bufs=2))
         codes = ctx.enter_context(tc.tile_pool(name="codes", bufs=3))
         hid = ctx.enter_context(tc.tile_pool(name="hid", bufs=3))
-        psum = ctx.enter_context(tc.psum_pool(name="psum", bufs=3))
-        psum_y = ctx.enter_context(tc.psum_pool(name="psum_y", bufs=2))
+        psum = ctx.enter_context(tc.psum_pool(name="psum", bufs=2))
+        psum_y = ctx.enter_context(tc.psum_pool(name="psum_y", bufs=4))
 
         offs_sb = keep.tile([P, E * LIST_COLS], U16, name="offs_sb")
         dst_sb = keep.tile([P, E * LIST_COLS], U16, name="dst_sb")
         warm = keep.tile([P, 1], F32, name="warm")
         windows = [keep.tile([P, T], F32, name=f"window{b}") for b in range(N // P)]
-        gates = [keep.tile([P, 2 * C], F32, name=f"gates{g}") for g in range(E // 2)]
+        gates = [keep.tile([P, C], F32, name=f"gate{e}") for e in range(E)]
 
         x_rows = xT.rearrange("(p j) t -> p j t", j=PACK)
         halves = [slice(0, T // 2), slice(T // 2, T)]
@@ -55,27 +55,32 @@ def tile_moe_two_glu_silu_kernel(tc, xT, w1, w3, w2, gate, offs, dst, out):
             nc.sync.dma_start(out=tile[:], in_=x_rows[:, j, :])
             return tile
 
-        x_first = load_halves(0)
+        x_plane2 = load_plane(2)
         nc.sync.dma_start(offs_sb[:], offs)
-        x_mid = [load_plane(2), load_plane(3)]
-        x_last = load_halves(1)
+        x_plane0 = load_halves(0)
+        x_plane3 = load_plane(3)
+        x_plane1 = load_halves(1)
+
+        def load_gate(e):
+            nc.sync.dma_start(out=gates[e][:], in_=gate[:P, e * C:(e + 1) * C])
 
         raws = []
         for e in range(E):
             tiles = {}
             for name, w, width in (("w1", w1, H), ("w3", w3, H), ("w2", w2, N)):
-                tiles[name] = keep.tile([P, PACK, width], F32, name=f"{name}_raw{e}")
+                tiles[name] = keep.tile([P, PACK, width], F32, name=f"{name}_raw{e}", align_bytes=64)
                 if name == "w2":
                     rows = w[e].rearrange("(a t i) n -> i a t n", t=PACK, i=RUN)
                     for i in range(RUN):
                         nc.sync.dma_start(out=tiles[name][i:P:RUN, :, :], in_=rows[i])
                 else:
                     nc.sync.dma_start(out=tiles[name][:], in_=w[e].rearrange("(p j) n -> p j n", j=PACK))
+                if e > 0 and name == ("w1" if e == 1 else "w3"):
+                    load_gate(e - 1)
             if e == 0:
                 nc.sync.dma_start(dst_sb[:], dst)
-            if e % 2 == 0:
-                nc.sync.dma_start(out=gates[e // 2][:], in_=gate[:P, e * C:(e + 2) * C])
             raws.append(tiles)
+        load_gate(E - 1)
 
         nc.vector.memset(warm[:], 0.0)
         nc.scalar.activation(out=warm[:], in_=warm[:], func=SILU)
@@ -87,37 +92,49 @@ def tile_moe_two_glu_silu_kernel(tc, xT, w1, w3, w2, gate, offs, dst, out):
         def offsets(e):
             return offs_sb[:, e * LIST_COLS:(e + 1) * LIST_COLS]
 
-        def gather_on_scalar(j, tiles):
+        def gather_on_scalar(j, tiles, copies):
             plane = keep.tile([P, T], BF16, name=f"x_bf{j}")
-            for tile, cols in zip(tiles, halves):
-                nc.scalar.copy(out=plane[:, cols], in_=tile[:])
+            for tile, cols, copy in zip(tiles, halves, copies):
+                copy(out=plane[:, cols], in_=tile[:])
             for e in range(E):
                 nc.scalar.activation(out=slot_bf[e][:, :, j], in_=plane[:].indirect(offsets(e)), func=COPY)
 
-        gather_on_scalar(0, x_first)
-        for j, plane in zip((2, 3), x_mid):
+        def gather_on_vector(j, plane):
             for e in range(E):
                 nc.vector.tensor_copy(out=slot_bf[e][:, :, j], in_=plane[:].indirect(offsets(e)))
-        gather_on_scalar(1, x_last)
 
-        def quantize_slots(e):
-            words = keep.tile([P, C], U32, name="slot_codes", align_bytes=64)
-            planes = keep.tile([P, C], U8, name="slot_scales", align_bytes=64)
-            nc.vector.quantize_mx(out=words[:].bitcast(FP8X4), scales=planes[:], in_=slot_bf[e][:].rearrange("p c j -> p (c j)"))
-            return words, planes
+        gather_on_vector(2, x_plane2)
+        gather_on_scalar(0, x_plane0, (nc.scalar.copy, nc.scalar.copy))
+        gather_on_vector(3, x_plane3)
+        gather_on_scalar(1, x_plane1, (nc.scalar.copy, nc.vector.tensor_copy))
 
-        def quantize_first(name, raw, at):
-            bf = cast.tile([P, PACK, H // PACK, PACK], BF16, name=f"{name}_bf", align_bytes=64)
-            out_codes = codes.tile([P, H], U32, name=f"{name}_codes", align_bytes=64)
-            out_scales = codes.tile([P, H], U8, name=f"{name}_scales", align_bytes=64)
+        def quantize_slots(experts, tag):
+            words = keep.tile([P, len(experts), C], U32, name=tag, align_bytes=64)
+            planes = keep.tile([P, len(experts), C], U8, name=f"slot_scales{experts[0]}", align_bytes=64)
+            for n, e in enumerate(experts):
+                nc.vector.quantize_mx(
+                    out=words[:, n, :].bitcast(FP8X4), scales=planes[:, n, :], in_=slot_bf[e][:].rearrange("p c j -> p (c j)")
+                )
+            return [(words[:, n, :], planes[:, n, :]) for n in range(len(experts))]
+
+        def round_first(name, raw, at, pool):
+            bf = pool.tile([P, PACK, H // PACK, PACK], BF16, name=f"{name}_bf", align_bytes=64)
             for a, b, copy in ((0, at, nc.vector.tensor_copy), (at, PACK, nc.scalar.copy)):
                 if a < b:
                     copy(
                         out=bf[:, a:b, :, :].rearrange("p t (a i) j -> p a t j i", i=RUN),
                         in_=raw[:].rearrange("p j (a t i) -> p a t j i", t=PACK, i=RUN)[:, :, a:b],
                     )
+            return bf
+
+        def quantize_rounded(name, bf):
+            out_codes = codes.tile([P, H], U32, name=f"{name}_codes", align_bytes=64)
+            out_scales = codes.tile([P, H], U8, name=f"{name}_scales", align_bytes=64)
             nc.vector.quantize_mx(out=out_codes[:].bitcast(FP8X4), scales=out_scales[:], in_=bf[:].rearrange("p t m j -> p (t m j)"))
             return out_codes, out_scales
+
+        def quantize_first(name, raw, at, pool):
+            return quantize_rounded(name, round_first(name, raw, at, pool))
 
         def first_product(bank_name, slots, weights):
             banks = []
@@ -166,11 +183,13 @@ def tile_moe_two_glu_silu_kernel(tc, xT, w1, w3, w2, gate, offs, dst, out):
                     op=MULT,
                 )
             nc.vector.quantize_mx(out=h_codes[:].bitcast(FP8X4), scales=h_scales[:], in_=bf[:].rearrange("p c t -> p (c t)"))
-            y_bank = psum_y.tile([P, N // P, C], F32, name="y_bank")
+            y_banks = []
             for b in range(N // P):
+                y_bank = psum_y.tile([P, C], F32, name="y_bank")
+                y_banks.append(y_bank)
                 w_cols = slice(b * P, (b + 1) * P)
                 nc.tensor.matmul_mx(
-                    out=y_bank[:, b, :],
+                    out=y_bank[:],
                     lhsT=weights[0][:, w_cols].bitcast(FP8X4),
                     lhsT_scale=weights[1][:, w_cols],
                     rhs=h_codes[:].bitcast(FP8X4),
@@ -178,23 +197,24 @@ def tile_moe_two_glu_silu_kernel(tc, xT, w1, w3, w2, gate, offs, dst, out):
                     start=True,
                     stop=True,
                 )
-            return y_bank
+            return y_banks
 
-        def scatter(e, y_bank, b, y):
-            nc.scalar.copy(out=y, in_=y_bank[:, b, :])
+        def scatter(e, y_banks, b, y):
+            nc.scalar.copy(out=y, in_=y_banks[b][:])
             at = slice(e * LIST_COLS, (e + 1) * LIST_COLS)
-            gate_cols = slice((e % 2) * C, (e % 2 + 1) * C)
             nc.vector.tensor_tensor(
                 out=windows[b][:].indirect(dst_sb[:, at]),
                 in0=y,
-                in1=gates[e // 2][:, gate_cols],
+                in1=gates[e][:],
                 op=MULT,
             )
 
         spare = keep.tile([P, 2, C], F32, name="spare")
-        slots = [quantize_slots(0)]
-        a_banks = first_product("a_bank", slots[0], quantize_first("w1", raws[0]["w1"], W1_VECTOR[0]))
-        b_banks = first_product("b_bank", slots[0], quantize_first("w3", raws[0]["w3"], W3_VECTOR[0]))
+        rounded = round_first("w1", raws[0]["w1"], W1_VECTOR[0], cast)
+        slots = quantize_slots([0], "w1_raw0")
+        a_banks = first_product("a_bank", slots[0], quantize_rounded("w1", rounded))
+        b_banks = first_product("b_bank", slots[0], quantize_first("w3", raws[0]["w3"], W3_VECTOR[0], keep))
+        slots.extend(quantize_slots(list(range(1, E)), "w3_bf"))
         y_banks = []
         for e in range(E):
             home = raws[e]["w3"]
@@ -202,11 +222,10 @@ def tile_moe_two_glu_silu_kernel(tc, xT, w1, w3, w2, gate, offs, dst, out):
             activate(a_banks, acts)
             y_banks.append(second_product(quantize_second(raws[e]["w2"], W2_VECTOR[e]), acts, b_banks))
             if e + 1 < E:
-                slots.append(quantize_slots(e + 1))
-                a_banks = first_product("a_bank", slots[e + 1], quantize_first("w1", raws[e + 1]["w1"], W1_VECTOR[e + 1]))
+                a_banks = first_product("a_bank", slots[e + 1], quantize_first("w1", raws[e + 1]["w1"], W1_VECTOR[e + 1], cast))
                 if e == 0:
                     scatter(e, y_banks[e], 0, raws[1]["w1"][:, 0, :C])
-                b_banks = first_product("b_bank", slots[e + 1], quantize_first("w3", raws[e + 1]["w3"], W3_VECTOR[e + 1]))
+                b_banks = first_product("b_bank", slots[e + 1], quantize_first("w3", raws[e + 1]["w3"], W3_VECTOR[e + 1], cast))
                 spent = raws[e + 1]["w3"]
                 if e > 0:
                     scatter(e, y_banks[e], 0, spent[:, 0, :C])

@@ -14,15 +14,17 @@ FP8X4 = mybir.dt.float8_e4m3fn_x4
 COPY = mybir.ActivationFunctionType.Copy
 SILU = mybir.ActivationFunctionType.Silu
 MULT = mybir.AluOpType.mult
+ADD = mybir.AluOpType.add
 
 P = 128
 PACK = 4
 RUN = 2
-W1_VECTOR = (4, 2, 0, 0)
+W1_VECTOR = (4, 0, 0, 0)
 W3_VECTOR = (4, 2, 0, 0)
-W2_VECTOR = (False, True, True, False)
 HALF = 128
 LIST_COLS = C // 16
+KIB = 1024
+REGION = 10 * KIB
 
 
 def tile_moe_two_glu_silu_kernel(tc, xT, w1, w3, w2, gate, offs, dst, out):
@@ -32,6 +34,7 @@ def tile_moe_two_glu_silu_kernel(tc, xT, w1, w3, w2, gate, offs, dst, out):
         cast = ctx.enter_context(tc.tile_pool(name="cast", bufs=2))
         codes = ctx.enter_context(tc.tile_pool(name="codes", bufs=3))
         hid = ctx.enter_context(tc.tile_pool(name="hid", bufs=3))
+        placed = ctx.enter_context(tc.tile_pool(name="placed", bufs=1))
         psum = ctx.enter_context(tc.psum_pool(name="psum", bufs=2))
         psum_y = ctx.enter_context(tc.psum_pool(name="psum_y", bufs=4))
 
@@ -68,7 +71,10 @@ def tile_moe_two_glu_silu_kernel(tc, xT, w1, w3, w2, gate, offs, dst, out):
         for e in range(E):
             tiles = {}
             for name, w, width in (("w1", w1, H), ("w3", w3, H), ("w2", w2, N)):
-                tiles[name] = keep.tile([P, PACK, width], F32, name=f"{name}_raw{e}", align_bytes=64)
+                if name == "w3":
+                    tiles[name] = placed.tile([P, PACK, width], F32, name=f"w3_raw{e}", align_bytes=64, offset=e * REGION)
+                else:
+                    tiles[name] = keep.tile([P, PACK, width], F32, name=f"{name}_raw{e}", align_bytes=64)
                 if name == "w2":
                     rows = w[e].rearrange("(a t i) n -> i a t n", t=PACK, i=RUN)
                     for i in range(RUN):
@@ -117,9 +123,18 @@ def tile_moe_two_glu_silu_kernel(tc, xT, w1, w3, w2, gate, offs, dst, out):
                 )
             return [(words[:, n, :], planes[:, n, :]) for n in range(len(experts))]
 
-        def round_first(name, raw, at, pool):
+        def round_first(name, raw, at, pool, on_gpsimd=0):
             bf = pool.tile([P, PACK, H // PACK, PACK], BF16, name=f"{name}_bf", align_bytes=64)
-            for a, b, copy in ((0, at, nc.vector.tensor_copy), (at, PACK, nc.scalar.copy)):
+            for t in range(on_gpsimd):
+                nc.gpsimd.tensor_scalar(
+                    out=bf[:, t, :, :].rearrange("p (a i) j -> p a i j", i=RUN),
+                    in0=raw[:].rearrange("p j (a t i) -> p t a i j", t=PACK, i=RUN)[:, t],
+                    scalar1=1.0,
+                    scalar2=0.0,
+                    op0=MULT,
+                    op1=ADD,
+                )
+            for a, b, copy in ((on_gpsimd, on_gpsimd + at, nc.vector.tensor_copy), (on_gpsimd + at, PACK, nc.scalar.copy)):
                 if a < b:
                     copy(
                         out=bf[:, a:b, :, :].rearrange("p t (a i) j -> p a t j i", i=RUN),
@@ -133,8 +148,8 @@ def tile_moe_two_glu_silu_kernel(tc, xT, w1, w3, w2, gate, offs, dst, out):
             nc.vector.quantize_mx(out=out_codes[:].bitcast(FP8X4), scales=out_scales[:], in_=bf[:].rearrange("p t m j -> p (t m j)"))
             return out_codes, out_scales
 
-        def quantize_first(name, raw, at, pool):
-            return quantize_rounded(name, round_first(name, raw, at, pool))
+        def quantize_first(name, raw, at, pool, on_gpsimd=0):
+            return quantize_rounded(name, round_first(name, raw, at, pool, on_gpsimd))
 
         def first_product(bank_name, slots, weights):
             banks = []
@@ -157,32 +172,39 @@ def tile_moe_two_glu_silu_kernel(tc, xT, w1, w3, w2, gate, offs, dst, out):
 
         def activate(a_banks, acts):
             for bank, act in zip(a_banks, acts):
-                nc.scalar.activation(out=act.rearrange("p (c t) -> p c t", t=PACK), in_=bank[:].rearrange("p t c -> p c t"), func=SILU)
+                nc.scalar.activation(out=act[:].rearrange("p (c t) -> p c t", t=PACK), in_=bank[:].rearrange("p t c -> p c t"), func=SILU)
 
-        def quantize_second(w2_raw, on_vector):
-            bf = cast.tile([P, N, PACK], BF16, name="w2_bf", align_bytes=64)
-            out_codes = codes.tile([P, N], U32, name="w2_codes", align_bytes=64)
-            out_scales = codes.tile([P, N], U8, name="w2_scales", align_bytes=64)
-            copy = nc.vector.tensor_copy if on_vector else nc.scalar.copy
-            copy(
-                out=bf[:].rearrange("p (c i) j -> p c j i", i=RUN),
-                in_=w2_raw[:].rearrange("p j (c i) -> p c j i", i=RUN),
-            )
-            nc.vector.quantize_mx(out=out_codes[:].bitcast(FP8X4), scales=out_scales[:], in_=bf[:].rearrange("p c t -> p (c t)"))
-            return out_codes, out_scales
+        def second_product(e, acts, b_banks):
+            on_gpsimd = e in (1, 2)
+            if on_gpsimd:
+                bf = placed.tile([P, N + C, PACK], BF16, name=f"second_bf{e}", align_bytes=64, offset=e * REGION + 6 * KIB)
+            else:
+                bf = keep.tile([P, N + C, PACK], BF16, name=f"second_bf{e}", align_bytes=64)
+            both_codes = hid.tile([P, N + C], U32, name="second_codes", align_bytes=64)
+            both_scales = hid.tile([P, N + C], U8, name="second_scales", align_bytes=64)
+            w2_raw = raws[e]["w2"]
 
-        def second_product(weights, acts, b_banks):
-            bf = hid.tile([P, C, PACK], BF16, name="h_bf", align_bytes=64)
-            h_codes = hid.tile([P, C], U32, name="h_codes", align_bytes=64)
-            h_scales = hid.tile([P, C], U8, name="h_scales", align_bytes=64)
+            def quantize(cols):
+                nc.vector.quantize_mx(
+                    out=both_codes[:, cols].bitcast(FP8X4), scales=both_scales[:, cols], in_=bf[:, cols, :].rearrange("p c t -> p (c t)")
+                )
+
+            if on_gpsimd:
+                nc.gpsimd.tensor_scalar(out=bf[:, :N, :], in0=w2_raw[:].rearrange("p j c -> p c j"), scalar1=1.0, scalar2=0.0, op0=MULT, op1=ADD)
+            else:
+                nc.scalar.copy(
+                    out=bf[:, :N, :].rearrange("p (c i) j -> p c j i", i=RUN),
+                    in_=w2_raw[:].rearrange("p j (c i) -> p c j i", i=RUN),
+                )
+                quantize(slice(0, N))
             for s, bank in enumerate(b_banks):
                 nc.vector.tensor_tensor(
-                    out=bf[:, s * HALF:(s + 1) * HALF, :],
-                    in0=acts[s].rearrange("p (c t) -> p c t", t=PACK),
+                    out=bf[:, N + s * HALF:N + (s + 1) * HALF, :],
+                    in0=acts[s][:].rearrange("p (c t) -> p c t", t=PACK),
                     in1=bank[:].rearrange("p t c -> p c t"),
                     op=MULT,
                 )
-            nc.vector.quantize_mx(out=h_codes[:].bitcast(FP8X4), scales=h_scales[:], in_=bf[:].rearrange("p c t -> p (c t)"))
+            quantize(slice(0 if on_gpsimd else N, N + C))
             y_banks = []
             for b in range(N // P):
                 y_bank = psum_y.tile([P, C], F32, name="y_bank")
@@ -190,10 +212,10 @@ def tile_moe_two_glu_silu_kernel(tc, xT, w1, w3, w2, gate, offs, dst, out):
                 w_cols = slice(b * P, (b + 1) * P)
                 nc.tensor.matmul_mx(
                     out=y_bank[:],
-                    lhsT=weights[0][:, w_cols].bitcast(FP8X4),
-                    lhsT_scale=weights[1][:, w_cols],
-                    rhs=h_codes[:].bitcast(FP8X4),
-                    rhs_scale=h_scales[:],
+                    lhsT=both_codes[:, w_cols].bitcast(FP8X4),
+                    lhsT_scale=both_scales[:, w_cols],
+                    rhs=both_codes[:, N:].bitcast(FP8X4),
+                    rhs_scale=both_scales[:, N:],
                     start=True,
                     stop=True,
                 )
@@ -217,20 +239,18 @@ def tile_moe_two_glu_silu_kernel(tc, xT, w1, w3, w2, gate, offs, dst, out):
         slots.extend(quantize_slots(list(range(1, E)), "w3_bf"))
         y_banks = []
         for e in range(E):
-            home = raws[e]["w3"]
-            acts = [home[:, 1 + s, :] for s in range(C // HALF)]
+            acts = [
+                placed.tile([P, HALF * PACK], F32, name=f"act{e}_{s}", align_bytes=64, offset=e * REGION + 2 * s * KIB)
+                for s in range(C // HALF)
+            ]
             activate(a_banks, acts)
-            y_banks.append(second_product(quantize_second(raws[e]["w2"], W2_VECTOR[e]), acts, b_banks))
+            y_banks.append(second_product(e, acts, b_banks))
             if e + 1 < E:
-                a_banks = first_product("a_bank", slots[e + 1], quantize_first("w1", raws[e + 1]["w1"], W1_VECTOR[e + 1], cast))
-                if e == 0:
-                    scatter(e, y_banks[e], 0, raws[1]["w1"][:, 0, :C])
+                a_banks = first_product("a_bank", slots[e + 1], quantize_first("w1", raws[e + 1]["w1"], W1_VECTOR[e + 1], cast, 2 if e == 0 else 0))
                 b_banks = first_product("b_bank", slots[e + 1], quantize_first("w3", raws[e + 1]["w3"], W3_VECTOR[e + 1], cast))
-                spent = raws[e + 1]["w3"]
-                if e > 0:
-                    scatter(e, y_banks[e], 0, spent[:, 0, :C])
+                scatter(e, y_banks[e], 0, placed.tile([P, C], F32, name=f"y{e}_0", align_bytes=64, offset=(e + 1) * REGION + 6 * KIB)[:])
                 if e + 2 < E:
-                    scatter(e, y_banks[e], 1, spent[:, 0, C:])
+                    scatter(e, y_banks[e], 1, placed.tile([P, C], F32, name=f"y{e}_1", align_bytes=64, offset=(e + 1) * REGION + 4 * KIB)[:])
         scatter(E - 2, y_banks[E - 2], 1, acts[-1][:, :C])
         scatter(E - 1, y_banks[E - 1], 0, spare[:, 0, :])
         nc.sync.dma_start(out=out[:P, :], in_=windows[0][:])

@@ -18,13 +18,27 @@ ADD = mybir.AluOpType.add
 
 P = 128
 PACK = 4
-RUN = 2
-W1_VECTOR = (4, 0, 0, 0)
-W3_VECTOR = (4, 2, 0, 0)
+PAIR = 2
 HALF = 128
 LIST_COLS = C // 16
+
 KIB = 1024
+ACT_AT = (0, 2 * KIB)
+Y_AT = (6 * KIB, 4 * KIB)
+SECOND_AT = Y_AT[0]
 REGION = 10 * KIB
+
+
+def first_layer_shares(name, e):
+    if e == 0:
+        return 0, PACK
+    if e == 1:
+        return (PACK // 2, 0) if name == "w1" else (0, PACK // 2)
+    return 0, 0
+
+
+def round_on_gpsimd(nc, out, in_):
+    nc.gpsimd.tensor_scalar(out=out, in0=in_, scalar1=1.0, scalar2=0.0, op0=MULT, op1=ADD)
 
 
 def tile_moe_two_glu_silu_kernel(tc, xT, w1, w3, w2, gate, offs, dst, out):
@@ -33,10 +47,12 @@ def tile_moe_two_glu_silu_kernel(tc, xT, w1, w3, w2, gate, offs, dst, out):
         keep = ctx.enter_context(tc.tile_pool(name="keep", bufs=1))
         cast = ctx.enter_context(tc.tile_pool(name="cast", bufs=2))
         codes = ctx.enter_context(tc.tile_pool(name="codes", bufs=3))
-        hid = ctx.enter_context(tc.tile_pool(name="hid", bufs=3))
         placed = ctx.enter_context(tc.tile_pool(name="placed", bufs=1))
         psum = ctx.enter_context(tc.psum_pool(name="psum", bufs=2))
         psum_y = ctx.enter_context(tc.psum_pool(name="psum_y", bufs=4))
+
+        def in_region(e, at, shape, dtype, name):
+            return placed.tile(shape, dtype, name=name, align_bytes=64, offset=e * REGION + at)
 
         offs_sb = keep.tile([P, E * LIST_COLS], U16, name="offs_sb")
         dst_sb = keep.tile([P, E * LIST_COLS], U16, name="dst_sb")
@@ -67,25 +83,20 @@ def tile_moe_two_glu_silu_kernel(tc, xT, w1, w3, w2, gate, offs, dst, out):
         def load_gate(e):
             nc.sync.dma_start(out=gates[e][:], in_=gate[:P, e * C:(e + 1) * C])
 
-        raws = []
+        w1_raw, w3_raw, w2_raw = [], [], []
         for e in range(E):
-            tiles = {}
-            for name, w, width in (("w1", w1, H), ("w3", w3, H), ("w2", w2, N)):
-                if name == "w3":
-                    tiles[name] = placed.tile([P, PACK, width], F32, name=f"w3_raw{e}", align_bytes=64, offset=e * REGION)
-                else:
-                    tiles[name] = keep.tile([P, PACK, width], F32, name=f"{name}_raw{e}", align_bytes=64)
-                if name == "w2":
-                    rows = w[e].rearrange("(a t i) n -> i a t n", t=PACK, i=RUN)
-                    for i in range(RUN):
-                        nc.sync.dma_start(out=tiles[name][i:P:RUN, :, :], in_=rows[i])
-                else:
-                    nc.sync.dma_start(out=tiles[name][:], in_=w[e].rearrange("(p j) n -> p j n", j=PACK))
-                if e > 0 and name == ("w1" if e == 1 else "w3"):
-                    load_gate(e - 1)
+            w1_raw.append(keep.tile([P, PACK, H], F32, name=f"w1_raw{e}", align_bytes=64))
+            nc.sync.dma_start(out=w1_raw[e][:], in_=w1[e].rearrange("(p j) n -> p j n", j=PACK))
+            w3_raw.append(in_region(e, 0, [P, PACK, H], F32, f"w3_raw{e}"))
+            nc.sync.dma_start(out=w3_raw[e][:], in_=w3[e].rearrange("(p j) n -> p j n", j=PACK))
+            if e > 0:
+                load_gate(e - 1)
+            w2_raw.append(keep.tile([P, PACK, N], F32, name=f"w2_raw{e}", align_bytes=64))
+            rows = w2[e].rearrange("(a t r) n -> r a t n", t=PACK, r=PAIR)
+            for r in range(PAIR):
+                nc.sync.dma_start(out=w2_raw[e][r:P:PAIR, :, :], in_=rows[r])
             if e == 0:
                 nc.sync.dma_start(dst_sb[:], dst)
-            raws.append(tiles)
         load_gate(E - 1)
 
         nc.vector.memset(warm[:], 0.0)
@@ -95,19 +106,19 @@ def tile_moe_two_glu_silu_kernel(tc, xT, w1, w3, w2, gate, offs, dst, out):
 
         slot_bf = [keep.tile([P, C, PACK], BF16, name=f"slot_bf{e}", align_bytes=64) for e in range(E)]
 
-        def offsets(e):
-            return offs_sb[:, e * LIST_COLS:(e + 1) * LIST_COLS]
+        def entries(list_sb, e):
+            return list_sb[:, e * LIST_COLS:(e + 1) * LIST_COLS]
 
         def gather_on_scalar(j, tiles, copies):
             plane = keep.tile([P, T], BF16, name=f"x_bf{j}")
             for tile, cols, copy in zip(tiles, halves, copies):
                 copy(out=plane[:, cols], in_=tile[:])
             for e in range(E):
-                nc.scalar.activation(out=slot_bf[e][:, :, j], in_=plane[:].indirect(offsets(e)), func=COPY)
+                nc.scalar.activation(out=slot_bf[e][:, :, j], in_=plane[:].indirect(entries(offs_sb, e)), func=COPY)
 
         def gather_on_vector(j, plane):
             for e in range(E):
-                nc.vector.tensor_copy(out=slot_bf[e][:, :, j], in_=plane[:].indirect(offsets(e)))
+                nc.vector.tensor_copy(out=slot_bf[e][:, :, j], in_=plane[:].indirect(entries(offs_sb, e)))
 
         gather_on_vector(2, x_plane2)
         gather_on_scalar(0, x_plane0, (nc.scalar.copy, nc.scalar.copy))
@@ -116,143 +127,134 @@ def tile_moe_two_glu_silu_kernel(tc, xT, w1, w3, w2, gate, offs, dst, out):
 
         def quantize_slots(experts, tag):
             words = keep.tile([P, len(experts), C], U32, name=tag, align_bytes=64)
-            planes = keep.tile([P, len(experts), C], U8, name=f"slot_scales{experts[0]}", align_bytes=64)
+            scales = keep.tile([P, len(experts), C], U8, name=f"slot_scales{experts[0]}", align_bytes=64)
             for n, e in enumerate(experts):
                 nc.vector.quantize_mx(
-                    out=words[:, n, :].bitcast(FP8X4), scales=planes[:, n, :], in_=slot_bf[e][:].rearrange("p c j -> p (c j)")
+                    out=words[:, n, :].bitcast(FP8X4),
+                    scales=scales[:, n, :],
+                    in_=slot_bf[e][:].rearrange("p c j -> p (c j)"),
                 )
-            return [(words[:, n, :], planes[:, n, :]) for n in range(len(experts))]
+            return [(words[:, n, :], scales[:, n, :]) for n in range(len(experts))]
 
-        def round_first(name, raw, at, pool, on_gpsimd=0):
+        def round_first(name, e, raw, pool):
             bf = pool.tile([P, PACK, H // PACK, PACK], BF16, name=f"{name}_bf", align_bytes=64)
+            on_gpsimd, on_vector = first_layer_shares(name, e)
             for t in range(on_gpsimd):
-                nc.gpsimd.tensor_scalar(
-                    out=bf[:, t, :, :].rearrange("p (a i) j -> p a i j", i=RUN),
-                    in0=raw[:].rearrange("p j (a t i) -> p t a i j", t=PACK, i=RUN)[:, t],
-                    scalar1=1.0,
-                    scalar2=0.0,
-                    op0=MULT,
-                    op1=ADD,
+                round_on_gpsimd(
+                    nc,
+                    bf[:, t, :, :].rearrange("p (a r) j -> p a r j", r=PAIR),
+                    raw[:].rearrange("p j (a t r) -> p t a r j", t=PACK, r=PAIR)[:, t],
                 )
-            for a, b, copy in ((on_gpsimd, on_gpsimd + at, nc.vector.tensor_copy), (on_gpsimd + at, PACK, nc.scalar.copy)):
-                if a < b:
+            split = on_gpsimd + on_vector
+            for lo, hi, copy in ((on_gpsimd, split, nc.vector.tensor_copy), (split, PACK, nc.scalar.copy)):
+                if lo < hi:
                     copy(
-                        out=bf[:, a:b, :, :].rearrange("p t (a i) j -> p a t j i", i=RUN),
-                        in_=raw[:].rearrange("p j (a t i) -> p a t j i", t=PACK, i=RUN)[:, :, a:b],
+                        out=bf[:, lo:hi, :, :].rearrange("p t (a r) j -> p a t j r", r=PAIR),
+                        in_=raw[:].rearrange("p j (a t r) -> p a t j r", t=PACK, r=PAIR)[:, :, lo:hi],
                     )
             return bf
 
-        def quantize_rounded(name, bf):
-            out_codes = codes.tile([P, H], U32, name=f"{name}_codes", align_bytes=64)
-            out_scales = codes.tile([P, H], U8, name=f"{name}_scales", align_bytes=64)
-            nc.vector.quantize_mx(out=out_codes[:].bitcast(FP8X4), scales=out_scales[:], in_=bf[:].rearrange("p t m j -> p (t m j)"))
-            return out_codes, out_scales
-
-        def quantize_first(name, raw, at, pool, on_gpsimd=0):
-            return quantize_rounded(name, round_first(name, raw, at, pool, on_gpsimd))
-
-        def first_product(bank_name, slots, weights):
+        def first_product(name, bf, slots):
+            words = codes.tile([P, H], U32, name=f"{name}_codes", align_bytes=64)
+            scales = codes.tile([P, H], U8, name=f"{name}_scales", align_bytes=64)
+            nc.vector.quantize_mx(
+                out=words[:].bitcast(FP8X4), scales=scales[:], in_=bf[:].rearrange("p t m j -> p (t m j)")
+            )
+            slot_words, slot_scales = slots
             banks = []
             for s in range(C // HALF):
                 cols = slice(s * HALF, (s + 1) * HALF)
-                bank = psum.tile([P, PACK, HALF], F32, name=bank_name)
+                bank = psum.tile([P, PACK, HALF], F32, name=f"{name}_bank")
                 for t in range(PACK):
                     w_cols = slice(t * P, (t + 1) * P)
                     nc.tensor.matmul_mx(
                         out=bank[:, t, :],
-                        lhsT=weights[0][:, w_cols].bitcast(FP8X4),
-                        lhsT_scale=weights[1][:, w_cols],
-                        rhs=slots[0][:, cols].bitcast(FP8X4),
-                        rhs_scale=slots[1][:, cols],
+                        lhsT=words[:, w_cols].bitcast(FP8X4),
+                        lhsT_scale=scales[:, w_cols],
+                        rhs=slot_words[:, cols].bitcast(FP8X4),
+                        rhs_scale=slot_scales[:, cols],
                         start=True,
                         stop=True,
                     )
                 banks.append(bank)
             return banks
 
-        def activate(a_banks, acts):
-            for bank, act in zip(a_banks, acts):
-                nc.scalar.activation(out=act[:].rearrange("p (c t) -> p c t", t=PACK), in_=bank[:].rearrange("p t c -> p c t"), func=SILU)
+        def activate(e, w1_banks):
+            acts = [in_region(e, at, [P, HALF, PACK], F32, f"act{e}_{s}") for s, at in enumerate(ACT_AT)]
+            for bank, act in zip(w1_banks, acts):
+                nc.scalar.activation(out=act[:], in_=bank[:].rearrange("p t c -> p c t"), func=SILU)
+            return acts
 
-        def second_product(e, acts, b_banks):
-            on_gpsimd = e in (1, 2)
+        def second_product(e, acts, w3_banks):
+            on_gpsimd = 0 < e < E - 1
             if on_gpsimd:
-                bf = placed.tile([P, N + C, PACK], BF16, name=f"second_bf{e}", align_bytes=64, offset=e * REGION + 6 * KIB)
+                bf = in_region(e, SECOND_AT, [P, N + C, PACK], BF16, f"second_bf{e}")
             else:
                 bf = keep.tile([P, N + C, PACK], BF16, name=f"second_bf{e}", align_bytes=64)
-            both_codes = hid.tile([P, N + C], U32, name="second_codes", align_bytes=64)
-            both_scales = hid.tile([P, N + C], U8, name="second_scales", align_bytes=64)
-            w2_raw = raws[e]["w2"]
+            words = codes.tile([P, N + C], U32, name="second_codes", align_bytes=64)
+            scales = codes.tile([P, N + C], U8, name="second_scales", align_bytes=64)
 
             def quantize(cols):
                 nc.vector.quantize_mx(
-                    out=both_codes[:, cols].bitcast(FP8X4), scales=both_scales[:, cols], in_=bf[:, cols, :].rearrange("p c t -> p (c t)")
+                    out=words[:, cols].bitcast(FP8X4),
+                    scales=scales[:, cols],
+                    in_=bf[:, cols, :].rearrange("p c t -> p (c t)"),
                 )
 
             if on_gpsimd:
-                nc.gpsimd.tensor_scalar(out=bf[:, :N, :], in0=w2_raw[:].rearrange("p j c -> p c j"), scalar1=1.0, scalar2=0.0, op0=MULT, op1=ADD)
+                round_on_gpsimd(nc, bf[:, :N, :], w2_raw[e][:].rearrange("p t c -> p c t"))
             else:
                 nc.scalar.copy(
-                    out=bf[:, :N, :].rearrange("p (c i) j -> p c j i", i=RUN),
-                    in_=w2_raw[:].rearrange("p j (c i) -> p c j i", i=RUN),
+                    out=bf[:, :N, :].rearrange("p (c r) t -> p c t r", r=PAIR),
+                    in_=w2_raw[e][:].rearrange("p t (c r) -> p c t r", r=PAIR),
                 )
                 quantize(slice(0, N))
-            for s, bank in enumerate(b_banks):
+            for s, bank in enumerate(w3_banks):
                 nc.vector.tensor_tensor(
                     out=bf[:, N + s * HALF:N + (s + 1) * HALF, :],
-                    in0=acts[s][:].rearrange("p (c t) -> p c t", t=PACK),
+                    in0=acts[s][:],
                     in1=bank[:].rearrange("p t c -> p c t"),
                     op=MULT,
                 )
             quantize(slice(0 if on_gpsimd else N, N + C))
-            y_banks = []
+            banks = []
             for b in range(N // P):
-                y_bank = psum_y.tile([P, C], F32, name="y_bank")
-                y_banks.append(y_bank)
+                bank = psum_y.tile([P, C], F32, name="y_bank")
                 w_cols = slice(b * P, (b + 1) * P)
                 nc.tensor.matmul_mx(
-                    out=y_bank[:],
-                    lhsT=both_codes[:, w_cols].bitcast(FP8X4),
-                    lhsT_scale=both_scales[:, w_cols],
-                    rhs=both_codes[:, N:].bitcast(FP8X4),
-                    rhs_scale=both_scales[:, N:],
+                    out=bank[:],
+                    lhsT=words[:, w_cols].bitcast(FP8X4),
+                    lhsT_scale=scales[:, w_cols],
+                    rhs=words[:, N:].bitcast(FP8X4),
+                    rhs_scale=scales[:, N:],
                     start=True,
                     stop=True,
                 )
-            return y_banks
+                banks.append(bank)
+            return banks
 
-        def scatter(e, y_banks, b, y):
-            nc.scalar.copy(out=y, in_=y_banks[b][:])
-            at = slice(e * LIST_COLS, (e + 1) * LIST_COLS)
-            nc.vector.tensor_tensor(
-                out=windows[b][:].indirect(dst_sb[:, at]),
-                in0=y,
-                in1=gates[e][:],
-                op=MULT,
-            )
+        def scatter(e, b, y):
+            nc.scalar.copy(out=y, in_=y_banks[e][b][:])
+            nc.vector.tensor_tensor(out=windows[b][:].indirect(entries(dst_sb, e)), in0=y, in1=gates[e][:], op=MULT)
 
-        spare = keep.tile([P, 2, C], F32, name="spare")
-        rounded = round_first("w1", raws[0]["w1"], W1_VECTOR[0], cast)
+        last_y = keep.tile([P, N // P, C], F32, name="last_y")
+        rounded = round_first("w1", 0, w1_raw[0], cast)
         slots = quantize_slots([0], "w1_raw0")
-        a_banks = first_product("a_bank", slots[0], quantize_rounded("w1", rounded))
-        b_banks = first_product("b_bank", slots[0], quantize_first("w3", raws[0]["w3"], W3_VECTOR[0], keep))
+        w1_banks = first_product("w1", rounded, slots[0])
+        w3_banks = first_product("w3", round_first("w3", 0, w3_raw[0], keep), slots[0])
         slots.extend(quantize_slots(list(range(1, E)), "w3_bf"))
+
         y_banks = []
         for e in range(E):
-            acts = [
-                placed.tile([P, HALF * PACK], F32, name=f"act{e}_{s}", align_bytes=64, offset=e * REGION + 2 * s * KIB)
-                for s in range(C // HALF)
-            ]
-            activate(a_banks, acts)
-            y_banks.append(second_product(e, acts, b_banks))
+            acts = activate(e, w1_banks)
+            y_banks.append(second_product(e, acts, w3_banks))
             if e + 1 < E:
-                a_banks = first_product("a_bank", slots[e + 1], quantize_first("w1", raws[e + 1]["w1"], W1_VECTOR[e + 1], cast, 2 if e == 0 else 0))
-                b_banks = first_product("b_bank", slots[e + 1], quantize_first("w3", raws[e + 1]["w3"], W3_VECTOR[e + 1], cast))
-                scatter(e, y_banks[e], 0, placed.tile([P, C], F32, name=f"y{e}_0", align_bytes=64, offset=(e + 1) * REGION + 6 * KIB)[:])
-                if e + 2 < E:
-                    scatter(e, y_banks[e], 1, placed.tile([P, C], F32, name=f"y{e}_1", align_bytes=64, offset=(e + 1) * REGION + 4 * KIB)[:])
-        scatter(E - 2, y_banks[E - 2], 1, acts[-1][:, :C])
-        scatter(E - 1, y_banks[E - 1], 0, spare[:, 0, :])
-        nc.sync.dma_start(out=out[:P, :], in_=windows[0][:])
-        scatter(E - 1, y_banks[E - 1], 1, spare[:, 1, :])
-        nc.scalar.dma_start(out=out[P:, :], in_=windows[1][:])
+                w1_banks = first_product("w1", round_first("w1", e + 1, w1_raw[e + 1], cast), slots[e + 1])
+                w3_banks = first_product("w3", round_first("w3", e + 1, w3_raw[e + 1], cast), slots[e + 1])
+                for b in range(N // P if e + 2 < E else 1):
+                    scatter(e, b, in_region(e + 1, Y_AT[b], [P, C], F32, f"y{e}_{b}")[:])
+
+        scatter(E - 2, 1, acts[-1][:].rearrange("p c t -> p (c t)")[:, :C])
+        for b, queue in enumerate((nc.sync, nc.scalar)):
+            scatter(E - 1, b, last_y[:, b, :])
+            queue.dma_start(out=out[b * P:(b + 1) * P, :], in_=windows[b][:])

@@ -1,6 +1,7 @@
 from contextlib import ExitStack
 
 import concourse.mybir as mybir
+from concourse.masks import make_identity
 
 K, T, E, C, H, N = 512, 2048, 4, 256, 512, 256
 FLOPS = 2 * E * C * (2 * K * H + H * N)
@@ -20,21 +21,15 @@ P = 128
 PACK = 4
 PAIR = 2
 HALF = 128
+SLOTS_A_PARTITION = E * C // P
 LIST_COLS = C // 16
 
 KIB = 1024
-ACT_AT = (0, 2 * KIB)
-Y_AT = (6 * KIB, 4 * KIB)
+ACT_AT = (2 * KIB, 4 * KIB)
+Y_AT = (7 * KIB, 6 * KIB)
 SECOND_AT = Y_AT[0]
-REGION = 10 * KIB
-
-
-def first_layer_shares(name, e):
-    if e == 0:
-        return 0, PACK
-    if e == 1:
-        return (PACK // 2, 0) if name == "w1" else (0, PACK // 2)
-    return 0, 0
+HALF_AT = 7 * KIB // 2
+REGION = 9 * KIB
 
 
 def round_on_gpsimd(nc, out, in_):
@@ -58,7 +53,9 @@ def tile_moe_two_glu_silu_kernel(tc, xT, w1, w3, w2, gate, offs, dst, out):
         dst_sb = keep.tile([P, E * LIST_COLS], U16, name="dst_sb")
         warm = keep.tile([P, 1], F32, name="warm")
         windows = [keep.tile([P, T], F32, name=f"window{b}") for b in range(N // P)]
-        gates = [keep.tile([P, C], F32, name=f"gate{e}") for e in range(E)]
+        gates = keep.tile([P, E * C], F32, name="gates")
+        gate_cols = keep.tile([P, SLOTS_A_PARTITION], F32, name="gate_cols")
+        identity = keep.tile([P, P], F32, name="identity")
 
         x_rows = xT.rearrange("(p j) t -> p j t", j=PACK)
         halves = [slice(0, T // 2), slice(T // 2, T)]
@@ -74,35 +71,61 @@ def tile_moe_two_glu_silu_kernel(tc, xT, w1, w3, w2, gate, offs, dst, out):
             nc.sync.dma_start(out=tile[:], in_=x_rows[:, j, :])
             return tile
 
+        nc.sync.dma_start(out=gate_cols[:], in_=gate[0].rearrange("(p m) -> p m", m=SLOTS_A_PARTITION))
         x_plane2 = load_plane(2)
         nc.sync.dma_start(offs_sb[:], offs)
         x_plane0 = load_halves(0)
         x_plane3 = load_plane(3)
         x_plane1 = load_halves(1)
 
-        def load_gate(e):
-            nc.sync.dma_start(out=gates[e][:], in_=gate[:P, e * C:(e + 1) * C])
+        def load_first(w, e, tiles):
+            width = H // len(tiles)
+            for n, tile in enumerate(tiles):
+                rows = w[e].rearrange("(p j) n -> p j n", j=PACK)
+                nc.sync.dma_start(out=tile[:], in_=rows[:, :, n * width:(n + 1) * width])
+            return tiles
+
+        def load_second(e):
+            raw = keep.tile([P, PACK, N], F32, name=f"w2_raw{e}", align_bytes=64)
+            rows = w2[e].rearrange("(a t r) n -> r a t n", t=PACK, r=PAIR)
+            for r in range(PAIR):
+                nc.sync.dma_start(out=raw[r:P:PAIR, :, :], in_=rows[r])
+            return raw
+
+        def half_tile(name):
+            return keep.tile([P, PACK, H // 2], F32, name=name, align_bytes=64)
 
         w1_raw, w3_raw, w2_raw = [], [], []
         for e in range(E):
-            w1_raw.append(keep.tile([P, PACK, H], F32, name=f"w1_raw{e}", align_bytes=64))
-            nc.sync.dma_start(out=w1_raw[e][:], in_=w1[e].rearrange("(p j) n -> p j n", j=PACK))
-            w3_raw.append(in_region(e, 0, [P, PACK, H], F32, f"w3_raw{e}"))
-            nc.sync.dma_start(out=w3_raw[e][:], in_=w3[e].rearrange("(p j) n -> p j n", j=PACK))
-            if e > 0:
-                load_gate(e - 1)
-            w2_raw.append(keep.tile([P, PACK, N], F32, name=f"w2_raw{e}", align_bytes=64))
-            rows = w2[e].rearrange("(a t r) n -> r a t n", t=PACK, r=PAIR)
-            for r in range(PAIR):
-                nc.sync.dma_start(out=w2_raw[e][r:P:PAIR, :, :], in_=rows[r])
-            if e == 0:
+            if e in (0, 2):
+                w1_raw.append(load_first(w1, e, [half_tile(f"w1_raw{e}_0"), half_tile(f"w1_raw{e}_1")]))
+            else:
+                w1_raw.append(load_first(w1, e, [keep.tile([P, PACK, H], F32, name=f"w1_raw{e}", align_bytes=64)]))
+            if e == 1:
+                w2_raw.append(load_second(0))
                 nc.sync.dma_start(dst_sb[:], dst)
-        load_gate(E - 1)
+            if e == 0:
+                w3_raw.append(load_first(w3, e, [half_tile("w3_raw0_0"), half_tile("w3_raw0_1")]))
+            else:
+                last = in_region(e, HALF_AT, [P, PACK, H // 2], F32, f"w3_raw{e}_1")
+                w3_raw.append(load_first(w3, e, [half_tile(f"w3_raw{e}_0"), last]))
+            if e > 0:
+                w2_raw.append(load_second(e))
 
         nc.vector.memset(warm[:], 0.0)
         nc.scalar.activation(out=warm[:], in_=warm[:], func=SILU)
+        make_identity(nc, identity[:])
         nc.vector.memset(windows[0][:], 0.0)
         nc.gpsimd.memset(windows[1][:], 0.0)
+
+        for m0 in range(0, SLOTS_A_PARTITION, PACK):
+            bank = psum_y.tile([P, PACK, P], F32, name="y_bank")
+            for m in range(PACK):
+                nc.tensor.transpose(bank[:, m, :], gate_cols[:, m0 + m:m0 + m + 1].to_broadcast([P, P]), identity[:])
+            nc.vector.tensor_copy(
+                out=gates[:].rearrange("q (p m) -> q p m", m=SLOTS_A_PARTITION)[:, :, m0:m0 + PACK],
+                in_=bank[:].rearrange("q m p -> q p m"),
+            )
 
         slot_bf = [keep.tile([P, C, PACK], BF16, name=f"slot_bf{e}", align_bytes=64) for e in range(E)]
 
@@ -136,30 +159,58 @@ def tile_moe_two_glu_silu_kernel(tc, xT, w1, w3, w2, gate, offs, dst, out):
                 )
             return [(words[:, n, :], scales[:, n, :]) for n in range(len(experts))]
 
-        def round_first(name, e, raw, pool):
-            bf = pool.tile([P, PACK, H // PACK, PACK], BF16, name=f"{name}_bf", align_bytes=64)
-            on_gpsimd, on_vector = first_layer_shares(name, e)
-            for t in range(on_gpsimd):
-                round_on_gpsimd(
-                    nc,
-                    bf[:, t, :, :].rearrange("p (a r) j -> p a r j", r=PAIR),
-                    raw[:].rearrange("p j (a t r) -> p t a r j", t=PACK, r=PAIR)[:, t],
+        def round_first(bf, raws, copies):
+            width = P // len(raws)
+            for n, (raw, copy) in enumerate(zip(raws, copies)):
+                copy(
+                    out=bf[:, :, n * width:(n + 1) * width, :].rearrange("p t (a r) j -> p a t j r", r=PAIR),
+                    in_=raw[:].rearrange("p j (a t r) -> p a t j r", t=PACK, r=PAIR),
                 )
-            split = on_gpsimd + on_vector
-            for lo, hi, copy in ((on_gpsimd, split, nc.vector.tensor_copy), (split, PACK, nc.scalar.copy)):
-                if lo < hi:
-                    copy(
-                        out=bf[:, lo:hi, :, :].rearrange("p t (a r) j -> p a t j r", r=PAIR),
-                        in_=raw[:].rearrange("p j (a t r) -> p a t j r", t=PACK, r=PAIR)[:, :, lo:hi],
-                    )
-            return bf
+            return [bf]
 
-        def first_product(name, bf, slots):
-            words = codes.tile([P, H], U32, name=f"{name}_codes", align_bytes=64)
-            scales = codes.tile([P, H], U8, name=f"{name}_scales", align_bytes=64)
-            nc.vector.quantize_mx(
-                out=words[:].bitcast(FP8X4), scales=scales[:], in_=bf[:].rearrange("p t m j -> p (t m j)")
+        def rounded_tile(pool, name, tag):
+            return pool.tile([P, PACK, H // PACK, PACK], BF16, name=name, tag=tag, align_bytes=64)
+
+        def round_w1(e):
+            if e == 0:
+                return round_first(rounded_tile(cast, "w1_bf", "w1_bf"), w1_raw[e], [nc.vector.tensor_copy] * 2)
+            if e > 1:
+                return round_first(rounded_tile(cast, "w1_bf", "w1_bf"), w1_raw[e], [nc.scalar.copy] * 2)
+            raw = w1_raw[e][0]
+            low = keep.tile([P, PAIR, H // PACK, PACK], BF16, name="w1_low", align_bytes=64)
+            high = keep.tile([P, PAIR, H // PACK, PACK], BF16, name="w1_high", tag="slot_bf2", align_bytes=64)
+            nc.scalar.copy(
+                out=low[:].rearrange("p t (a r) j -> p a t j r", r=PAIR),
+                in_=raw[:].rearrange("p j (a t r) -> p a t j r", t=PACK, r=PAIR)[:, :, :PAIR],
             )
+            round_on_gpsimd(
+                nc,
+                high[:].rearrange("p t (a r) j -> p a t r j", r=PAIR),
+                raw[:].rearrange("p j (a t r) -> p a t r j", t=PACK, r=PAIR)[:, :, PAIR:],
+            )
+            return [low, high]
+
+        def round_w3(e):
+            if e == 0:
+                return round_first(rounded_tile(keep, "w3_bf0", "w3_bf0"), w3_raw[e], [nc.vector.tensor_copy] * 2)
+            copies = [nc.scalar.copy, nc.vector.tensor_copy] if e == 1 else [nc.scalar.copy] * 2
+            return round_first(rounded_tile(cast, "w3_bf", "w3_bf"), w3_raw[e], copies)
+
+        def first_product(name, pieces, slots):
+            scales = codes.tile([P, H], U8, name=f"{name}_scales", align_bytes=64)
+            width = H // len(pieces)
+            quarters = []
+            for n, bf in enumerate(pieces):
+                if n == 0:
+                    words = codes.tile([P, width], U32, name=f"{name}_codes", align_bytes=64)
+                else:
+                    words = keep.tile([P, width], U32, name="w1_high_codes", tag="w3_raw1_0", align_bytes=64)
+                nc.vector.quantize_mx(
+                    out=words[:].bitcast(FP8X4),
+                    scales=scales[:, n * width:(n + 1) * width],
+                    in_=bf[:].rearrange("p t m j -> p (t m j)"),
+                )
+                quarters.extend(words[:, c:c + P] for c in range(0, width, P))
             slot_words, slot_scales = slots
             banks = []
             for s in range(C // HALF):
@@ -169,7 +220,7 @@ def tile_moe_two_glu_silu_kernel(tc, xT, w1, w3, w2, gate, offs, dst, out):
                     w_cols = slice(t * P, (t + 1) * P)
                     nc.tensor.matmul_mx(
                         out=bank[:, t, :],
-                        lhsT=words[:, w_cols].bitcast(FP8X4),
+                        lhsT=quarters[t].bitcast(FP8X4),
                         lhsT_scale=scales[:, w_cols],
                         rhs=slot_words[:, cols].bitcast(FP8X4),
                         rhs_scale=slot_scales[:, cols],
@@ -186,37 +237,41 @@ def tile_moe_two_glu_silu_kernel(tc, xT, w1, w3, w2, gate, offs, dst, out):
             return acts
 
         def second_product(e, acts, w3_banks):
-            on_gpsimd = 0 < e < E - 1
-            if on_gpsimd:
-                bf = in_region(e, SECOND_AT, [P, N + C, PACK], BF16, f"second_bf{e}")
-            else:
-                bf = keep.tile([P, N + C, PACK], BF16, name=f"second_bf{e}", align_bytes=64)
-            words = codes.tile([P, N + C], U32, name="second_codes", align_bytes=64)
-            scales = codes.tile([P, N + C], U8, name="second_scales", align_bytes=64)
+            h_bf = cast.tile([P, C, PACK], BF16, name="h_bf", align_bytes=64)
+            h_scales = codes.tile([P, C], U8, name="h_scales", align_bytes=64)
+            scales = codes.tile([P, N], U8, name="w2_scales", align_bytes=64)
 
-            def quantize(cols):
+            def quantize(words, scales, bf):
                 nc.vector.quantize_mx(
-                    out=words[:, cols].bitcast(FP8X4),
-                    scales=scales[:, cols],
-                    in_=bf[:, cols, :].rearrange("p c t -> p (c t)"),
+                    out=words[:].bitcast(FP8X4), scales=scales[:], in_=bf[:].rearrange("p c t -> p (c t)")
                 )
 
-            if on_gpsimd:
-                round_on_gpsimd(nc, bf[:, :N, :], w2_raw[e][:].rearrange("p t c -> p c t"))
+            if 0 < e < E - 1:
+                bf = in_region(e, SECOND_AT, [P, N, PACK], BF16, f"w2_bf{e}")
+                round_on_gpsimd(nc, bf[:], w2_raw[e][:].rearrange("p t c -> p c t"))
             else:
+                bf = keep.tile([P, N, PACK], BF16, name=f"w2_bf{e}", align_bytes=64)
                 nc.scalar.copy(
-                    out=bf[:, :N, :].rearrange("p (c r) t -> p c t r", r=PAIR),
+                    out=bf[:].rearrange("p (c r) t -> p c t r", r=PAIR),
                     in_=w2_raw[e][:].rearrange("p t (c r) -> p c t r", r=PAIR),
                 )
-                quantize(slice(0, N))
             for s, bank in enumerate(w3_banks):
                 nc.vector.tensor_tensor(
-                    out=bf[:, N + s * HALF:N + (s + 1) * HALF, :],
+                    out=h_bf[:, s * HALF:(s + 1) * HALF, :],
                     in0=acts[s][:],
                     in1=bank[:].rearrange("p t c -> p c t"),
                     op=MULT,
                 )
-            quantize(slice(0 if on_gpsimd else N, N + C))
+            if e == E - 1:
+                words = codes.tile([P, N], U32, name="w2_codes", align_bytes=64)
+                quantize(words, scales, bf)
+                h_words = keep.tile([P, C], U32, name="last_h_codes", tag=f"w2_raw{e}", align_bytes=64)
+                quantize(h_words, h_scales, h_bf)
+            else:
+                h_words = codes.tile([P, C], U32, name="h_codes", align_bytes=64)
+                quantize(h_words, h_scales, h_bf)
+                words = in_region(e, ACT_AT[1], [P, N], U32, f"w2_codes{e}")
+                quantize(words, scales, bf)
             banks = []
             for b in range(N // P):
                 bank = psum_y.tile([P, C], F32, name="y_bank")
@@ -225,8 +280,8 @@ def tile_moe_two_glu_silu_kernel(tc, xT, w1, w3, w2, gate, offs, dst, out):
                     out=bank[:],
                     lhsT=words[:, w_cols].bitcast(FP8X4),
                     lhsT_scale=scales[:, w_cols],
-                    rhs=words[:, N:].bitcast(FP8X4),
-                    rhs_scale=scales[:, N:],
+                    rhs=h_words[:].bitcast(FP8X4),
+                    rhs_scale=h_scales[:],
                     start=True,
                     stop=True,
                 )
@@ -235,26 +290,27 @@ def tile_moe_two_glu_silu_kernel(tc, xT, w1, w3, w2, gate, offs, dst, out):
 
         def scatter(e, b, y):
             nc.scalar.copy(out=y, in_=y_banks[e][b][:])
-            nc.vector.tensor_tensor(out=windows[b][:].indirect(entries(dst_sb, e)), in0=y, in1=gates[e][:], op=MULT)
+            nc.vector.tensor_tensor(out=windows[b][:].indirect(entries(dst_sb, e)), in0=y, in1=gates[:, e * C:(e + 1) * C], op=MULT)
 
         last_y = keep.tile([P, N // P, C], F32, name="last_y")
-        rounded = round_first("w1", 0, w1_raw[0], cast)
-        slots = quantize_slots([0], "w1_raw0")
+        rounded = round_w1(0)
+        slots = quantize_slots([0], "w1_raw0_1")
         w1_banks = first_product("w1", rounded, slots[0])
-        w3_banks = first_product("w3", round_first("w3", 0, w3_raw[0], keep), slots[0])
-        slots.extend(quantize_slots(list(range(1, E)), "w3_bf"))
+        w3_banks = first_product("w3", round_w3(0), slots[0])
+        slots.extend(quantize_slots(list(range(1, E)), "w3_bf0"))
 
         y_banks = []
         for e in range(E):
             acts = activate(e, w1_banks)
             y_banks.append(second_product(e, acts, w3_banks))
             if e + 1 < E:
-                w1_banks = first_product("w1", round_first("w1", e + 1, w1_raw[e + 1], cast), slots[e + 1])
-                w3_banks = first_product("w3", round_first("w3", e + 1, w3_raw[e + 1], cast), slots[e + 1])
+                w1_bf, w3_bf = round_w1(e + 1), round_w3(e + 1)
+                w1_banks = first_product("w1", w1_bf, slots[e + 1])
+                w3_banks = first_product("w3", w3_bf, slots[e + 1])
                 for b in range(N // P if e + 2 < E else 1):
                     scatter(e, b, in_region(e + 1, Y_AT[b], [P, C], F32, f"y{e}_{b}")[:])
 
-        scatter(E - 2, 1, acts[-1][:].rearrange("p c t -> p (c t)")[:, :C])
+        scatter(E - 2, 1, acts[0][:].rearrange("p c t -> p (c t)")[:, :C])
         for b, queue in enumerate((nc.sync, nc.scalar)):
             scatter(E - 1, b, last_y[:, b, :])
             queue.dma_start(out=out[b * P:(b + 1) * P, :], in_=windows[b][:])

@@ -71,7 +71,7 @@ def tile_moe_two_glu_silu_kernel(tc, xT, w1, w3, w2, gate, offs, dst, out):
             nc.sync.dma_start(out=tile[:], in_=x_rows[:, j, :])
             return tile
 
-        nc.sync.dma_start(out=gate_cols[:], in_=gate[0].rearrange("(p m) -> p m", m=SLOTS_A_PARTITION))
+        nc.scalar.dma_start(out=gate_cols[:], in_=gate[0].rearrange("(p m) -> p m", m=SLOTS_A_PARTITION))
         x_plane2 = load_plane(2)
         nc.sync.dma_start(offs_sb[:], offs)
         x_plane0 = load_halves(0)
@@ -97,7 +97,7 @@ def tile_moe_two_glu_silu_kernel(tc, xT, w1, w3, w2, gate, offs, dst, out):
 
         w1_raw, w3_raw, w2_raw = [], [], []
         for e in range(E):
-            if e in (0, 2):
+            if e == 2:
                 w1_raw.append(load_first(w1, e, [half_tile(f"w1_raw{e}_0"), half_tile(f"w1_raw{e}_1")]))
             else:
                 w1_raw.append(load_first(w1, e, [keep.tile([P, PACK, H], F32, name=f"w1_raw{e}", align_bytes=64)]))
@@ -105,7 +105,7 @@ def tile_moe_two_glu_silu_kernel(tc, xT, w1, w3, w2, gate, offs, dst, out):
                 w2_raw.append(load_second(0))
                 nc.sync.dma_start(dst_sb[:], dst)
             if e == 0:
-                w3_raw.append(load_first(w3, e, [half_tile("w3_raw0_0"), half_tile("w3_raw0_1")]))
+                w3_raw.append(load_first(w3, e, [keep.tile([P, PACK, H], F32, name="w3_raw0", align_bytes=64)]))
             else:
                 last = in_region(e, HALF_AT, [P, PACK, H // 2], F32, f"w3_raw{e}_1")
                 w3_raw.append(load_first(w3, e, [half_tile(f"w3_raw{e}_0"), last]))
@@ -115,14 +115,14 @@ def tile_moe_two_glu_silu_kernel(tc, xT, w1, w3, w2, gate, offs, dst, out):
         nc.vector.memset(warm[:], 0.0)
         nc.scalar.activation(out=warm[:], in_=warm[:], func=SILU)
         make_identity(nc, identity[:])
-        nc.vector.memset(windows[0][:], 0.0)
-        nc.gpsimd.memset(windows[1][:], 0.0)
+        for window in windows:
+            nc.vector.memset(window[:], 0.0)
 
         for m0 in range(0, SLOTS_A_PARTITION, PACK):
             bank = psum_y.tile([P, PACK, P], F32, name="y_bank")
             for m in range(PACK):
                 nc.tensor.transpose(bank[:, m, :], gate_cols[:, m0 + m:m0 + m + 1].to_broadcast([P, P]), identity[:])
-            nc.vector.tensor_copy(
+            nc.scalar.copy(
                 out=gates[:].rearrange("q (p m) -> q p m", m=SLOTS_A_PARTITION)[:, :, m0:m0 + PACK],
                 in_=bank[:].rearrange("q m p -> q p m"),
             )
@@ -171,9 +171,20 @@ def tile_moe_two_glu_silu_kernel(tc, xT, w1, w3, w2, gate, offs, dst, out):
         def rounded_tile(pool, name, tag):
             return pool.tile([P, PACK, H // PACK, PACK], BF16, name=name, tag=tag, align_bytes=64)
 
+        def round_on_vector(name, raw):
+            pieces = []
+            for n in range(2):
+                bf = keep.tile([P, PAIR, H // PACK, PACK], BF16, name=f"{name}_{n}", align_bytes=64)
+                nc.vector.tensor_copy(
+                    out=bf[:].rearrange("p t (a r) j -> p a t j r", r=PAIR),
+                    in_=raw[:].rearrange("p j (a t r) -> p a t j r", t=PACK, r=PAIR)[:, :, n * PAIR:(n + 1) * PAIR],
+                )
+                pieces.append(bf)
+            return pieces
+
         def round_w1(e):
             if e == 0:
-                return round_first(rounded_tile(cast, "w1_bf", "w1_bf"), w1_raw[e], [nc.vector.tensor_copy] * 2)
+                return round_on_vector("w1_bf0", w1_raw[e][0])
             if e > 1:
                 return round_first(rounded_tile(cast, "w1_bf", "w1_bf"), w1_raw[e], [nc.scalar.copy] * 2)
             raw = w1_raw[e][0]
@@ -183,34 +194,39 @@ def tile_moe_two_glu_silu_kernel(tc, xT, w1, w3, w2, gate, offs, dst, out):
                 out=low[:].rearrange("p t (a r) j -> p a t j r", r=PAIR),
                 in_=raw[:].rearrange("p j (a t r) -> p a t j r", t=PACK, r=PAIR)[:, :, :PAIR],
             )
-            round_on_gpsimd(
-                nc,
-                high[:].rearrange("p t (a r) j -> p a t r j", r=PAIR),
-                raw[:].rearrange("p j (a t r) -> p a t r j", t=PACK, r=PAIR)[:, :, PAIR:],
-            )
+            for t in range(PAIR):
+                round_on_gpsimd(
+                    nc,
+                    high[:, t].rearrange("p (a r) j -> p a r j", r=PAIR),
+                    raw[:].rearrange("p j (a t r) -> p t a r j", t=PACK, r=PAIR)[:, PAIR + t],
+                )
             return [low, high]
 
         def round_w3(e):
             if e == 0:
-                return round_first(rounded_tile(keep, "w3_bf0", "w3_bf0"), w3_raw[e], [nc.vector.tensor_copy] * 2)
+                return round_on_vector("w3_bf0", w3_raw[e][0])
             copies = [nc.scalar.copy, nc.vector.tensor_copy] if e == 1 else [nc.scalar.copy] * 2
             return round_first(rounded_tile(cast, "w3_bf", "w3_bf"), w3_raw[e], copies)
 
-        def first_product(name, pieces, slots):
+        def quantize_first(name, pieces, last_behind=None):
             scales = codes.tile([P, H], U8, name=f"{name}_scales", align_bytes=64)
             width = H // len(pieces)
             quarters = []
             for n, bf in enumerate(pieces):
-                if n == 0:
-                    words = codes.tile([P, width], U32, name=f"{name}_codes", align_bytes=64)
+                if n > 0 and last_behind:
+                    words = keep.tile([P, width], U32, name="w1_high_codes", tag=last_behind, align_bytes=64)
                 else:
-                    words = keep.tile([P, width], U32, name="w1_high_codes", tag="w3_raw1_0", align_bytes=64)
+                    words = codes.tile([P, width], U32, name=f"{name}_codes", align_bytes=64)
                 nc.vector.quantize_mx(
                     out=words[:].bitcast(FP8X4),
                     scales=scales[:, n * width:(n + 1) * width],
                     in_=bf[:].rearrange("p t m j -> p (t m j)"),
                 )
                 quarters.extend(words[:, c:c + P] for c in range(0, width, P))
+            return quarters, scales
+
+        def first_product(name, matrix, slots):
+            quarters, scales = matrix
             slot_words, slot_scales = slots
             banks = []
             for s in range(C // HALF):
@@ -293,11 +309,11 @@ def tile_moe_two_glu_silu_kernel(tc, xT, w1, w3, w2, gate, offs, dst, out):
             nc.vector.tensor_tensor(out=windows[b][:].indirect(entries(dst_sb, e)), in0=y, in1=gates[:, e * C:(e + 1) * C], op=MULT)
 
         last_y = keep.tile([P, N // P, C], F32, name="last_y")
-        rounded = round_w1(0)
-        slots = quantize_slots([0], "w1_raw0_1")
-        w1_banks = first_product("w1", rounded, slots[0])
-        w3_banks = first_product("w3", round_w3(0), slots[0])
-        slots.extend(quantize_slots(list(range(1, E)), "w3_bf0"))
+        matrix = quantize_first("w1", round_w1(0))
+        slots = quantize_slots([0], "w1_bf0_0")
+        w1_banks = first_product("w1", matrix, slots[0])
+        w3_banks = first_product("w3", quantize_first("w3", round_w3(0)), slots[0])
+        slots.extend(quantize_slots(list(range(1, E)), "w3_bf0_0"))
 
         y_banks = []
         for e in range(E):
@@ -305,8 +321,8 @@ def tile_moe_two_glu_silu_kernel(tc, xT, w1, w3, w2, gate, offs, dst, out):
             y_banks.append(second_product(e, acts, w3_banks))
             if e + 1 < E:
                 w1_bf, w3_bf = round_w1(e + 1), round_w3(e + 1)
-                w1_banks = first_product("w1", w1_bf, slots[e + 1])
-                w3_banks = first_product("w3", w3_bf, slots[e + 1])
+                w1_banks = first_product("w1", quantize_first("w1", w1_bf, "w3_raw1_0"), slots[e + 1])
+                w3_banks = first_product("w3", quantize_first("w3", w3_bf), slots[e + 1])
                 for b in range(N // P if e + 2 < E else 1):
                     scatter(e, b, in_region(e + 1, Y_AT[b], [P, C], F32, f"y{e}_{b}")[:])
 

@@ -9,6 +9,7 @@ FLOPS = 2 * E * C * (2 * K * H + H * N)
 F32 = mybir.dt.float32
 BF16 = mybir.dt.bfloat16
 U32 = mybir.dt.uint32
+I32 = mybir.dt.int32
 U16 = mybir.dt.uint16
 U8 = mybir.dt.uint8
 FP8X4 = mybir.dt.float8_e4m3fn_x4
@@ -60,11 +61,10 @@ def tile_moe_two_glu_silu_kernel(tc, xT, w1, w3, w2, gate, offs, dst, out):
         x_rows = xT.rearrange("(p j) t -> p j t", j=PACK)
         halves = [slice(0, T // 2), slice(T // 2, T)]
 
-        def load_halves(j):
-            tiles = [keep.tile([P, T // 2], F32, name=f"x_half{j}_{h}") for h in range(2)]
-            for tile, cols in zip(tiles, halves):
-                nc.sync.dma_start(out=tile[:], in_=x_rows[:, j, cols])
-            return tiles
+        def load_half(j, h):
+            tile = keep.tile([P, T // 2], F32, name=f"x_half{j}_{h}", align_bytes=64)
+            nc.sync.dma_start(out=tile[:], in_=x_rows[:, j, halves[h]])
+            return tile
 
         def load_plane(j):
             tile = keep.tile([P, T], F32, name=f"x_plane{j}")
@@ -74,9 +74,10 @@ def tile_moe_two_glu_silu_kernel(tc, xT, w1, w3, w2, gate, offs, dst, out):
         nc.scalar.dma_start(out=gate_cols[:], in_=gate[0].rearrange("(p m) -> p m", m=SLOTS_A_PARTITION))
         x_plane2 = load_plane(2)
         nc.sync.dma_start(offs_sb[:], offs)
-        x_plane0 = load_halves(0)
+        x_plane0 = [load_half(0, 0), load_half(0, 1)]
+        x_plane1 = [load_half(1, 0)]
         x_plane3 = load_plane(3)
-        x_plane1 = load_halves(1)
+        x_plane1.append(load_half(1, 1))
 
         def load_first(w, e, tiles):
             width = H // len(tiles)
@@ -127,7 +128,7 @@ def tile_moe_two_glu_silu_kernel(tc, xT, w1, w3, w2, gate, offs, dst, out):
                 in_=bank[:].rearrange("q m p -> q p m"),
             )
 
-        slot_bf = [keep.tile([P, C, PACK], BF16, name=f"slot_bf{e}", align_bytes=64) for e in range(E)]
+        pairs = [keep.tile([P, PAIR, C, PAIR], BF16, name=f"pairs{e}", align_bytes=64) for e in range(E)]
 
         def entries(list_sb, e):
             return list_sb[:, e * LIST_COLS:(e + 1) * LIST_COLS]
@@ -137,16 +138,28 @@ def tile_moe_two_glu_silu_kernel(tc, xT, w1, w3, w2, gate, offs, dst, out):
             for tile, cols, copy in zip(tiles, halves, copies):
                 copy(out=plane[:, cols], in_=tile[:])
             for e in range(E):
-                nc.scalar.activation(out=slot_bf[e][:, :, j], in_=plane[:].indirect(entries(offs_sb, e)), func=COPY)
+                nc.scalar.activation(out=pairs[e][:, 0, :, j], in_=plane[:].indirect(entries(offs_sb, e)), func=COPY)
 
         def gather_on_vector(j, plane):
             for e in range(E):
-                nc.vector.tensor_copy(out=slot_bf[e][:, :, j], in_=plane[:].indirect(entries(offs_sb, e)))
+                nc.vector.tensor_copy(out=pairs[e][:, 1, :, j - PAIR], in_=plane[:].indirect(entries(offs_sb, e)))
 
         gather_on_vector(2, x_plane2)
         gather_on_scalar(0, x_plane0, (nc.scalar.copy, nc.scalar.copy))
+        gather_on_scalar(1, x_plane1, (nc.vector.tensor_copy, nc.scalar.copy))
         gather_on_vector(3, x_plane3)
-        gather_on_scalar(1, x_plane1, (nc.scalar.copy, nc.vector.tensor_copy))
+
+        slot_bf = {}
+
+        def weave(e, copy, word, tag):
+            slot_bf[e] = keep.tile([P, C, PACK], BF16, name=f"slot_bf{e}", tag=tag, align_bytes=64)
+            copy(
+                out=slot_bf[e][:].rearrange("p c j -> p (c j)").bitcast(word).rearrange("p (c u) -> p c u", u=PAIR),
+                in_=pairs[e][:].rearrange("p u c j -> p (u c j)").bitcast(word).rearrange("p (u c) -> p c u", u=PAIR),
+            )
+
+        for e, tag in ((1, "x_half0_0"), (2, "x_half0_1"), (3, "x_half1_1")):
+            weave(e, nc.scalar.copy, U32, tag)
 
         def quantize_slots(experts, tag):
             words = keep.tile([P, len(experts), C], U32, name=tag, align_bytes=64)
@@ -189,7 +202,7 @@ def tile_moe_two_glu_silu_kernel(tc, xT, w1, w3, w2, gate, offs, dst, out):
                 return round_first(rounded_tile(cast, "w1_bf", "w1_bf"), w1_raw[e], [nc.scalar.copy] * 2)
             raw = w1_raw[e][0]
             low = keep.tile([P, PAIR, H // PACK, PACK], BF16, name="w1_low", align_bytes=64)
-            high = keep.tile([P, PAIR, H // PACK, PACK], BF16, name="w1_high", tag="slot_bf2", align_bytes=64)
+            high = keep.tile([P, PAIR, H // PACK, PACK], BF16, name="w1_high", tag="x_half0_0", align_bytes=64)
             nc.scalar.copy(
                 out=low[:].rearrange("p t (a r) j -> p a t j r", r=PAIR),
                 in_=raw[:].rearrange("p j (a t r) -> p a t j r", t=PACK, r=PAIR)[:, :, :PAIR],
@@ -309,11 +322,13 @@ def tile_moe_two_glu_silu_kernel(tc, xT, w1, w3, w2, gate, offs, dst, out):
             nc.vector.tensor_tensor(out=windows[b][:].indirect(entries(dst_sb, e)), in0=y, in1=gates[:, e * C:(e + 1) * C], op=MULT)
 
         last_y = keep.tile([P, N // P, C], F32, name="last_y")
-        matrix = quantize_first("w1", round_w1(0))
+        rounded = round_w1(0)
+        weave(0, nc.vector.tensor_copy, I32, "w1_raw0")
+        matrix = quantize_first("w1", rounded)
         slots = quantize_slots([0], "w1_bf0_0")
         w1_banks = first_product("w1", matrix, slots[0])
         w3_banks = first_product("w3", quantize_first("w3", round_w3(0)), slots[0])
-        slots.extend(quantize_slots(list(range(1, E)), "w3_bf0_0"))
+        slots.extend(quantize_slots([1, 2], "w3_bf0_0"))
 
         y_banks = []
         for e in range(E):
@@ -321,7 +336,9 @@ def tile_moe_two_glu_silu_kernel(tc, xT, w1, w3, w2, gate, offs, dst, out):
             y_banks.append(second_product(e, acts, w3_banks))
             if e + 1 < E:
                 w1_bf, w3_bf = round_w1(e + 1), round_w3(e + 1)
-                w1_banks = first_product("w1", quantize_first("w1", w1_bf, "w3_raw1_0"), slots[e + 1])
+                w1_banks = first_product("w1", quantize_first("w1", w1_bf), slots[e + 1])
+                if e == 0:
+                    slots.extend(quantize_slots([E - 1], "w3_raw1_0"))
                 w3_banks = first_product("w3", quantize_first("w3", w3_bf), slots[e + 1])
                 for b in range(N // P if e + 2 < E else 1):
                     scatter(e, b, in_region(e + 1, Y_AT[b], [P, C], F32, f"y{e}_{b}")[:])

@@ -21,16 +21,20 @@ ADD = mybir.AluOpType.add
 P = 128
 PACK = 4
 PAIR = 2
-HALF = 128
-SLOTS_A_PARTITION = E * C // P
+BANK_SLOTS = 128
+GATE_COLS = E * C // P
 LIST_COLS = C // 16
+LAST = E - 1
 
 KIB = 1024
+W3_HALF_AT = 7 * KIB // 2
 ACT_AT = (2 * KIB, 4 * KIB)
 Y_AT = (7 * KIB, 6 * KIB)
-SECOND_AT = Y_AT[0]
-HALF_AT = 7 * KIB // 2
+W2_BF_AT = Y_AT[0]
+W2_CODES_AT = ACT_AT[1]
 REGION = 9 * KIB
+
+X_CUTS = {0: (0, T // 2, T), 1: (0, T // 2, 3 * T // 4, T)}
 
 
 def round_on_gpsimd(nc, out, in_):
@@ -47,23 +51,31 @@ def tile_moe_two_glu_silu_kernel(tc, xT, w1, w3, w2, gate, offs, dst, out):
         psum = ctx.enter_context(tc.psum_pool(name="psum", bufs=2))
         psum_y = ctx.enter_context(tc.psum_pool(name="psum_y", bufs=4))
 
-        def in_region(e, at, shape, dtype, name):
-            return placed.tile(shape, dtype, name=name, align_bytes=64, offset=e * REGION + at)
+        def kept(shape, dtype, name, behind=""):
+            return keep.tile(shape, dtype, name=name, tag=behind or name, align_bytes=64)
+
+        def in_region(region, at, shape, dtype, name):
+            return placed.tile(shape, dtype, name=name, align_bytes=64, offset=region * REGION + at)
+
+        def quantize(words, scales, values):
+            nc.vector.quantize_mx(out=words.bitcast(FP8X4), scales=scales, in_=values)
 
         offs_sb = keep.tile([P, E * LIST_COLS], U16, name="offs_sb")
         dst_sb = keep.tile([P, E * LIST_COLS], U16, name="dst_sb")
         warm = keep.tile([P, 1], F32, name="warm")
         windows = [keep.tile([P, T], F32, name=f"window{b}") for b in range(N // P)]
         gates = keep.tile([P, E * C], F32, name="gates")
-        gate_cols = keep.tile([P, SLOTS_A_PARTITION], F32, name="gate_cols")
+        gate_cols = keep.tile([P, GATE_COLS], F32, name="gate_cols")
         identity = keep.tile([P, P], F32, name="identity")
 
-        x_rows = xT.rearrange("(p j) t -> p j t", j=PACK)
-        halves = [slice(0, T // 2), slice(T // 2, T)]
+        nc.scalar.dma_start(out=gate_cols[:], in_=gate[0].rearrange("(p m) -> p m", m=GATE_COLS))
 
-        def load_half(j, h):
-            tile = keep.tile([P, T // 2], F32, name=f"x_half{j}_{h}", align_bytes=64)
-            nc.sync.dma_start(out=tile[:], in_=x_rows[:, j, halves[h]])
+        x_rows = xT.rearrange("(p j) t -> p j t", j=PACK)
+
+        def load_piece(j, n):
+            lo, hi = X_CUTS[j][n:n + 2]
+            tile = kept([P, hi - lo], F32, f"x_piece{j}_{n}")
+            nc.sync.dma_start(out=tile[:], in_=x_rows[:, j, lo:hi])
             return tile
 
         def load_plane(j):
@@ -71,13 +83,12 @@ def tile_moe_two_glu_silu_kernel(tc, xT, w1, w3, w2, gate, offs, dst, out):
             nc.sync.dma_start(out=tile[:], in_=x_rows[:, j, :])
             return tile
 
-        nc.scalar.dma_start(out=gate_cols[:], in_=gate[0].rearrange("(p m) -> p m", m=SLOTS_A_PARTITION))
-        x_plane2 = load_plane(2)
+        x_plane0 = [load_piece(0, 0), load_piece(0, 1)]
         nc.sync.dma_start(offs_sb[:], offs)
-        x_plane0 = [load_half(0, 0), load_half(0, 1)]
-        x_plane1 = [load_half(1, 0)]
+        x_plane2 = load_plane(2)
+        x_plane1 = [load_piece(1, 0)]
         x_plane3 = load_plane(3)
-        x_plane1.append(load_half(1, 1))
+        x_plane1.extend([load_piece(1, 1), load_piece(1, 2)])
 
         def load_first(w, e, tiles):
             width = H // len(tiles)
@@ -87,31 +98,28 @@ def tile_moe_two_glu_silu_kernel(tc, xT, w1, w3, w2, gate, offs, dst, out):
             return tiles
 
         def load_second(e):
-            raw = keep.tile([P, PACK, N], F32, name=f"w2_raw{e}", align_bytes=64)
+            raw = kept([P, PACK, N], F32, f"w2_raw{e}")
             rows = w2[e].rearrange("(a t r) n -> r a t n", t=PACK, r=PAIR)
             for r in range(PAIR):
                 nc.sync.dma_start(out=raw[r:P:PAIR, :, :], in_=rows[r])
             return raw
 
-        def half_tile(name):
-            return keep.tile([P, PACK, H // 2], F32, name=name, align_bytes=64)
-
+        whole, half = [P, PACK, H], [P, PACK, H // 2]
         w1_raw, w3_raw, w2_raw = [], [], []
         for e in range(E):
             if e == 2:
-                w1_raw.append(load_first(w1, e, [half_tile(f"w1_raw{e}_0"), half_tile(f"w1_raw{e}_1")]))
+                w1_raw.append(load_first(w1, e, [kept(half, F32, f"w1_raw{e}_{h}") for h in range(2)]))
             else:
-                w1_raw.append(load_first(w1, e, [keep.tile([P, PACK, H], F32, name=f"w1_raw{e}", align_bytes=64)]))
+                w1_raw.append(load_first(w1, e, [kept(whole, F32, f"w1_raw{e}")]))
+            if e == 0:
+                w3_raw.append(load_first(w3, e, [kept(whole, F32, "w3_raw0")]))
+                continue
             if e == 1:
                 w2_raw.append(load_second(0))
                 nc.sync.dma_start(dst_sb[:], dst)
-            if e == 0:
-                w3_raw.append(load_first(w3, e, [keep.tile([P, PACK, H], F32, name="w3_raw0", align_bytes=64)]))
-            else:
-                last = in_region(e, HALF_AT, [P, PACK, H // 2], F32, f"w3_raw{e}_1")
-                w3_raw.append(load_first(w3, e, [half_tile(f"w3_raw{e}_0"), last]))
-            if e > 0:
-                w2_raw.append(load_second(e))
+            second = in_region(e, W3_HALF_AT, half, F32, f"w3_raw{e}_1")
+            w3_raw.append(load_first(w3, e, [kept(half, F32, f"w3_raw{e}_0"), second]))
+            w2_raw.append(load_second(e))
 
         nc.vector.memset(warm[:], 0.0)
         nc.scalar.activation(out=warm[:], in_=warm[:], func=SILU)
@@ -119,24 +127,25 @@ def tile_moe_two_glu_silu_kernel(tc, xT, w1, w3, w2, gate, offs, dst, out):
         for window in windows:
             nc.vector.memset(window[:], 0.0)
 
-        for m0 in range(0, SLOTS_A_PARTITION, PACK):
+        for m0 in range(0, GATE_COLS, PACK):
             bank = psum_y.tile([P, PACK, P], F32, name="y_bank")
             for m in range(PACK):
                 nc.tensor.transpose(bank[:, m, :], gate_cols[:, m0 + m:m0 + m + 1].to_broadcast([P, P]), identity[:])
-            nc.scalar.copy(
-                out=gates[:].rearrange("q (p m) -> q p m", m=SLOTS_A_PARTITION)[:, :, m0:m0 + PACK],
+            nc.vector.tensor_copy(
+                out=gates[:].rearrange("q (p m) -> q p m", m=GATE_COLS)[:, :, m0:m0 + PACK],
                 in_=bank[:].rearrange("q m p -> q p m"),
             )
 
-        pairs = [keep.tile([P, PAIR, C, PAIR], BF16, name=f"pairs{e}", align_bytes=64) for e in range(E)]
+        pairs = [kept([P, PAIR, C, PAIR], BF16, f"pairs{e}") for e in range(E)]
+        slot_bf = {}
 
         def entries(list_sb, e):
             return list_sb[:, e * LIST_COLS:(e + 1) * LIST_COLS]
 
-        def gather_on_scalar(j, tiles, copies):
+        def gather_on_scalar(j, tiles):
             plane = keep.tile([P, T], BF16, name=f"x_bf{j}")
-            for tile, cols, copy in zip(tiles, halves, copies):
-                copy(out=plane[:, cols], in_=tile[:])
+            for tile, lo, hi in zip(tiles, X_CUTS[j], X_CUTS[j][1:]):
+                nc.scalar.copy(out=plane[:, lo:hi], in_=tile[:])
             for e in range(E):
                 nc.scalar.activation(out=pairs[e][:, 0, :, j], in_=plane[:].indirect(entries(offs_sb, e)), func=COPY)
 
@@ -144,69 +153,55 @@ def tile_moe_two_glu_silu_kernel(tc, xT, w1, w3, w2, gate, offs, dst, out):
             for e in range(E):
                 nc.vector.tensor_copy(out=pairs[e][:, 1, :, j - PAIR], in_=plane[:].indirect(entries(offs_sb, e)))
 
-        gather_on_vector(2, x_plane2)
-        gather_on_scalar(0, x_plane0, (nc.scalar.copy, nc.scalar.copy))
-        gather_on_scalar(1, x_plane1, (nc.vector.tensor_copy, nc.scalar.copy))
-        gather_on_vector(3, x_plane3)
-
-        slot_bf = {}
-
-        def weave(e, copy, word, tag):
-            slot_bf[e] = keep.tile([P, C, PACK], BF16, name=f"slot_bf{e}", tag=tag, align_bytes=64)
+        def weave(e, copy, word, behind=""):
+            slot_bf[e] = kept([P, C, PACK], BF16, f"slot_bf{e}", behind)
             copy(
                 out=slot_bf[e][:].rearrange("p c j -> p (c j)").bitcast(word).rearrange("p (c u) -> p c u", u=PAIR),
-                in_=pairs[e][:].rearrange("p u c j -> p (u c j)").bitcast(word).rearrange("p (u c) -> p c u", u=PAIR),
+                in_=pairs[e][:].rearrange("p u c v -> p (u c v)").bitcast(word).rearrange("p (u c) -> p c u", u=PAIR),
             )
 
-        for e, tag in ((1, "x_half0_0"), (2, "x_half0_1"), (3, "x_half1_1")):
-            weave(e, nc.scalar.copy, U32, tag)
+        gather_on_scalar(0, x_plane0)
+        gather_on_vector(2, x_plane2)
+        gather_on_scalar(1, x_plane1)
+        gather_on_vector(3, x_plane3)
+        for e, spent in zip(range(1, E), ("x_piece0_0", "x_piece0_1", "x_piece1_0")):
+            weave(e, nc.scalar.copy, U32, spent)
 
-        def quantize_slots(experts, tag):
-            words = keep.tile([P, len(experts), C], U32, name=tag, align_bytes=64)
-            scales = keep.tile([P, len(experts), C], U8, name=f"slot_scales{experts[0]}", align_bytes=64)
+        def quantize_slots(experts, behind):
+            words = kept([P, len(experts), C], U32, f"slot_codes{experts[0]}", behind)
+            scales = kept([P, len(experts), C], U8, f"slot_scales{experts[0]}")
             for n, e in enumerate(experts):
-                nc.vector.quantize_mx(
-                    out=words[:, n, :].bitcast(FP8X4),
-                    scales=scales[:, n, :],
-                    in_=slot_bf[e][:].rearrange("p c j -> p (c j)"),
-                )
+                quantize(words[:, n, :], scales[:, n, :], slot_bf[e][:].rearrange("p c j -> p (c j)"))
             return [(words[:, n, :], scales[:, n, :]) for n in range(len(experts))]
 
-        def round_first(bf, raws, copies):
+        def by_lines(bf):
+            return bf.rearrange("p t (a r) j -> p a t j r", r=PAIR)
+
+        def raw_by_lines(raw):
+            return raw[:].rearrange("p j (a t r) -> p a t j r", t=PACK, r=PAIR)
+
+        def round_columns(name, raws, copies):
+            bf = cast.tile([P, PACK, P, PACK], BF16, name=name, align_bytes=64)
             width = P // len(raws)
             for n, (raw, copy) in enumerate(zip(raws, copies)):
-                copy(
-                    out=bf[:, :, n * width:(n + 1) * width, :].rearrange("p t (a r) j -> p a t j r", r=PAIR),
-                    in_=raw[:].rearrange("p j (a t r) -> p a t j r", t=PACK, r=PAIR),
-                )
+                copy(out=by_lines(bf[:, :, n * width:(n + 1) * width, :]), in_=raw_by_lines(raw))
             return [bf]
 
-        def rounded_tile(pool, name, tag):
-            return pool.tile([P, PACK, H // PACK, PACK], BF16, name=name, tag=tag, align_bytes=64)
-
         def round_on_vector(name, raw):
-            pieces = []
-            for n in range(2):
-                bf = keep.tile([P, PAIR, H // PACK, PACK], BF16, name=f"{name}_{n}", align_bytes=64)
-                nc.vector.tensor_copy(
-                    out=bf[:].rearrange("p t (a r) j -> p a t j r", r=PAIR),
-                    in_=raw[:].rearrange("p j (a t r) -> p a t j r", t=PACK, r=PAIR)[:, :, n * PAIR:(n + 1) * PAIR],
-                )
-                pieces.append(bf)
+            pieces = [kept([P, PAIR, P, PACK], BF16, f"{name}_{n}") for n in range(2)]
+            for n, bf in enumerate(pieces):
+                nc.vector.tensor_copy(out=by_lines(bf[:]), in_=raw_by_lines(raw)[:, :, n * PAIR:(n + 1) * PAIR])
             return pieces
 
         def round_w1(e):
             if e == 0:
                 return round_on_vector("w1_bf0", w1_raw[e][0])
             if e > 1:
-                return round_first(rounded_tile(cast, "w1_bf", "w1_bf"), w1_raw[e], [nc.scalar.copy] * 2)
+                return round_columns("w1_bf", w1_raw[e], [nc.scalar.copy] * 2)
             raw = w1_raw[e][0]
-            low = keep.tile([P, PAIR, H // PACK, PACK], BF16, name="w1_low", align_bytes=64)
-            high = keep.tile([P, PAIR, H // PACK, PACK], BF16, name="w1_high", tag="x_half0_0", align_bytes=64)
-            nc.scalar.copy(
-                out=low[:].rearrange("p t (a r) j -> p a t j r", r=PAIR),
-                in_=raw[:].rearrange("p j (a t r) -> p a t j r", t=PACK, r=PAIR)[:, :, :PAIR],
-            )
+            low = kept([P, PAIR, P, PACK], BF16, "w1_low")
+            high = kept([P, PAIR, P, PACK], BF16, "w1_high", "x_piece0_0")
+            nc.scalar.copy(out=by_lines(low[:]), in_=raw_by_lines(raw)[:, :, :PAIR])
             for t in range(PAIR):
                 round_on_gpsimd(
                     nc,
@@ -218,39 +213,31 @@ def tile_moe_two_glu_silu_kernel(tc, xT, w1, w3, w2, gate, offs, dst, out):
         def round_w3(e):
             if e == 0:
                 return round_on_vector("w3_bf0", w3_raw[e][0])
-            copies = [nc.scalar.copy, nc.vector.tensor_copy] if e == 1 else [nc.scalar.copy] * 2
-            return round_first(rounded_tile(cast, "w3_bf", "w3_bf"), w3_raw[e], copies)
+            second = nc.vector.tensor_copy if e == 1 else nc.scalar.copy
+            return round_columns("w3_bf", w3_raw[e], [nc.scalar.copy, second])
 
-        def quantize_first(name, pieces, last_behind=None):
+        def quantize_first(name, pieces):
             scales = codes.tile([P, H], U8, name=f"{name}_scales", align_bytes=64)
             width = H // len(pieces)
-            quarters = []
+            by_t = []
             for n, bf in enumerate(pieces):
-                if n > 0 and last_behind:
-                    words = keep.tile([P, width], U32, name="w1_high_codes", tag=last_behind, align_bytes=64)
-                else:
-                    words = codes.tile([P, width], U32, name=f"{name}_codes", align_bytes=64)
-                nc.vector.quantize_mx(
-                    out=words[:].bitcast(FP8X4),
-                    scales=scales[:, n * width:(n + 1) * width],
-                    in_=bf[:].rearrange("p t m j -> p (t m j)"),
-                )
-                quarters.extend(words[:, c:c + P] for c in range(0, width, P))
-            return quarters, scales
+                words = codes.tile([P, width], U32, name=f"{name}_codes", align_bytes=64)
+                quantize(words[:], scales[:, n * width:(n + 1) * width], bf[:].rearrange("p t m j -> p (t m j)"))
+                by_t.extend(words[:, c:c + P] for c in range(0, width, P))
+            return by_t, scales
 
         def first_product(name, matrix, slots):
-            quarters, scales = matrix
+            by_t, scales = matrix
             slot_words, slot_scales = slots
             banks = []
-            for s in range(C // HALF):
-                cols = slice(s * HALF, (s + 1) * HALF)
-                bank = psum.tile([P, PACK, HALF], F32, name=f"{name}_bank")
+            for s in range(C // BANK_SLOTS):
+                cols = slice(s * BANK_SLOTS, (s + 1) * BANK_SLOTS)
+                bank = psum.tile([P, PACK, BANK_SLOTS], F32, name=f"{name}_bank")
                 for t in range(PACK):
-                    w_cols = slice(t * P, (t + 1) * P)
                     nc.tensor.matmul_mx(
                         out=bank[:, t, :],
-                        lhsT=quarters[t].bitcast(FP8X4),
-                        lhsT_scale=scales[:, w_cols],
+                        lhsT=by_t[t].bitcast(FP8X4),
+                        lhsT_scale=scales[:, t * P:(t + 1) * P],
                         rhs=slot_words[:, cols].bitcast(FP8X4),
                         rhs_scale=slot_scales[:, cols],
                         start=True,
@@ -260,7 +247,7 @@ def tile_moe_two_glu_silu_kernel(tc, xT, w1, w3, w2, gate, offs, dst, out):
             return banks
 
         def activate(e, w1_banks):
-            acts = [in_region(e, at, [P, HALF, PACK], F32, f"act{e}_{s}") for s, at in enumerate(ACT_AT)]
+            acts = [in_region(e, at, [P, BANK_SLOTS, PACK], F32, f"act{e}_{s}") for s, at in enumerate(ACT_AT)]
             for bank, act in zip(w1_banks, acts):
                 nc.scalar.activation(out=act[:], in_=bank[:].rearrange("p t c -> p c t"), func=SILU)
             return acts
@@ -268,47 +255,41 @@ def tile_moe_two_glu_silu_kernel(tc, xT, w1, w3, w2, gate, offs, dst, out):
         def second_product(e, acts, w3_banks):
             h_bf = cast.tile([P, C, PACK], BF16, name="h_bf", align_bytes=64)
             h_scales = codes.tile([P, C], U8, name="h_scales", align_bytes=64)
-            scales = codes.tile([P, N], U8, name="w2_scales", align_bytes=64)
-
-            def quantize(words, scales, bf):
-                nc.vector.quantize_mx(
-                    out=words[:].bitcast(FP8X4), scales=scales[:], in_=bf[:].rearrange("p c t -> p (c t)")
-                )
-
-            if 0 < e < E - 1:
-                bf = in_region(e, SECOND_AT, [P, N, PACK], BF16, f"w2_bf{e}")
-                round_on_gpsimd(nc, bf[:], w2_raw[e][:].rearrange("p t c -> p c t"))
+            w2_scales = codes.tile([P, N], U8, name="w2_scales", align_bytes=64)
+            if 0 < e < LAST:
+                w2_bf = in_region(e, W2_BF_AT, [P, N, PACK], BF16, f"w2_bf{e}")
+                round_on_gpsimd(nc, w2_bf[:], w2_raw[e][:].rearrange("p t c -> p c t"))
             else:
-                bf = keep.tile([P, N, PACK], BF16, name=f"w2_bf{e}", align_bytes=64)
+                w2_bf = kept([P, N, PACK], BF16, f"w2_bf{e}")
                 nc.scalar.copy(
-                    out=bf[:].rearrange("p (c r) t -> p c t r", r=PAIR),
+                    out=w2_bf[:].rearrange("p (c r) t -> p c t r", r=PAIR),
                     in_=w2_raw[e][:].rearrange("p t (c r) -> p c t r", r=PAIR),
                 )
             for s, bank in enumerate(w3_banks):
                 nc.vector.tensor_tensor(
-                    out=h_bf[:, s * HALF:(s + 1) * HALF, :],
+                    out=h_bf[:, s * BANK_SLOTS:(s + 1) * BANK_SLOTS, :],
                     in0=acts[s][:],
                     in1=bank[:].rearrange("p t c -> p c t"),
                     op=MULT,
                 )
-            if e == E - 1:
-                words = codes.tile([P, N], U32, name="w2_codes", align_bytes=64)
-                quantize(words, scales, bf)
-                h_words = keep.tile([P, C], U32, name="last_h_codes", tag=f"w2_raw{e}", align_bytes=64)
-                quantize(h_words, h_scales, h_bf)
+            w2_values, h_values = w2_bf[:].rearrange("p c t -> p (c t)"), h_bf[:].rearrange("p c t -> p (c t)")
+            if e == LAST:
+                w2_words = codes.tile([P, N], U32, name="w2_codes", align_bytes=64)
+                quantize(w2_words[:], w2_scales[:], w2_values)
+                h_words = kept([P, C], U32, "last_h_codes", f"w2_raw{e}")
+                quantize(h_words[:], h_scales[:], h_values)
             else:
                 h_words = codes.tile([P, C], U32, name="h_codes", align_bytes=64)
-                quantize(h_words, h_scales, h_bf)
-                words = in_region(e, ACT_AT[1], [P, N], U32, f"w2_codes{e}")
-                quantize(words, scales, bf)
+                quantize(h_words[:], h_scales[:], h_values)
+                w2_words = in_region(e, W2_CODES_AT, [P, N], U32, f"w2_codes{e}")
+                quantize(w2_words[:], w2_scales[:], w2_values)
             banks = []
             for b in range(N // P):
                 bank = psum_y.tile([P, C], F32, name="y_bank")
-                w_cols = slice(b * P, (b + 1) * P)
                 nc.tensor.matmul_mx(
                     out=bank[:],
-                    lhsT=words[:, w_cols].bitcast(FP8X4),
-                    lhsT_scale=scales[:, w_cols],
+                    lhsT=w2_words[:, b * P:(b + 1) * P].bitcast(FP8X4),
+                    lhsT_scale=w2_scales[:, b * P:(b + 1) * P],
                     rhs=h_words[:].bitcast(FP8X4),
                     rhs_scale=h_scales[:],
                     start=True,
@@ -319,31 +300,33 @@ def tile_moe_two_glu_silu_kernel(tc, xT, w1, w3, w2, gate, offs, dst, out):
 
         def scatter(e, b, y):
             nc.scalar.copy(out=y, in_=y_banks[e][b][:])
-            nc.vector.tensor_tensor(out=windows[b][:].indirect(entries(dst_sb, e)), in0=y, in1=gates[:, e * C:(e + 1) * C], op=MULT)
+            nc.vector.tensor_tensor(
+                out=windows[b][:].indirect(entries(dst_sb, e)), in0=y, in1=gates[:, e * C:(e + 1) * C], op=MULT
+            )
 
         last_y = keep.tile([P, N // P, C], F32, name="last_y")
-        rounded = round_w1(0)
-        weave(0, nc.vector.tensor_copy, I32, "w1_raw0")
-        matrix = quantize_first("w1", rounded)
+        weave(0, nc.vector.tensor_copy, I32)
+        matrix = quantize_first("w1", round_w1(0))
         slots = quantize_slots([0], "w1_bf0_0")
         w1_banks = first_product("w1", matrix, slots[0])
         w3_banks = first_product("w3", quantize_first("w3", round_w3(0)), slots[0])
-        slots.extend(quantize_slots([1, 2], "w3_bf0_0"))
+        slots.extend(quantize_slots(list(range(1, LAST)), "w3_bf0_0"))
 
         y_banks = []
-        for e in range(E):
+        for e in range(LAST):
             acts = activate(e, w1_banks)
             y_banks.append(second_product(e, acts, w3_banks))
-            if e + 1 < E:
-                w1_bf, w3_bf = round_w1(e + 1), round_w3(e + 1)
-                w1_banks = first_product("w1", quantize_first("w1", w1_bf), slots[e + 1])
-                if e == 0:
-                    slots.extend(quantize_slots([E - 1], "w3_raw1_0"))
-                w3_banks = first_product("w3", quantize_first("w3", w3_bf), slots[e + 1])
-                for b in range(N // P if e + 2 < E else 1):
-                    scatter(e, b, in_region(e + 1, Y_AT[b], [P, C], F32, f"y{e}_{b}")[:])
+            w1_bf, w3_bf = round_w1(e + 1), round_w3(e + 1)
+            w1_banks = first_product("w1", quantize_first("w1", w1_bf), slots[e + 1])
+            if e == 0:
+                slots.extend(quantize_slots([LAST], "w3_raw1_0"))
+            w3_banks = first_product("w3", quantize_first("w3", w3_bf), slots[e + 1])
+            for b in range(N // P if e + 1 < LAST else 1):
+                scatter(e, b, in_region(e + 1, Y_AT[b], [P, C], F32, f"y{e}_{b}")[:])
 
-        scatter(E - 2, 1, acts[0][:].rearrange("p c t -> p (c t)")[:, :C])
+        acts = activate(LAST, w1_banks)
+        y_banks.append(second_product(LAST, acts, w3_banks))
+        scatter(LAST - 1, 1, acts[0][:].rearrange("p c t -> p (c t)")[:, :C])
         for b, queue in enumerate((nc.sync, nc.scalar)):
-            scatter(E - 1, b, last_y[:, b, :])
+            scatter(LAST, b, last_y[:, b, :])
             queue.dma_start(out=out[b * P:(b + 1) * P, :], in_=windows[b][:])

@@ -9,7 +9,6 @@ FLOPS = 2 * E * C * (2 * K * H + H * N)
 F32 = mybir.dt.float32
 BF16 = mybir.dt.bfloat16
 U32 = mybir.dt.uint32
-I32 = mybir.dt.int32
 U16 = mybir.dt.uint16
 U8 = mybir.dt.uint8
 FP8X4 = mybir.dt.float8_e4m3fn_x4
@@ -20,33 +19,20 @@ ADD = mybir.AluOpType.add
 
 P = 128
 PACK = 4
-PAIR = 2
+HALF = 2
 BANK_SLOTS = 128
 GATE_COLS = E * C // P
 LIST_COLS = C // 16
+BLOCKS = N // P
 LAST = E - 1
-
 KIB = 1024
-W3_HALF_AT = 7 * KIB // 2
-ACT_AT = (2 * KIB, 4 * KIB)
-Y_AT = (7 * KIB, 6 * KIB)
-W2_BF_AT = Y_AT[0]
-W2_CODES_AT = ACT_AT[1]
-REGION = 9 * KIB
-
-X_CUTS = {0: (0, T // 2, T), 1: (0, T // 2, 3 * T // 4, T)}
-
-
-def round_on_gpsimd(nc, out, in_):
-    nc.gpsimd.tensor_scalar(out=out, in0=in_, scalar1=1.0, scalar2=0.0, op0=MULT, op1=ADD)
+REGION = 4 * KIB
 
 
 def tile_moe_two_glu_silu_kernel(tc, xT, w1, w3, w2, gate, offs, dst, out):
     nc = tc.nc
     with ExitStack() as ctx:
         keep = ctx.enter_context(tc.tile_pool(name="keep", bufs=1))
-        cast = ctx.enter_context(tc.tile_pool(name="cast", bufs=2))
-        codes = ctx.enter_context(tc.tile_pool(name="codes", bufs=3))
         placed = ctx.enter_context(tc.tile_pool(name="placed", bufs=1))
         psum = ctx.enter_context(tc.psum_pool(name="psum", bufs=2))
         psum_y = ctx.enter_context(tc.psum_pool(name="psum_y", bufs=4))
@@ -62,71 +48,37 @@ def tile_moe_two_glu_silu_kernel(tc, xT, w1, w3, w2, gate, offs, dst, out):
 
         offs_sb = keep.tile([P, E * LIST_COLS], U16, name="offs_sb")
         dst_sb = keep.tile([P, E * LIST_COLS], U16, name="dst_sb")
-        warm = keep.tile([P, 1], F32, name="warm")
-        windows = [keep.tile([P, T], F32, name=f"window{b}") for b in range(N // P)]
+        windows = [keep.tile([P, T], F32, name=f"window{b}") for b in range(BLOCKS)]
         gates = keep.tile([P, E * C], F32, name="gates")
         gate_cols = keep.tile([P, GATE_COLS], F32, name="gate_cols")
         identity = keep.tile([P, P], F32, name="identity")
 
         nc.scalar.dma_start(out=gate_cols[:], in_=gate[0].rearrange("(p m) -> p m", m=GATE_COLS))
-
         x_rows = xT.rearrange("(p j) t -> p j t", j=PACK)
+        x_planes = []
+        for j in range(PACK):
+            plane = keep.tile([P, T], F32, name=f"x_plane{j}")
+            nc.sync.dma_start(out=plane[:], in_=x_rows[:, j, :])
+            x_planes.append(plane)
+            if j == 0:
+                nc.sync.dma_start(offs_sb[:], offs)
 
-        def load_piece(j, n):
-            lo, hi = X_CUTS[j][n:n + 2]
-            tile = kept([P, hi - lo], F32, f"x_piece{j}_{n}")
-            nc.sync.dma_start(out=tile[:], in_=x_rows[:, j, lo:hi])
-            return tile
-
-        def load_plane(j):
-            tile = keep.tile([P, T], F32, name=f"x_plane{j}")
-            nc.sync.dma_start(out=tile[:], in_=x_rows[:, j, :])
-            return tile
-
-        x_plane0 = [load_piece(0, 0), load_piece(0, 1)]
-        nc.sync.dma_start(offs_sb[:], offs)
-        x_plane2 = load_plane(2)
-        x_plane1 = [load_piece(1, 0)]
-        x_plane3 = load_plane(3)
-        x_plane1.extend([load_piece(1, 1), load_piece(1, 2)])
-
-        def load_first(w, e, tiles):
-            width = H // len(tiles)
-            for n, tile in enumerate(tiles):
-                rows = w[e].rearrange("(p j) n -> p j n", j=PACK)
-                nc.sync.dma_start(out=tile[:], in_=rows[:, :, n * width:(n + 1) * width])
-            return tiles
-
-        def load_second(e):
-            raw = kept([P, PACK, N], F32, f"w2_raw{e}")
-            rows = w2[e].rearrange("(a t r) n -> r a t n", t=PACK, r=PAIR)
-            for r in range(PAIR):
-                nc.sync.dma_start(out=raw[r:P:PAIR, :, :], in_=rows[r])
+        def load(w, e, name):
+            raw = kept([P, PACK, w.shape[2]], F32, f"{name}_raw{e}")
+            nc.sync.dma_start(out=raw[:], in_=w[e].rearrange("(p j) n -> p j n", j=PACK))
             return raw
 
-        whole, half = [P, PACK, H], [P, PACK, H // 2]
         w1_raw, w3_raw, w2_raw = [], [], []
         for e in range(E):
-            if e == 2:
-                w1_raw.append(load_first(w1, e, [kept(half, F32, f"w1_raw{e}_{h}") for h in range(2)]))
-            else:
-                w1_raw.append(load_first(w1, e, [kept(whole, F32, f"w1_raw{e}")]))
-            if e == 0:
-                w3_raw.append(load_first(w3, e, [kept(whole, F32, "w3_raw0")]))
-                continue
+            w1_raw.append(load(w1, e, "w1"))
             if e == 1:
-                w2_raw.append(load_second(0))
                 nc.sync.dma_start(dst_sb[:], dst)
-            second = in_region(e, W3_HALF_AT, half, F32, f"w3_raw{e}_1")
-            w3_raw.append(load_first(w3, e, [kept(half, F32, f"w3_raw{e}_0"), second]))
-            w2_raw.append(load_second(e))
+            w3_raw.append(load(w3, e, "w3"))
+            w2_raw.append(load(w2, e, "w2"))
 
-        nc.vector.memset(warm[:], 0.0)
-        nc.scalar.activation(out=warm[:], in_=warm[:], func=SILU)
         make_identity(nc, identity[:])
         for window in windows:
             nc.vector.memset(window[:], 0.0)
-
         for m0 in range(0, GATE_COLS, PACK):
             bank = psum_y.tile([P, PACK, P], F32, name="y_bank")
             for m in range(PACK):
@@ -136,108 +88,53 @@ def tile_moe_two_glu_silu_kernel(tc, xT, w1, w3, w2, gate, offs, dst, out):
                 in_=bank[:].rearrange("q m p -> q p m"),
             )
 
-        pairs = [kept([P, PAIR, C, PAIR], BF16, f"pairs{e}") for e in range(E)]
-        slot_bf = {}
+        def entries(list_sb, first, count=1):
+            return list_sb[:, first * LIST_COLS:(first + count) * LIST_COLS]
 
-        def entries(list_sb, e):
-            return list_sb[:, e * LIST_COLS:(e + 1) * LIST_COLS]
-
-        def gather_on_scalar(j, tiles):
-            plane = keep.tile([P, T], BF16, name=f"x_bf{j}")
-            for tile, lo, hi in zip(tiles, X_CUTS[j], X_CUTS[j][1:]):
-                nc.scalar.copy(out=plane[:, lo:hi], in_=tile[:])
-            for e in range(E):
-                nc.scalar.activation(out=pairs[e][:, 0, :, j], in_=plane[:].indirect(entries(offs_sb, e)), func=COPY)
-
-        def gather_on_vector(j, plane):
-            for e in range(E):
-                nc.vector.tensor_copy(out=pairs[e][:, 1, :, j - PAIR], in_=plane[:].indirect(entries(offs_sb, e)))
-
-        def weave(e, copy, word, behind=""):
-            slot_bf[e] = kept([P, C, PACK], BF16, f"slot_bf{e}", behind)
-            copy(
-                out=slot_bf[e][:].rearrange("p c j -> p (c j)").bitcast(word).rearrange("p (c u) -> p c u", u=PAIR),
-                in_=pairs[e][:].rearrange("p u c v -> p (u c v)").bitcast(word).rearrange("p (u c) -> p c u", u=PAIR),
+        rows = [kept([P, PACK, HALF * C], BF16, f"rows{n}") for n in range(2)]
+        for j in range(PACK):
+            nc.vector.tensor_copy(out=rows[0][:, j, :], in_=x_planes[j][:].indirect(entries(offs_sb, 0, HALF)))
+            nc.scalar.activation(
+                out=rows[1][:, j, :], in_=x_planes[j][:].indirect(entries(offs_sb, HALF, HALF)), func=COPY
             )
 
-        gather_on_scalar(0, x_plane0)
-        gather_on_vector(2, x_plane2)
-        gather_on_scalar(1, x_plane1)
-        gather_on_vector(3, x_plane3)
-        for e, spent in zip(range(1, E), ("x_piece0_0", "x_piece0_1", "x_piece1_0")):
-            weave(e, nc.scalar.copy, U32, spent)
+        def interleave(copy, side_by_side, planes):
+            copy(
+                out=side_by_side.rearrange("p (c i) j -> p c j i", i=PACK),
+                in_=planes.rearrange("p j (c i) -> p c j i", i=PACK),
+            )
 
-        def quantize_slots(experts, behind):
-            words = kept([P, len(experts), C], U32, f"slot_codes{experts[0]}", behind)
-            scales = kept([P, len(experts), C], U8, f"slot_scales{experts[0]}")
-            for n, e in enumerate(experts):
-                quantize(words[:, n, :], scales[:, n, :], slot_bf[e][:].rearrange("p c j -> p (c j)"))
-            return [(words[:, n, :], scales[:, n, :]) for n in range(len(experts))]
+        slot_bf = [kept([P, C, PACK], BF16, f"slot_bf{e}") for e in range(HALF)]
+        late_bf = kept([P, HALF * C, PACK], BF16, "late_bf")
 
-        def by_lines(bf):
-            return bf.rearrange("p t (a r) j -> p a t j r", r=PAIR)
+        def quantize_slots(values, words, name):
+            scales = kept([P, words.shape[1]], U8, name)
+            quantize(words[:], scales[:], values[:].rearrange("p c j -> p (c j)"))
+            return [(words[:, c:c + C], scales[:, c:c + C]) for c in range(0, words.shape[1], C)]
 
-        def raw_by_lines(raw):
-            return raw[:].rearrange("p j (a t r) -> p a t j r", t=PACK, r=PAIR)
+        def round_half(copy, bf, raw, h):
+            copy(
+                out=bf[:].rearrange("p t m j -> p m j t"),
+                in_=raw[:].rearrange("p j (m t) -> p m j t", t=PACK)[:, :, :, h * HALF:(h + 1) * HALF],
+            )
 
-        def round_columns(name, raws, copies):
-            bf = cast.tile([P, PACK, P, PACK], BF16, name=name, align_bytes=64)
-            width = P // len(raws)
-            for n, (raw, copy) in enumerate(zip(raws, copies)):
-                copy(out=by_lines(bf[:, :, n * width:(n + 1) * width, :]), in_=raw_by_lines(raw))
-            return [bf]
+        def quantize_half(name, bf):
+            words = kept([P, HALF * P], U32, f"{name}_codes")
+            scales = kept([P, HALF * P], U8, f"{name}_scales")
+            quantize(words[:], scales[:], bf[:].rearrange("p t m j -> p (t m j)"))
+            return [(words[:, c:c + P], scales[:, c:c + P]) for c in range(0, HALF * P, P)]
 
-        def round_on_vector(name, raw):
-            pieces = [kept([P, PAIR, P, PACK], BF16, f"{name}_{n}") for n in range(2)]
-            for n, bf in enumerate(pieces):
-                nc.vector.tensor_copy(out=by_lines(bf[:]), in_=raw_by_lines(raw)[:, :, n * PAIR:(n + 1) * PAIR])
-            return pieces
-
-        def round_w1(e):
-            if e == 0:
-                return round_on_vector("w1_bf0", w1_raw[e][0])
-            if e > 1:
-                return round_columns("w1_bf", w1_raw[e], [nc.scalar.copy] * 2)
-            raw = w1_raw[e][0]
-            low = kept([P, PAIR, P, PACK], BF16, "w1_low")
-            high = kept([P, PAIR, P, PACK], BF16, "w1_high", "x_piece0_0")
-            nc.scalar.copy(out=by_lines(low[:]), in_=raw_by_lines(raw)[:, :, :PAIR])
-            for t in range(PAIR):
-                round_on_gpsimd(
-                    nc,
-                    high[:, t].rearrange("p (a r) j -> p a r j", r=PAIR),
-                    raw[:].rearrange("p j (a t r) -> p t a r j", t=PACK, r=PAIR)[:, PAIR + t],
-                )
-            return [low, high]
-
-        def round_w3(e):
-            if e == 0:
-                return round_on_vector("w3_bf0", w3_raw[e][0])
-            second = nc.vector.tensor_copy if e == 1 else nc.scalar.copy
-            return round_columns("w3_bf", w3_raw[e], [nc.scalar.copy, second])
-
-        def quantize_first(name, pieces):
-            scales = codes.tile([P, H], U8, name=f"{name}_scales", align_bytes=64)
-            width = H // len(pieces)
-            by_t = []
-            for n, bf in enumerate(pieces):
-                words = codes.tile([P, width], U32, name=f"{name}_codes", align_bytes=64)
-                quantize(words[:], scales[:, n * width:(n + 1) * width], bf[:].rearrange("p t m j -> p (t m j)"))
-                by_t.extend(words[:, c:c + P] for c in range(0, width, P))
-            return by_t, scales
-
-        def first_product(name, matrix, slots):
-            by_t, scales = matrix
+        def first_product(name, by_t, slots):
             slot_words, slot_scales = slots
             banks = []
             for s in range(C // BANK_SLOTS):
                 cols = slice(s * BANK_SLOTS, (s + 1) * BANK_SLOTS)
                 bank = psum.tile([P, PACK, BANK_SLOTS], F32, name=f"{name}_bank")
-                for t in range(PACK):
+                for t, (words, scales) in enumerate(by_t):
                     nc.tensor.matmul_mx(
                         out=bank[:, t, :],
-                        lhsT=by_t[t].bitcast(FP8X4),
-                        lhsT_scale=scales[:, t * P:(t + 1) * P],
+                        lhsT=words.bitcast(FP8X4),
+                        lhsT_scale=scales,
                         rhs=slot_words[:, cols].bitcast(FP8X4),
                         rhs_scale=slot_scales[:, cols],
                         start=True,
@@ -246,45 +143,62 @@ def tile_moe_two_glu_silu_kernel(tc, xT, w1, w3, w2, gate, offs, dst, out):
                 banks.append(bank)
             return banks
 
-        def activate(e, w1_banks):
-            acts = [in_region(e, at, [P, BANK_SLOTS, PACK], F32, f"act{e}_{s}") for s, at in enumerate(ACT_AT)]
-            for bank, act in zip(w1_banks, acts):
-                nc.scalar.activation(out=act[:], in_=bank[:].rearrange("p t c -> p c t"), func=SILU)
-            return acts
+        def times_gate(e, b, bank, y):
+            nc.vector.tensor_tensor(out=y[:], in0=bank[:], in1=gates[:, e * C:(e + 1) * C], op=MULT)
 
-        def second_product(e, acts, w3_banks):
-            h_bf = cast.tile([P, C, PACK], BF16, name="h_bf", align_bytes=64)
-            h_scales = codes.tile([P, C], U8, name="h_scales", align_bytes=64)
-            w2_scales = codes.tile([P, N], U8, name="w2_scales", align_bytes=64)
-            if 0 < e < LAST:
-                w2_bf = in_region(e, W2_BF_AT, [P, N, PACK], BF16, f"w2_bf{e}")
-                round_on_gpsimd(nc, w2_bf[:], w2_raw[e][:].rearrange("p t c -> p c t"))
-            else:
-                w2_bf = kept([P, N, PACK], BF16, f"w2_bf{e}")
-                nc.scalar.copy(
-                    out=w2_bf[:].rearrange("p (c r) t -> p c t r", r=PAIR),
-                    in_=w2_raw[e][:].rearrange("p t (c r) -> p c t r", r=PAIR),
+        def scatter_on_scalar(e, b, y):
+            nc.scalar.activation(out=windows[b][:].indirect(entries(dst_sb, e)), in_=y[:], func=COPY)
+
+        interleave(nc.vector.tensor_copy, slot_bf[0][:], rows[0][:, :, :C])
+        interleave(nc.scalar.copy, slot_bf[1][:], rows[0][:, :, C:])
+        for n in range(HALF):
+            interleave(nc.scalar.copy, late_bf[:, n * C:(n + 1) * C, :], rows[1][:, :, n * C:(n + 1) * C])
+        slots = quantize_slots(slot_bf[0], kept([P, C], U32, "slot_codes0"), "slot_scales0")
+
+        half = [P, HALF, P, PACK]
+        y_banks = []
+        for e in range(E):
+            w1_bf = [kept(half, BF16, f"w1_bf{e}_{h}") for h in range(2)]
+            w3_bf = [in_region(e, h * 2 * KIB, half, BF16, f"w3_bf{e}_{h}") for h in range(2)]
+            for h in range(2):
+                round_half(nc.vector.tensor_copy, w1_bf[h], w1_raw[e], h)
+            w1_low = quantize_half(f"w1_{e}_0", w1_bf[0])
+            round_half(nc.scalar.copy, w3_bf[1], w3_raw[e], 1)
+            round_half(nc.vector.tensor_copy, w3_bf[0], w3_raw[e], 0)
+            w1_banks = first_product("w1", w1_low + quantize_half(f"w1_{e}_1", w1_bf[1]), slots[e])
+            if e == 0:
+                slots.extend(quantize_slots(slot_bf[1], kept([P, C], U32, "slot_codes1"), "slot_scales1"))
+            w3_low = quantize_half(f"w3_{e}_0", w3_bf[0])
+            w3_banks = first_product("w3", w3_low + quantize_half(f"w3_{e}_1", w3_bf[1]), slots[e])
+            acts = kept([P, C, PACK], F32, f"acts{e}", f"w3_raw{e}")
+            for s, bank in enumerate(w1_banks):
+                nc.scalar.activation(
+                    out=acts[:, s * BANK_SLOTS:(s + 1) * BANK_SLOTS, :], in_=bank[:].rearrange("p t c -> p c t"), func=SILU
                 )
+            if e == 0:
+                slots.extend(quantize_slots(late_bf, in_region(e, 0, [P, HALF * C], U32, "late_codes"), "late_scales"))
+                w2_bf = kept([P, N, PACK], BF16, "w2_bf0", "late_bf")
+            else:
+                for b in range(BLOCKS):
+                    y = in_region(e, b * KIB, [P, C], F32, f"y{e - 1}_{b}")
+                    times_gate(e - 1, b, y_banks[b], y)
+                    scatter_on_scalar(e - 1, b, y)
+                w2_bf = in_region(e, 2 * KIB, [P, N, PACK], BF16, f"w2_bf{e}")
+            nc.gpsimd.tensor_scalar(
+                out=w2_bf[:], in0=w2_raw[e][:].rearrange("p t c -> p c t"), scalar1=1.0, scalar2=0.0, op0=MULT, op1=ADD
+            )
+            h_bf = kept([P, C, PACK], BF16, f"h_bf{e}")
             for s, bank in enumerate(w3_banks):
+                cols = slice(s * BANK_SLOTS, (s + 1) * BANK_SLOTS)
                 nc.vector.tensor_tensor(
-                    out=h_bf[:, s * BANK_SLOTS:(s + 1) * BANK_SLOTS, :],
-                    in0=acts[s][:],
-                    in1=bank[:].rearrange("p t c -> p c t"),
-                    op=MULT,
+                    out=h_bf[:, cols, :], in0=acts[:, cols, :], in1=bank[:].rearrange("p t c -> p c t"), op=MULT
                 )
-            w2_values, h_values = w2_bf[:].rearrange("p c t -> p (c t)"), h_bf[:].rearrange("p c t -> p (c t)")
-            if e == LAST:
-                w2_words = codes.tile([P, N], U32, name="w2_codes", align_bytes=64)
-                quantize(w2_words[:], w2_scales[:], w2_values)
-                h_words = kept([P, C], U32, "last_h_codes", f"w2_raw{e}")
-                quantize(h_words[:], h_scales[:], h_values)
-            else:
-                h_words = codes.tile([P, C], U32, name="h_codes", align_bytes=64)
-                quantize(h_words[:], h_scales[:], h_values)
-                w2_words = in_region(e, W2_CODES_AT, [P, N], U32, f"w2_codes{e}")
-                quantize(w2_words[:], w2_scales[:], w2_values)
-            banks = []
-            for b in range(N // P):
+            w2_words, w2_scales = kept([P, N], U32, f"w2_codes{e}"), kept([P, N], U8, f"w2_scales{e}")
+            h_words, h_scales = kept([P, C], U32, f"h_codes{e}"), kept([P, C], U8, f"h_scales{e}")
+            quantize(w2_words[:], w2_scales[:], w2_bf[:].rearrange("p c t -> p (c t)"))
+            quantize(h_words[:], h_scales[:], h_bf[:].rearrange("p c t -> p (c t)"))
+            y_banks = []
+            for b in range(BLOCKS):
                 bank = psum_y.tile([P, C], F32, name="y_bank")
                 nc.tensor.matmul_mx(
                     out=bank[:],
@@ -295,38 +209,12 @@ def tile_moe_two_glu_silu_kernel(tc, xT, w1, w3, w2, gate, offs, dst, out):
                     start=True,
                     stop=True,
                 )
-                banks.append(bank)
-            return banks
+                y_banks.append(bank)
 
-        def scatter(e, b, y):
-            nc.scalar.copy(out=y, in_=y_banks[e][b][:])
-            nc.vector.tensor_tensor(
-                out=windows[b][:].indirect(entries(dst_sb, e)), in0=y, in1=gates[:, e * C:(e + 1) * C], op=MULT
-            )
-
-        last_y = keep.tile([P, N // P, C], F32, name="last_y")
-        weave(0, nc.vector.tensor_copy, I32)
-        matrix = quantize_first("w1", round_w1(0))
-        slots = quantize_slots([0], "w1_bf0_0")
-        w1_banks = first_product("w1", matrix, slots[0])
-        w3_banks = first_product("w3", quantize_first("w3", round_w3(0)), slots[0])
-        slots.extend(quantize_slots(list(range(1, LAST)), "w3_bf0_0"))
-
-        y_banks = []
-        for e in range(LAST):
-            acts = activate(e, w1_banks)
-            y_banks.append(second_product(e, acts, w3_banks))
-            w1_bf, w3_bf = round_w1(e + 1), round_w3(e + 1)
-            w1_banks = first_product("w1", quantize_first("w1", w1_bf), slots[e + 1])
-            if e == 0:
-                slots.extend(quantize_slots([LAST], "w3_raw1_0"))
-            w3_banks = first_product("w3", quantize_first("w3", w3_bf), slots[e + 1])
-            for b in range(N // P if e + 1 < LAST else 1):
-                scatter(e, b, in_region(e + 1, Y_AT[b], [P, C], F32, f"y{e}_{b}")[:])
-
-        acts = activate(LAST, w1_banks)
-        y_banks.append(second_product(LAST, acts, w3_banks))
-        scatter(LAST - 1, 1, acts[0][:].rearrange("p c t -> p (c t)")[:, :C])
-        for b, queue in enumerate((nc.sync, nc.scalar)):
-            scatter(LAST, b, last_y[:, b, :])
-            queue.dma_start(out=out[b * P:(b + 1) * P, :], in_=windows[b][:])
+        last_y = [kept([P, C], F32, f"last_y{b}") for b in range(BLOCKS)]
+        for b in range(BLOCKS):
+            times_gate(LAST, b, y_banks[b], last_y[b])
+        nc.vector.tensor_copy(out=windows[0][:].indirect(entries(dst_sb, LAST)), in_=last_y[0][:])
+        nc.sync.dma_start(out=out[:P, :], in_=windows[0][:])
+        scatter_on_scalar(LAST, 1, last_y[1])
+        nc.scalar.dma_start(out=out[P:, :], in_=windows[1][:])

@@ -76,6 +76,9 @@ def tile_moe_two_glu_silu_kernel(tc, xT, w1, w3, w2, gate, offs, dst, out):
             w3_raw.append(load(w3, e, "w3"))
             w2_raw.append(load(w2, e, "w2"))
 
+        warm = keep.tile([P, 1], F32, name="warm")
+        nc.vector.memset(warm[:], 0.0)
+        nc.scalar.activation(out=warm[:], in_=warm[:], func=SILU)
         make_identity(nc, identity[:])
         for window in windows:
             nc.vector.memset(window[:], 0.0)

@@ -68,17 +68,21 @@ def tile_moe_two_glu_silu_kernel(tc, xT, w1, w3, w2, gate, offs, dst, out):
             nc.sync.dma_start(out=raw[:], in_=w[e].rearrange("(p j) n -> p j n", j=PACK))
             return raw
 
+        def load_second(e):
+            raw = kept([P, PACK, N], F32, f"w2_raw{e}")
+            rows = w2[e].rearrange("(a h r t) n -> r a h (t n)", h=HALF, r=HALF, t=HALF)
+            for r in range(HALF):
+                nc.sync.dma_start(out=raw[r:P:HALF].rearrange("p (h t) n -> p h (t n)", h=HALF), in_=rows[r])
+            return raw
+
         w1_raw, w3_raw, w2_raw = [], [], []
         for e in range(E):
             w1_raw.append(load(w1, e, "w1"))
             if e == 1:
                 nc.sync.dma_start(dst_sb[:], dst)
             w3_raw.append(load(w3, e, "w3"))
-            w2_raw.append(load(w2, e, "w2"))
+            w2_raw.append(load_second(e))
 
-        warm = keep.tile([P, 1], F32, name="warm")
-        nc.vector.memset(warm[:], 0.0)
-        nc.scalar.activation(out=warm[:], in_=warm[:], func=SILU)
         make_identity(nc, identity[:])
         for window in windows:
             nc.vector.memset(window[:], 0.0)
@@ -94,12 +98,12 @@ def tile_moe_two_glu_silu_kernel(tc, xT, w1, w3, w2, gate, offs, dst, out):
         def entries(list_sb, first, count=1):
             return list_sb[:, first * LIST_COLS:(first + count) * LIST_COLS]
 
-        rows = [kept([P, PACK, HALF * C], BF16, f"rows{n}") for n in range(2)]
+        slot_bf = [kept([P, C, PACK], BF16, f"slot_bf{e}") for e in range(HALF)]
+        rows = kept([P, PACK, HALF * C], BF16, "rows")
         for j in range(PACK):
-            nc.vector.tensor_copy(out=rows[0][:, j, :], in_=x_planes[j][:].indirect(entries(offs_sb, 0, HALF)))
-            nc.scalar.activation(
-                out=rows[1][:, j, :], in_=x_planes[j][:].indirect(entries(offs_sb, HALF, HALF)), func=COPY
-            )
+            for e in range(HALF):
+                nc.vector.tensor_copy(out=slot_bf[e][:, :, j], in_=x_planes[j][:].indirect(entries(offs_sb, e)))
+            nc.scalar.activation(out=rows[:, j, :], in_=x_planes[j][:].indirect(entries(offs_sb, HALF, HALF)), func=COPY)
 
         def interleave(copy, side_by_side, planes):
             copy(
@@ -107,7 +111,6 @@ def tile_moe_two_glu_silu_kernel(tc, xT, w1, w3, w2, gate, offs, dst, out):
                 in_=planes.rearrange("p j (c i) -> p c j i", i=PACK),
             )
 
-        slot_bf = [kept([P, C, PACK], BF16, f"slot_bf{e}") for e in range(HALF)]
         late_bf = kept([P, HALF * C, PACK], BF16, "late_bf")
 
         def quantize_slots(values, words, name):
@@ -117,8 +120,8 @@ def tile_moe_two_glu_silu_kernel(tc, xT, w1, w3, w2, gate, offs, dst, out):
 
         def round_half(copy, bf, raw, h):
             copy(
-                out=bf[:].rearrange("p t m j -> p m j t"),
-                in_=raw[:].rearrange("p j (m t) -> p m j t", t=PACK)[:, :, :, h * HALF:(h + 1) * HALF],
+                out=bf[:].rearrange("p t (a r) j -> p a j r t", r=HALF),
+                in_=raw[:].rearrange("p j (a h r t) -> p h a j r t", h=HALF, r=HALF, t=HALF)[:, h],
             )
 
         def quantize_half(name, bf):
@@ -147,15 +150,12 @@ def tile_moe_two_glu_silu_kernel(tc, xT, w1, w3, w2, gate, offs, dst, out):
             return banks
 
         def times_gate(e, b, bank, y):
-            nc.vector.tensor_tensor(out=y[:], in0=bank[:], in1=gates[:, e * C:(e + 1) * C], op=MULT)
+            nc.vector.tensor_tensor(out=y[:], in0=gates[:, e * C:(e + 1) * C], in1=bank[:], op=MULT)
 
         def scatter_on_scalar(e, b, y):
             nc.scalar.activation(out=windows[b][:].indirect(entries(dst_sb, e)), in_=y[:], func=COPY)
 
-        interleave(nc.vector.tensor_copy, slot_bf[0][:], rows[0][:, :, :C])
-        interleave(nc.scalar.copy, slot_bf[1][:], rows[0][:, :, C:])
-        for n in range(HALF):
-            interleave(nc.scalar.copy, late_bf[:, n * C:(n + 1) * C, :], rows[1][:, :, n * C:(n + 1) * C])
+        interleave(nc.scalar.copy, late_bf[:], rows[:])
         slots = quantize_slots(slot_bf[0], kept([P, C], U32, "slot_codes0"), "slot_scales0")
 
         half = [P, HALF, P, PACK]
@@ -163,17 +163,17 @@ def tile_moe_two_glu_silu_kernel(tc, xT, w1, w3, w2, gate, offs, dst, out):
         for e in range(E):
             w1_bf = [kept(half, BF16, f"w1_bf{e}_{h}") for h in range(2)]
             w3_bf = [in_region(e, h * 2 * KIB, half, BF16, f"w3_bf{e}_{h}") for h in range(2)]
-            for h in range(2):
-                round_half(nc.vector.tensor_copy, w1_bf[h], w1_raw[e], h)
+            round_half(nc.vector.tensor_copy, w1_bf[0], w1_raw[e], 0)
+            round_half(nc.scalar.copy if e == 1 else nc.vector.tensor_copy, w1_bf[1], w1_raw[e], 1)
             w1_low = quantize_half(f"w1_{e}_0", w1_bf[0])
-            round_half(nc.scalar.copy, w3_bf[1], w3_raw[e], 1)
             round_half(nc.vector.tensor_copy, w3_bf[0], w3_raw[e], 0)
+            round_half(nc.scalar.copy if e > 0 else nc.vector.tensor_copy, w3_bf[1], w3_raw[e], 1)
             w1_banks = first_product("w1", w1_low + quantize_half(f"w1_{e}_1", w1_bf[1]), slots[e])
             if e == 0:
                 slots.extend(quantize_slots(slot_bf[1], kept([P, C], U32, "slot_codes1"), "slot_scales1"))
             w3_low = quantize_half(f"w3_{e}_0", w3_bf[0])
             w3_banks = first_product("w3", w3_low + quantize_half(f"w3_{e}_1", w3_bf[1]), slots[e])
-            acts = kept([P, C, PACK], F32, f"acts{e}", f"w3_raw{e}")
+            acts = kept([P, C, PACK], F32, f"acts{e}", f"w3_raw{e}" if e > 0 else "")
             for s, bank in enumerate(w1_banks):
                 nc.scalar.activation(
                     out=acts[:, s * BANK_SLOTS:(s + 1) * BANK_SLOTS, :], in_=bank[:].rearrange("p t c -> p c t"), func=SILU
@@ -197,7 +197,7 @@ def tile_moe_two_glu_silu_kernel(tc, xT, w1, w3, w2, gate, offs, dst, out):
                     out=h_bf[:, cols, :], in0=acts[:, cols, :], in1=bank[:].rearrange("p t c -> p c t"), op=MULT
                 )
             w2_words, w2_scales = kept([P, N], U32, f"w2_codes{e}"), kept([P, N], U8, f"w2_scales{e}")
-            h_words, h_scales = kept([P, C], U32, f"h_codes{e}"), kept([P, C], U8, f"h_scales{e}")
+            h_words, h_scales = kept([P, C], U32, f"h_codes{e}", f"w2_raw{e}"), kept([P, C], U8, f"h_scales{e}")
             quantize(w2_words[:], w2_scales[:], w2_bf[:].rearrange("p c t -> p (c t)"))
             quantize(h_words[:], h_scales[:], h_bf[:].rearrange("p c t -> p (c t)"))
             y_banks = []

@@ -167,29 +167,35 @@ def tile_moe_two_glu_silu_kernel(tc, xT, w1, w3, w2, gate, offs, dst, out):
             round_half(nc.scalar.copy if e == 1 else nc.vector.tensor_copy, w1_bf[1], w1_raw[e], 1)
             w1_low = quantize_half(f"w1_{e}_0", w1_bf[0])
             round_half(nc.vector.tensor_copy, w3_bf[0], w3_raw[e], 0)
-            round_half(nc.scalar.copy if e > 0 else nc.vector.tensor_copy, w3_bf[1], w3_raw[e], 1)
+            round_half(nc.scalar.copy if e == 1 else nc.vector.tensor_copy, w3_bf[1], w3_raw[e], 1)
             w1_banks = first_product("w1", w1_low + quantize_half(f"w1_{e}_1", w1_bf[1]), slots[e])
             if e == 0:
                 slots.extend(quantize_slots(slot_bf[1], kept([P, C], U32, "slot_codes1"), "slot_scales1"))
             w3_low = quantize_half(f"w3_{e}_0", w3_bf[0])
             w3_banks = first_product("w3", w3_low + quantize_half(f"w3_{e}_1", w3_bf[1]), slots[e])
-            acts = kept([P, C, PACK], F32, f"acts{e}", f"w3_raw{e}" if e > 0 else "")
+            acts = kept([P, C, PACK], F32, f"acts{e}", f"w3_raw{e}" if e == 1 else "")
             for s, bank in enumerate(w1_banks):
                 nc.scalar.activation(
                     out=acts[:, s * BANK_SLOTS:(s + 1) * BANK_SLOTS, :], in_=bank[:].rearrange("p t c -> p c t"), func=SILU
                 )
             if e == 0:
                 slots.extend(quantize_slots(late_bf, in_region(e, 0, [P, HALF * C], U32, "late_codes"), "late_scales"))
-                w2_bf = kept([P, N, PACK], BF16, "w2_bf0", "late_bf")
+                w2_bf = kept([P, N, PACK], BF16, "w2_bf0")
+                interleave(nc.scalar.copy, w2_bf[:], w2_raw[e][:])
             else:
                 for b in range(BLOCKS):
                     y = in_region(e, b * KIB, [P, C], F32, f"y{e - 1}_{b}")
                     times_gate(e - 1, b, y_banks[b], y)
                     scatter_on_scalar(e - 1, b, y)
                 w2_bf = in_region(e, 2 * KIB, [P, N, PACK], BF16, f"w2_bf{e}")
-            nc.gpsimd.tensor_scalar(
-                out=w2_bf[:], in0=w2_raw[e][:].rearrange("p t c -> p c t"), scalar1=1.0, scalar2=0.0, op0=MULT, op1=ADD
-            )
+                nc.gpsimd.tensor_scalar(
+                    out=w2_bf[:],
+                    in0=w2_raw[e][:].rearrange("p t c -> p c t"),
+                    scalar1=1.0,
+                    scalar2=0.0,
+                    op0=MULT,
+                    op1=ADD,
+                )
             h_bf = kept([P, C, PACK], BF16, f"h_bf{e}")
             for s, bank in enumerate(w3_banks):
                 cols = slice(s * BANK_SLOTS, (s + 1) * BANK_SLOTS)
@@ -217,7 +223,6 @@ def tile_moe_two_glu_silu_kernel(tc, xT, w1, w3, w2, gate, offs, dst, out):
         last_y = [kept([P, C], F32, f"last_y{b}") for b in range(BLOCKS)]
         for b in range(BLOCKS):
             times_gate(LAST, b, y_banks[b], last_y[b])
-        nc.vector.tensor_copy(out=windows[0][:].indirect(entries(dst_sb, LAST)), in_=last_y[0][:])
-        nc.sync.dma_start(out=out[:P, :], in_=windows[0][:])
-        scatter_on_scalar(LAST, 1, last_y[1])
-        nc.scalar.dma_start(out=out[P:, :], in_=windows[1][:])
+        for b, queue in enumerate((nc.sync, nc.scalar)):
+            nc.vector.tensor_copy(out=windows[b][:].indirect(entries(dst_sb, LAST)), in_=last_y[b][:])
+            queue.dma_start(out=out[b * P:(b + 1) * P, :], in_=windows[b][:])

@@ -15,7 +15,6 @@ FP8X4 = mybir.dt.float8_e4m3fn_x4
 COPY = mybir.ActivationFunctionType.Copy
 SILU = mybir.ActivationFunctionType.Silu
 MULT = mybir.AluOpType.mult
-ADD = mybir.AluOpType.add
 
 P = 128
 PACK = 4
@@ -68,20 +67,13 @@ def tile_moe_two_glu_silu_kernel(tc, xT, w1, w3, w2, gate, offs, dst, out):
             nc.sync.dma_start(out=raw[:], in_=w[e].rearrange("(p j) n -> p j n", j=PACK))
             return raw
 
-        def load_second(e):
-            raw = kept([P, PACK, N], F32, f"w2_raw{e}")
-            rows = w2[e].rearrange("(a h r t) n -> r a h (t n)", h=HALF, r=HALF, t=HALF)
-            for r in range(HALF):
-                nc.sync.dma_start(out=raw[r:P:HALF].rearrange("p (h t) n -> p h (t n)", h=HALF), in_=rows[r])
-            return raw
-
         w1_raw, w3_raw, w2_raw = [], [], []
         for e in range(E):
             w1_raw.append(load(w1, e, "w1"))
             if e == 1:
                 nc.sync.dma_start(dst_sb[:], dst)
             w3_raw.append(load(w3, e, "w3"))
-            w2_raw.append(load_second(e))
+            w2_raw.append(load(w2, e, "w2"))
 
         make_identity(nc, identity[:])
         for window in windows:
@@ -120,8 +112,8 @@ def tile_moe_two_glu_silu_kernel(tc, xT, w1, w3, w2, gate, offs, dst, out):
 
         def round_half(copy, bf, raw, h):
             copy(
-                out=bf[:].rearrange("p t (a r) j -> p a j r t", r=HALF),
-                in_=raw[:].rearrange("p j (a h r t) -> p h a j r t", h=HALF, r=HALF, t=HALF)[:, h],
+                out=bf[:].rearrange("p t m j -> p m j t"),
+                in_=raw[:].rearrange("p j (m t) -> p m j t", t=PACK)[:, :, :, h * HALF:(h + 1) * HALF],
             )
 
         def quantize_half(name, bf):
@@ -183,19 +175,12 @@ def tile_moe_two_glu_silu_kernel(tc, xT, w1, w3, w2, gate, offs, dst, out):
                 w2_bf = kept([P, N, PACK], BF16, "w2_bf0")
                 interleave(nc.scalar.copy, w2_bf[:], w2_raw[e][:])
             else:
+                w2_bf = in_region(e, 0, [P, N, PACK], BF16, f"w2_bf{e}")
+                interleave(nc.vector.tensor_copy, w2_bf[:], w2_raw[e][:])
                 for b in range(BLOCKS):
-                    y = in_region(e, b * KIB, [P, C], F32, f"y{e - 1}_{b}")
+                    y = in_region(e, (2 + b) * KIB, [P, C], F32, f"y{e - 1}_{b}")
                     times_gate(e - 1, b, y_banks[b], y)
                     scatter_on_scalar(e - 1, b, y)
-                w2_bf = in_region(e, 2 * KIB, [P, N, PACK], BF16, f"w2_bf{e}")
-                nc.gpsimd.tensor_scalar(
-                    out=w2_bf[:],
-                    in0=w2_raw[e][:].rearrange("p t c -> p c t"),
-                    scalar1=1.0,
-                    scalar2=0.0,
-                    op0=MULT,
-                    op1=ADD,
-                )
             h_bf = kept([P, C, PACK], BF16, f"h_bf{e}")
             for s, bank in enumerate(w3_banks):
                 cols = slice(s * BANK_SLOTS, (s + 1) * BANK_SLOTS)

@@ -18,14 +18,18 @@ MULT = mybir.AluOpType.mult
 
 P = 128
 PACK = 4
-HALF = 2
+HALF = PACK // 2
+EARLY = 2
 BANK_SLOTS = 128
 GATE_COLS = E * C // P
 LIST_COLS = C // 16
 BLOCKS = N // P
 LAST = E - 1
-KIB = 1024
-REGION = 4 * KIB
+HELPED = 1
+
+HALF_BYTES = HALF * P * PACK * 2
+Y_BYTES = C * 4
+REGION = 2 * HALF_BYTES
 
 
 def tile_moe_two_glu_silu_kernel(tc, xT, w1, w3, w2, gate, offs, dst, out):
@@ -70,7 +74,7 @@ def tile_moe_two_glu_silu_kernel(tc, xT, w1, w3, w2, gate, offs, dst, out):
         w1_raw, w3_raw, w2_raw = [], [], []
         for e in range(E):
             w1_raw.append(load(w1, e, "w1"))
-            if e == 1:
+            if e == HELPED:
                 nc.sync.dma_start(dst_sb[:], dst)
             w3_raw.append(load(w3, e, "w3"))
             w2_raw.append(load(w2, e, "w2"))
@@ -90,12 +94,15 @@ def tile_moe_two_glu_silu_kernel(tc, xT, w1, w3, w2, gate, offs, dst, out):
         def entries(list_sb, first, count=1):
             return list_sb[:, first * LIST_COLS:(first + count) * LIST_COLS]
 
-        slot_bf = [kept([P, C, PACK], BF16, f"slot_bf{e}") for e in range(HALF)]
-        rows = kept([P, PACK, HALF * C], BF16, "rows")
+        late = E - EARLY
+        slot_bf = [kept([P, C, PACK], BF16, f"slot_bf{e}") for e in range(EARLY)]
+        rows = kept([P, PACK, late * C], BF16, "rows")
         for j in range(PACK):
-            for e in range(HALF):
+            for e in range(EARLY):
                 nc.vector.tensor_copy(out=slot_bf[e][:, :, j], in_=x_planes[j][:].indirect(entries(offs_sb, e)))
-            nc.scalar.activation(out=rows[:, j, :], in_=x_planes[j][:].indirect(entries(offs_sb, HALF, HALF)), func=COPY)
+            nc.scalar.activation(
+                out=rows[:, j, :], in_=x_planes[j][:].indirect(entries(offs_sb, EARLY, late)), func=COPY
+            )
 
         def interleave(copy, side_by_side, planes):
             copy(
@@ -103,17 +110,17 @@ def tile_moe_two_glu_silu_kernel(tc, xT, w1, w3, w2, gate, offs, dst, out):
                 in_=planes.rearrange("p j (c i) -> p c j i", i=PACK),
             )
 
-        late_bf = kept([P, HALF * C, PACK], BF16, "late_bf")
+        late_bf = kept([P, late * C, PACK], BF16, "late_bf")
 
         def quantize_slots(values, words, name):
             scales = kept([P, words.shape[1]], U8, name)
             quantize(words[:], scales[:], values[:].rearrange("p c j -> p (c j)"))
             return [(words[:, c:c + C], scales[:, c:c + C]) for c in range(0, words.shape[1], C)]
 
-        def round_half(copy, bf, raw, h):
+        def round_half(copy, bf, raw, h, cols=slice(0, P)):
             copy(
-                out=bf[:].rearrange("p t m j -> p m j t"),
-                in_=raw[:].rearrange("p j (m t) -> p m j t", t=PACK)[:, :, :, h * HALF:(h + 1) * HALF],
+                out=bf[:].rearrange("p t m j -> p m j t")[:, cols],
+                in_=raw[:].rearrange("p j (m t) -> p m j t", t=PACK)[:, cols, :, h * HALF:(h + 1) * HALF],
             )
 
         def quantize_half(name, bf):
@@ -122,8 +129,8 @@ def tile_moe_two_glu_silu_kernel(tc, xT, w1, w3, w2, gate, offs, dst, out):
             quantize(words[:], scales[:], bf[:].rearrange("p t m j -> p (t m j)"))
             return [(words[:, c:c + P], scales[:, c:c + P]) for c in range(0, HALF * P, P)]
 
-        def first_product(name, by_t, slots):
-            slot_words, slot_scales = slots
+        def first_product(name, by_t, slot_codes):
+            slot_words, slot_scales = slot_codes
             banks = []
             for s in range(C // BANK_SLOTS):
                 cols = slice(s * BANK_SLOTS, (s + 1) * BANK_SLOTS)
@@ -141,7 +148,7 @@ def tile_moe_two_glu_silu_kernel(tc, xT, w1, w3, w2, gate, offs, dst, out):
                 banks.append(bank)
             return banks
 
-        def times_gate(e, b, bank, y):
+        def times_gate(e, bank, y):
             nc.vector.tensor_tensor(out=y[:], in0=gates[:, e * C:(e + 1) * C], in1=bank[:], op=MULT)
 
         def scatter_on_scalar(e, b, y):
@@ -154,32 +161,37 @@ def tile_moe_two_glu_silu_kernel(tc, xT, w1, w3, w2, gate, offs, dst, out):
         y_banks = []
         for e in range(E):
             w1_bf = [kept(half, BF16, f"w1_bf{e}_{h}") for h in range(2)]
-            w3_bf = [in_region(e, h * 2 * KIB, half, BF16, f"w3_bf{e}_{h}") for h in range(2)]
-            round_half(nc.vector.tensor_copy, w1_bf[0], w1_raw[e], 0)
-            round_half(nc.scalar.copy if e == 1 else nc.vector.tensor_copy, w1_bf[1], w1_raw[e], 1)
+            w3_bf = [in_region(e, h * HALF_BYTES, half, BF16, f"w3_bf{e}_{h}") for h in range(2)]
+            if e == HELPED:
+                round_half(nc.scalar.copy, w1_bf[1], w1_raw[e], 1)
+                round_half(nc.scalar.copy, w1_bf[0], w1_raw[e], 0, slice(P // 2, P))
+                round_half(nc.vector.tensor_copy, w1_bf[0], w1_raw[e], 0, slice(0, P // 2))
+            else:
+                for h in range(2):
+                    round_half(nc.vector.tensor_copy, w1_bf[h], w1_raw[e], h)
             w1_low = quantize_half(f"w1_{e}_0", w1_bf[0])
             round_half(nc.vector.tensor_copy, w3_bf[0], w3_raw[e], 0)
-            round_half(nc.scalar.copy if e == 1 else nc.vector.tensor_copy, w3_bf[1], w3_raw[e], 1)
+            round_half(nc.scalar.copy if e == HELPED else nc.vector.tensor_copy, w3_bf[1], w3_raw[e], 1)
             w1_banks = first_product("w1", w1_low + quantize_half(f"w1_{e}_1", w1_bf[1]), slots[e])
             if e == 0:
                 slots.extend(quantize_slots(slot_bf[1], kept([P, C], U32, "slot_codes1"), "slot_scales1"))
             w3_low = quantize_half(f"w3_{e}_0", w3_bf[0])
             w3_banks = first_product("w3", w3_low + quantize_half(f"w3_{e}_1", w3_bf[1]), slots[e])
-            acts = kept([P, C, PACK], F32, f"acts{e}", f"w3_raw{e}" if e == 1 else "")
+            acts = kept([P, C, PACK], F32, f"acts{e}", f"w3_raw{e}" if e == HELPED else "")
             for s, bank in enumerate(w1_banks):
-                nc.scalar.activation(
-                    out=acts[:, s * BANK_SLOTS:(s + 1) * BANK_SLOTS, :], in_=bank[:].rearrange("p t c -> p c t"), func=SILU
-                )
+                cols = slice(s * BANK_SLOTS, (s + 1) * BANK_SLOTS)
+                nc.scalar.activation(out=acts[:, cols, :], in_=bank[:].rearrange("p t c -> p c t"), func=SILU)
             if e == 0:
-                slots.extend(quantize_slots(late_bf, in_region(e, 0, [P, HALF * C], U32, "late_codes"), "late_scales"))
+                slots.extend(quantize_slots(late_bf, in_region(e, 0, [P, late * C], U32, "late_codes"), "late_scales"))
                 w2_bf = kept([P, N, PACK], BF16, "w2_bf0")
                 interleave(nc.scalar.copy, w2_bf[:], w2_raw[e][:])
             else:
                 w2_bf = in_region(e, 0, [P, N, PACK], BF16, f"w2_bf{e}")
-                interleave(nc.vector.tensor_copy, w2_bf[:], w2_raw[e][:])
-                for b in range(BLOCKS):
-                    y = in_region(e, (2 + b) * KIB, [P, C], F32, f"y{e - 1}_{b}")
-                    times_gate(e - 1, b, y_banks[b], y)
+                interleave(nc.vector.tensor_copy, w2_bf[:, :P, :], w2_raw[e][:, :, :P])
+                interleave(nc.scalar.copy, w2_bf[:, P:, :], w2_raw[e][:, :, P:])
+                for b in range(BLOCKS if e < LAST else 1):
+                    y = in_region(e, HALF_BYTES + b * Y_BYTES, [P, C], F32, f"y{e - 1}_{b}")
+                    times_gate(e - 1, y_banks[b], y)
                     scatter_on_scalar(e - 1, b, y)
             h_bf = kept([P, C, PACK], BF16, f"h_bf{e}")
             for s, bank in enumerate(w3_banks):
@@ -191,6 +203,10 @@ def tile_moe_two_glu_silu_kernel(tc, xT, w1, w3, w2, gate, offs, dst, out):
             h_words, h_scales = kept([P, C], U32, f"h_codes{e}", f"w2_raw{e}"), kept([P, C], U8, f"h_scales{e}")
             quantize(w2_words[:], w2_scales[:], w2_bf[:].rearrange("p c t -> p (c t)"))
             quantize(h_words[:], h_scales[:], h_bf[:].rearrange("p c t -> p (c t)"))
+            if e == LAST:
+                y = in_region(e, HALF_BYTES + Y_BYTES, [P, C], F32, "kept_back_y")
+                times_gate(e - 1, y_banks[1], y)
+                scatter_on_scalar(e - 1, 1, y)
             y_banks = []
             for b in range(BLOCKS):
                 bank = psum_y.tile([P, C], F32, name="y_bank")
@@ -207,7 +223,7 @@ def tile_moe_two_glu_silu_kernel(tc, xT, w1, w3, w2, gate, offs, dst, out):
 
         last_y = [kept([P, C], F32, f"last_y{b}") for b in range(BLOCKS)]
         for b in range(BLOCKS):
-            times_gate(LAST, b, y_banks[b], last_y[b])
+            times_gate(LAST, y_banks[b], last_y[b])
         for b, queue in enumerate((nc.sync, nc.scalar)):
             nc.vector.tensor_copy(out=windows[b][:].indirect(entries(dst_sb, LAST)), in_=last_y[b][:])
             queue.dma_start(out=out[b * P:(b + 1) * P, :], in_=windows[b][:])

@@ -15,6 +15,7 @@ FP8X4 = mybir.dt.float8_e4m3fn_x4
 COPY = mybir.ActivationFunctionType.Copy
 SILU = mybir.ActivationFunctionType.Silu
 MULT = mybir.AluOpType.mult
+ADD = mybir.AluOpType.add
 
 P = 128
 PACK = 4
@@ -25,29 +26,24 @@ GATE_COLS = E * C // P
 LIST_COLS = C // 16
 BLOCKS = N // P
 LAST = E - 1
-HELPED = 1
-
-HALF_BYTES = HALF * P * PACK * 2
-Y_BYTES = C * 4
-REGION = 2 * HALF_BYTES
+W3_OWN = (128, 128, 128, 0)
 
 
 def tile_moe_two_glu_silu_kernel(tc, xT, w1, w3, w2, gate, offs, dst, out):
     nc = tc.nc
     with ExitStack() as ctx:
         keep = ctx.enter_context(tc.tile_pool(name="keep", bufs=1))
-        placed = ctx.enter_context(tc.tile_pool(name="placed", bufs=1))
         psum = ctx.enter_context(tc.psum_pool(name="psum", bufs=2))
         psum_y = ctx.enter_context(tc.psum_pool(name="psum_y", bufs=4))
 
         def kept(shape, dtype, name, behind=""):
             return keep.tile(shape, dtype, name=name, tag=behind or name, align_bytes=64)
 
-        def in_region(region, at, shape, dtype, name):
-            return placed.tile(shape, dtype, name=name, align_bytes=64, offset=region * REGION + at)
-
         def quantize(words, scales, values):
             nc.vector.quantize_mx(out=words.bitcast(FP8X4), scales=scales, in_=values)
+
+        def gpsimd_copy(out, in_):
+            nc.gpsimd.tensor_scalar(out=out, in0=in_, scalar1=1.0, scalar2=0.0, op0=MULT, op1=ADD)
 
         offs_sb = keep.tile([P, E * LIST_COLS], U16, name="offs_sb")
         dst_sb = keep.tile([P, E * LIST_COLS], U16, name="dst_sb")
@@ -60,7 +56,7 @@ def tile_moe_two_glu_silu_kernel(tc, xT, w1, w3, w2, gate, offs, dst, out):
         x_rows = xT.rearrange("(p j) t -> p j t", j=PACK)
         x_planes = []
         for j in range(PACK):
-            plane = keep.tile([P, T], F32, name=f"x_plane{j}")
+            plane = kept([P, T], F32, f"x_plane{j}")
             nc.sync.dma_start(out=plane[:], in_=x_rows[:, j, :])
             x_planes.append(plane)
             if j == 0:
@@ -71,13 +67,14 @@ def tile_moe_two_glu_silu_kernel(tc, xT, w1, w3, w2, gate, offs, dst, out):
             nc.sync.dma_start(out=raw[:], in_=w[e].rearrange("(p j) n -> p j n", j=PACK))
             return raw
 
-        w1_raw, w3_raw, w2_raw = [], [], []
+        w1_raw, w3_raw, w2_raw = [load(w1, 0, "w1")], [], []
         for e in range(E):
-            w1_raw.append(load(w1, e, "w1"))
-            if e == HELPED:
-                nc.sync.dma_start(dst_sb[:], dst)
             w3_raw.append(load(w3, e, "w3"))
+            if e < LAST:
+                w1_raw.append(load(w1, e + 1, "w1"))
             w2_raw.append(load(w2, e, "w2"))
+            if e == 0:
+                nc.sync.dma_start(dst_sb[:], dst)
 
         make_identity(nc, identity[:])
         for window in windows:
@@ -112,10 +109,11 @@ def tile_moe_two_glu_silu_kernel(tc, xT, w1, w3, w2, gate, offs, dst, out):
 
         late_bf = kept([P, late * C, PACK], BF16, "late_bf")
 
-        def quantize_slots(values, words, name):
-            scales = kept([P, words.shape[1]], U8, name)
+        def quantize_slots(values, name, behind=""):
+            width = values.shape[1]
+            words, scales = kept([P, width], U32, f"{name}_codes", behind), kept([P, width], U8, f"{name}_scales")
             quantize(words[:], scales[:], values[:].rearrange("p c j -> p (c j)"))
-            return [(words[:, c:c + C], scales[:, c:c + C]) for c in range(0, words.shape[1], C)]
+            return [(words[:, c:c + C], scales[:, c:c + C]) for c in range(0, width, C)]
 
         def round_half(copy, bf, raw, h, cols=slice(0, P)):
             copy(
@@ -123,8 +121,8 @@ def tile_moe_two_glu_silu_kernel(tc, xT, w1, w3, w2, gate, offs, dst, out):
                 in_=raw[:].rearrange("p j (m t) -> p m j t", t=PACK)[:, cols, :, h * HALF:(h + 1) * HALF],
             )
 
-        def quantize_half(name, bf):
-            words = kept([P, HALF * P], U32, f"{name}_codes")
+        def quantize_half(name, bf, behind=""):
+            words = kept([P, HALF * P], U32, f"{name}_codes", behind)
             scales = kept([P, HALF * P], U8, f"{name}_scales")
             quantize(words[:], scales[:], bf[:].rearrange("p t m j -> p (t m j)"))
             return [(words[:, c:c + P], scales[:, c:c + P]) for c in range(0, HALF * P, P)]
@@ -148,66 +146,82 @@ def tile_moe_two_glu_silu_kernel(tc, xT, w1, w3, w2, gate, offs, dst, out):
                 banks.append(bank)
             return banks
 
-        def times_gate(e, bank, y):
-            nc.vector.tensor_tensor(out=y[:], in0=gates[:, e * C:(e + 1) * C], in1=bank[:], op=MULT)
+        def times_gate(e, y, bank):
+            nc.vector.tensor_tensor(out=y, in0=gates[:, e * C:(e + 1) * C], in1=bank[:], op=MULT)
 
         def scatter_on_scalar(e, b, y):
-            nc.scalar.activation(out=windows[b][:].indirect(entries(dst_sb, e)), in_=y[:], func=COPY)
+            nc.scalar.activation(out=windows[b][:].indirect(entries(dst_sb, e)), in_=y, func=COPY)
+
+        def halves(name, e, behind=("", "")):
+            return [kept([P, HALF, P, PACK], BF16, f"{name}_bf{e}_{h}", behind[h]) for h in range(2)]
+
+        def round_shared(bf, raw, own):
+            round_half(nc.vector.tensor_copy, bf[0], raw, 0)
+            if own < P:
+                round_half(nc.scalar.copy, bf[1], raw, 1, slice(own, P))
+            if own:
+                round_half(nc.vector.tensor_copy, bf[1], raw, 1, slice(0, own))
 
         interleave(nc.scalar.copy, late_bf[:], rows[:])
-        slots = quantize_slots(slot_bf[0], kept([P, C], U32, "slot_codes0"), "slot_scales0")
-
-        half = [P, HALF, P, PACK]
-        y_banks = []
+        slots = quantize_slots(slot_bf[0], "slot0")
+        slots.extend(quantize_slots(slot_bf[1], "slot1"))
+        w1_bf = halves("w1", 0)
+        round_shared(w1_bf, w1_raw[0], P)
+        w1_codes = quantize_half("w1_0_0", w1_bf[0]) + quantize_half("w1_0_1", w1_bf[1])
+        w1_banks = first_product("w1", w1_codes, slots[0])
+        waiting = []
         for e in range(E):
-            w1_bf = [kept(half, BF16, f"w1_bf{e}_{h}") for h in range(2)]
-            w3_bf = [in_region(e, h * HALF_BYTES, half, BF16, f"w3_bf{e}_{h}") for h in range(2)]
-            if e == HELPED:
-                round_half(nc.scalar.copy, w1_bf[1], w1_raw[e], 1)
-                round_half(nc.scalar.copy, w1_bf[0], w1_raw[e], 0, slice(P // 2, P))
-                round_half(nc.vector.tensor_copy, w1_bf[0], w1_raw[e], 0, slice(0, P // 2))
-            else:
-                for h in range(2):
-                    round_half(nc.vector.tensor_copy, w1_bf[h], w1_raw[e], h)
-            w1_low = quantize_half(f"w1_{e}_0", w1_bf[0])
-            round_half(nc.vector.tensor_copy, w3_bf[0], w3_raw[e], 0)
-            round_half(nc.scalar.copy if e == HELPED else nc.vector.tensor_copy, w3_bf[1], w3_raw[e], 1)
-            w1_banks = first_product("w1", w1_low + quantize_half(f"w1_{e}_1", w1_bf[1]), slots[e])
-            if e == 0:
-                slots.extend(quantize_slots(slot_bf[1], kept([P, C], U32, "slot_codes1"), "slot_scales1"))
-            w3_low = quantize_half(f"w3_{e}_0", w3_bf[0])
-            w3_banks = first_product("w3", w3_low + quantize_half(f"w3_{e}_1", w3_bf[1]), slots[e])
-            acts = kept([P, C, PACK], F32, f"acts{e}", f"w3_raw{e}" if e == HELPED else "")
+            w2_at = [f"acts{f}_0" if f else "w2_bf0" for f in range(E)]
+            w3_at = (f"h_bf{e - 1}", f"w2_raw{e - 1}" if e == LAST else w2_at[e - 1]) if e else ("w3_bf0_0", "w3_bf0_1")
+            w3_bf = halves("w3", e, w3_at)
+            round_shared(w3_bf, w3_raw[e], W3_OWN[e])
+            acts = []
             for s, bank in enumerate(w1_banks):
-                cols = slice(s * BANK_SLOTS, (s + 1) * BANK_SLOTS)
-                nc.scalar.activation(out=acts[:, cols, :], in_=bank[:].rearrange("p t c -> p c t"), func=SILU)
+                act = kept([P, BANK_SLOTS, PACK], F32, f"acts{e}_{s}", f"w3_raw{e}" if s == 0 and W3_OWN[e] < P else "")
+                nc.scalar.activation(out=act[:], in_=bank[:].rearrange("p t c -> p c t"), func=SILU)
+                acts.append(act)
+            w3_codes = quantize_half(f"w3_{e}_0", w3_bf[0]) + quantize_half(f"w3_{e}_1", w3_bf[1], w2_at[e - 1] if e == LAST else "")
+            w3_banks = first_product("w3", w3_codes, slots[e])
+            spent = w3_at[0]
             if e == 0:
-                slots.extend(quantize_slots(late_bf, in_region(e, 0, [P, late * C], U32, "late_codes"), "late_scales"))
-                w2_bf = kept([P, N, PACK], BF16, "w2_bf0")
-                interleave(nc.scalar.copy, w2_bf[:], w2_raw[e][:])
-            else:
-                w2_bf = in_region(e, 0, [P, N, PACK], BF16, f"w2_bf{e}")
-                interleave(nc.vector.tensor_copy, w2_bf[:, :P, :], w2_raw[e][:, :, :P])
-                interleave(nc.scalar.copy, w2_bf[:, P:, :], w2_raw[e][:, :, P:])
-                for b in range(BLOCKS if e < LAST else 1):
-                    y = in_region(e, HALF_BYTES + b * Y_BYTES, [P, C], F32, f"y{e - 1}_{b}")
-                    times_gate(e - 1, y_banks[b], y)
-                    scatter_on_scalar(e - 1, b, y)
+                slots.extend(quantize_slots(late_bf, "late", "w3_bf0_0"))
+                spent = "late_bf"
+            now = waiting[:1] if e == LAST - 1 else waiting
+            waiting = waiting[len(now):]
+            now = sorted(now, key=lambda item: item[1])
+            region = kept([P, len(now) or 1, C], F32, f"y_region{e}", w3_at[1]) if now else None
+            for i, (f, b, bank) in enumerate(now):
+                times_gate(f, region[:, i, :], bank)
+            if e < LAST:
+                w1_bf = [
+                    kept([P, HALF, P, PACK], BF16, f"w1_bf{e + 1}_0", spent),
+                    kept([P, HALF, P, PACK], BF16, f"w1_bf{e + 1}_1", f"w3_raw{e}"),
+                ]
+                round_half(gpsimd_copy, w1_bf[0], w1_raw[e + 1], 0)
+                round_half(nc.scalar.copy, w1_bf[1], w1_raw[e + 1], 1)
+            for i, (f, b, bank) in enumerate(now):
+                scatter_on_scalar(f, b, region[:, i, :])
+            w2_bf = kept([P, N, PACK], BF16, f"w2_bf{e}", spent if e == LAST else (f"acts{e}_0" if e else ""))
+            if e == LAST:
+                gpsimd_copy(out=w2_bf[:], in_=w2_raw[e][:].rearrange("p j c -> p c j"))
             h_bf = kept([P, C, PACK], BF16, f"h_bf{e}")
             for s, bank in enumerate(w3_banks):
                 cols = slice(s * BANK_SLOTS, (s + 1) * BANK_SLOTS)
                 nc.vector.tensor_tensor(
-                    out=h_bf[:, cols, :], in0=acts[:, cols, :], in1=bank[:].rearrange("p t c -> p c t"), op=MULT
+                    out=h_bf[:, cols, :], in0=acts[s][:], in1=bank[:].rearrange("p t c -> p c t"), op=MULT
                 )
-            w2_words, w2_scales = kept([P, N], U32, f"w2_codes{e}"), kept([P, N], U8, f"w2_scales{e}")
-            h_words, h_scales = kept([P, C], U32, f"h_codes{e}", f"w2_raw{e}"), kept([P, C], U8, f"h_scales{e}")
-            quantize(w2_words[:], w2_scales[:], w2_bf[:].rearrange("p c t -> p (c t)"))
-            quantize(h_words[:], h_scales[:], h_bf[:].rearrange("p c t -> p (c t)"))
-            if e == LAST:
-                y = in_region(e, HALF_BYTES + Y_BYTES, [P, C], F32, "kept_back_y")
-                times_gate(e - 1, y_banks[1], y)
-                scatter_on_scalar(e - 1, 1, y)
-            y_banks = []
+            if e < LAST:
+                interleave(nc.scalar.copy if e == 0 else nc.vector.tensor_copy, w2_bf[:], w2_raw[e][:])
+            if e < LAST:
+                w1_codes = quantize_half(f"w1_{e + 1}_0", w1_bf[0])
+                w1_codes = w1_codes + quantize_half(f"w1_{e + 1}_1", w1_bf[1], f"w1_raw{e + 1}")
+                w1_banks = first_product("w1", w1_codes, slots[e + 1])
+            w2_words = kept([P, N], U32, f"w2_codes{e}", f"w3_raw{e}")
+            h_words = kept([P, C], U32, f"h_codes{e}", f"w2_raw{e}" if e == LAST else spent)
+            w2_scales, h_scales = kept([P, N], U8, f"w2_scales{e}"), kept([P, C], U8, f"h_scales{e}")
+            operands = [(h_words, h_scales, h_bf), (w2_words, w2_scales, w2_bf)]
+            for words, scales, values in operands[::-1] if e == LAST else operands:
+                quantize(words[:], scales[:], values[:].rearrange("p c t -> p (c t)"))
             for b in range(BLOCKS):
                 bank = psum_y.tile([P, C], F32, name="y_bank")
                 nc.tensor.matmul_mx(
@@ -219,11 +233,12 @@ def tile_moe_two_glu_silu_kernel(tc, xT, w1, w3, w2, gate, offs, dst, out):
                     start=True,
                     stop=True,
                 )
-                y_banks.append(bank)
+                waiting.append((e, b, bank))
 
-        last_y = [kept([P, C], F32, f"last_y{b}") for b in range(BLOCKS)]
-        for b in range(BLOCKS):
-            times_gate(LAST, y_banks[b], last_y[b])
-        for b, queue in enumerate((nc.sync, nc.scalar)):
-            nc.vector.tensor_copy(out=windows[b][:].indirect(entries(dst_sb, LAST)), in_=last_y[b][:])
-            queue.dma_start(out=out[b * P:(b + 1) * P, :], in_=windows[b][:])
+        last_y = kept([P, BLOCKS, C], F32, "last_y")
+        for f, b, bank in waiting:
+            times_gate(f, last_y[:, b, :], bank)
+        nc.vector.tensor_copy(out=windows[0][:].indirect(entries(dst_sb, LAST)), in_=last_y[:, 0, :])
+        nc.sync.dma_start(out=out[:P, :], in_=windows[0][:])
+        scatter_on_scalar(LAST, 1, last_y[:, 1, :])
+        nc.sync.dma_start(out=out[P:, :], in_=windows[1][:])

@@ -26,18 +26,24 @@ GATE_COLS = E * C // P
 LIST_COLS = C // 16
 BLOCKS = N // P
 LAST = E - 1
-W3_OWN = (128, 128, 128, 0)
+HALF_BYTES = HALF * P * PACK * 2
+Y_BYTES = C * 4
+REGION = HALF_BYTES + Y_BYTES
 
 
 def tile_moe_two_glu_silu_kernel(tc, xT, w1, w3, w2, gate, offs, dst, out):
     nc = tc.nc
     with ExitStack() as ctx:
         keep = ctx.enter_context(tc.tile_pool(name="keep", bufs=1))
+        placed = ctx.enter_context(tc.tile_pool(name="placed", bufs=1))
         psum = ctx.enter_context(tc.psum_pool(name="psum", bufs=2))
         psum_y = ctx.enter_context(tc.psum_pool(name="psum_y", bufs=4))
 
         def kept(shape, dtype, name, behind=""):
             return keep.tile(shape, dtype, name=name, tag=behind or name, align_bytes=64)
+
+        def at(offset, shape, dtype, name):
+            return placed.tile(shape, dtype, name=name, align_bytes=64, offset=offset)
 
         def quantize(words, scales, values):
             nc.vector.quantize_mx(out=words.bitcast(FP8X4), scales=scales, in_=values)
@@ -109,9 +115,9 @@ def tile_moe_two_glu_silu_kernel(tc, xT, w1, w3, w2, gate, offs, dst, out):
 
         late_bf = kept([P, late * C, PACK], BF16, "late_bf")
 
-        def quantize_slots(values, name, behind=""):
+        def quantize_slots(values, name, words=None):
             width = values.shape[1]
-            words, scales = kept([P, width], U32, f"{name}_codes", behind), kept([P, width], U8, f"{name}_scales")
+            words, scales = words if words is not None else kept([P, width], U32, f"{name}_codes"), kept([P, width], U8, f"{name}_scales")
             quantize(words[:], scales[:], values[:].rearrange("p c j -> p (c j)"))
             return [(words[:, c:c + C], scales[:, c:c + C]) for c in range(0, width, C)]
 
@@ -121,8 +127,8 @@ def tile_moe_two_glu_silu_kernel(tc, xT, w1, w3, w2, gate, offs, dst, out):
                 in_=raw[:].rearrange("p j (m t) -> p m j t", t=PACK)[:, cols, :, h * HALF:(h + 1) * HALF],
             )
 
-        def quantize_half(name, bf, behind=""):
-            words = kept([P, HALF * P], U32, f"{name}_codes", behind)
+        def quantize_half(name, bf, words=None):
+            words = words if words is not None else kept([P, HALF * P], U32, f"{name}_codes")
             scales = kept([P, HALF * P], U8, f"{name}_scales")
             quantize(words[:], scales[:], bf[:].rearrange("p t m j -> p (t m j)"))
             return [(words[:, c:c + P], scales[:, c:c + P]) for c in range(0, HALF * P, P)]
@@ -169,59 +175,72 @@ def tile_moe_two_glu_silu_kernel(tc, xT, w1, w3, w2, gate, offs, dst, out):
         round_shared(w1_bf, w1_raw[0], P)
         w1_codes = quantize_half("w1_0_0", w1_bf[0]) + quantize_half("w1_0_1", w1_bf[1])
         w1_banks = first_product("w1", w1_codes, slots[0])
+        half = [P, HALF, P, PACK]
         waiting = []
+
+        def release(blocks, ys):
+            for i, (f, b, bank) in enumerate(blocks):
+                times_gate(f, ys[:, i, :], bank)
+            for i, (f, b, bank) in enumerate(blocks):
+                scatter_on_scalar(f, b, ys[:, i, :])
+                waiting.remove((f, b, bank))
+
         for e in range(E):
-            w2_at = [f"acts{f}_0" if f else "w2_bf0" for f in range(E)]
-            w3_at = (f"h_bf{e - 1}", f"w2_raw{e - 1}" if e == LAST else w2_at[e - 1]) if e else ("w3_bf0_0", "w3_bf0_1")
-            w3_bf = halves("w3", e, w3_at)
-            round_shared(w3_bf, w3_raw[e], W3_OWN[e])
+            second_at = HALF_BYTES + e * REGION
+            first_at = second_at - HALF_BYTES
+            low = at(first_at, half, BF16, f"w3_bf{e}_0")
+            if e < LAST:
+                w3_bf = [low, at(second_at, half, BF16, f"w3_bf{e}_1")]
+            else:
+                w3_bf = [low, kept(half, BF16, f"w3_bf{e}_1", f"acts{e - 1}_0")]
+            round_half(nc.vector.tensor_copy, w3_bf[0], w3_raw[e], 0)
+            round_half(nc.scalar.copy if e == LAST else nc.vector.tensor_copy, w3_bf[1], w3_raw[e], 1)
             acts = []
             for s, bank in enumerate(w1_banks):
-                act = kept([P, BANK_SLOTS, PACK], F32, f"acts{e}_{s}", f"w3_raw{e}" if s == 0 and W3_OWN[e] < P else "")
+                act = kept([P, BANK_SLOTS, PACK], F32, f"acts{e}_{s}", f"w3_raw{e}" if s == 0 and e == LAST else "")
                 nc.scalar.activation(out=act[:], in_=bank[:].rearrange("p t c -> p c t"), func=SILU)
                 acts.append(act)
-            w3_codes = quantize_half(f"w3_{e}_0", w3_bf[0]) + quantize_half(f"w3_{e}_1", w3_bf[1], w2_at[e - 1] if e == LAST else "")
-            w3_banks = first_product("w3", w3_codes, slots[e])
-            spent = w3_at[0]
-            if e == 0:
-                slots.extend(quantize_slots(late_bf, "late", "w3_bf0_0"))
-                spent = "late_bf"
-            now = waiting[:1] if e == LAST - 1 else waiting
-            waiting = waiting[len(now):]
-            now = sorted(now, key=lambda item: item[1])
-            region = kept([P, len(now) or 1, C], F32, f"y_region{e}", w3_at[1]) if now else None
-            for i, (f, b, bank) in enumerate(now):
-                times_gate(f, region[:, i, :], bank)
             if e < LAST:
-                w1_bf = [
-                    kept([P, HALF, P, PACK], BF16, f"w1_bf{e + 1}_0", spent),
-                    kept([P, HALF, P, PACK], BF16, f"w1_bf{e + 1}_1", f"w3_raw{e}"),
-                ]
-                round_half(gpsimd_copy, w1_bf[0], w1_raw[e + 1], 0)
+                w3_codes = quantize_half(f"w3_{e}_0", w3_bf[0]) + quantize_half(f"w3_{e}_1", w3_bf[1])
+            else:
+                high = quantize_half(f"w3_{e}_1", w3_bf[1], at(second_at, [P, HALF * P], U32, "last_w3_codes"))
+                w3_codes = quantize_half(f"w3_{e}_0", w3_bf[0]) + high
+            w3_banks = first_product("w3", w3_codes, slots[e])
+            if e == 0:
+                slots.extend(quantize_slots(late_bf, "late", at(first_at, [P, late * C], U32, "late_codes")))
+            if e < LAST:
+                low = at(first_at, half, BF16, f"w1_bf{e + 1}_0") if e else kept(half, BF16, "w1_bf1_0")
+                w1_bf = [low, kept(half, BF16, f"w1_bf{e + 1}_1", f"w3_raw{e}")]
+                round_half(nc.vector.tensor_copy if e else nc.scalar.copy, w1_bf[0], w1_raw[e + 1], 0)
                 round_half(nc.scalar.copy, w1_bf[1], w1_raw[e + 1], 1)
-            for i, (f, b, bank) in enumerate(now):
-                scatter_on_scalar(f, b, region[:, i, :])
-            w2_bf = kept([P, N, PACK], BF16, f"w2_bf{e}", spent if e == LAST else (f"acts{e}_0" if e else ""))
+            w2_bf = at(first_at if e == LAST else second_at + Y_BYTES, [P, N, PACK], BF16, f"w2_bf{e}")
+            gpsimd_copy(out=w2_bf[:], in_=w2_raw[e][:].rearrange("p j c -> p c j"))
             if e == LAST:
-                gpsimd_copy(out=w2_bf[:], in_=w2_raw[e][:].rearrange("p j c -> p c j"))
-            h_bf = kept([P, C, PACK], BF16, f"h_bf{e}")
+                release(sorted(waiting, key=lambda item: item[1]), kept([P, 3, C], F32, "late_y", f"acts{e - 1}_0"))
+            elif e:
+                release(waiting[:1], at(second_at, [P, 1, C], F32, f"first_y{e}"))
+            h_bf = at(second_at + REGION, [P, C, PACK], BF16, f"h_bf{e}")
             for s, bank in enumerate(w3_banks):
                 cols = slice(s * BANK_SLOTS, (s + 1) * BANK_SLOTS)
                 nc.vector.tensor_tensor(
                     out=h_bf[:, cols, :], in0=acts[s][:], in1=bank[:].rearrange("p t c -> p c t"), op=MULT
                 )
+            if 0 < e < LAST - 1:
+                release(waiting[:1], kept([P, 1, C], F32, f"second_y{e}", f"acts{e}_0"))
             if e < LAST:
-                interleave(nc.scalar.copy if e == 0 else nc.vector.tensor_copy, w2_bf[:], w2_raw[e][:])
-            if e < LAST:
-                w1_codes = quantize_half(f"w1_{e + 1}_0", w1_bf[0])
-                w1_codes = w1_codes + quantize_half(f"w1_{e + 1}_1", w1_bf[1], f"w1_raw{e + 1}")
+                high = quantize_half(f"w1_{e + 1}_1", w1_bf[1], kept([P, HALF * P], U32, f"w1_{e + 1}_hi", f"acts{e}_1"))
+                w1_codes = quantize_half(f"w1_{e + 1}_0", w1_bf[0], kept([P, HALF * P], U32, f"w1_{e + 1}_lo", f"w2_raw{e}")) + high
                 w1_banks = first_product("w1", w1_codes, slots[e + 1])
-            w2_words = kept([P, N], U32, f"w2_codes{e}", f"w3_raw{e}")
-            h_words = kept([P, C], U32, f"h_codes{e}", f"w2_raw{e}" if e == LAST else spent)
+            w2_words = kept([P, N], U32, f"w2_codes{e}", f"w3_raw{e}" if e == LAST else "")
+            if e == LAST:
+                h_words = kept([P, C], U32, f"h_codes{e}", f"w2_raw{e}")
+            elif e:
+                h_words = at(first_at, [P, C], U32, f"h_codes{e}")
+            else:
+                h_words = kept([P, C], U32, f"h_codes{e}", "w1_bf1_0")
             w2_scales, h_scales = kept([P, N], U8, f"w2_scales{e}"), kept([P, C], U8, f"h_scales{e}")
-            operands = [(h_words, h_scales, h_bf), (w2_words, w2_scales, w2_bf)]
-            for words, scales, values in operands[::-1] if e == LAST else operands:
-                quantize(words[:], scales[:], values[:].rearrange("p c t -> p (c t)"))
+            quantize(w2_words[:], w2_scales[:], w2_bf[:].rearrange("p c t -> p (c t)"))
+            quantize(h_words[:], h_scales[:], h_bf[:].rearrange("p c t -> p (c t)"))
             for b in range(BLOCKS):
                 bank = psum_y.tile([P, C], F32, name="y_bank")
                 nc.tensor.matmul_mx(

@@ -15,7 +15,6 @@ FP8X4 = mybir.dt.float8_e4m3fn_x4
 COPY = mybir.ActivationFunctionType.Copy
 SILU = mybir.ActivationFunctionType.Silu
 MULT = mybir.AluOpType.mult
-ADD = mybir.AluOpType.add
 
 P = 128
 PACK = 4
@@ -27,8 +26,8 @@ LIST_COLS = C // 16
 BLOCKS = N // P
 LAST = E - 1
 HALF_BYTES = HALF * P * PACK * 2
-Y_BYTES = C * 4
-REGION = HALF_BYTES + Y_BYTES
+RAW_BYTES = PACK * H * 4
+OWN = 32
 
 
 def tile_moe_two_glu_silu_kernel(tc, xT, w1, w3, w2, gate, offs, dst, out):
@@ -48,9 +47,6 @@ def tile_moe_two_glu_silu_kernel(tc, xT, w1, w3, w2, gate, offs, dst, out):
         def quantize(words, scales, values):
             nc.vector.quantize_mx(out=words.bitcast(FP8X4), scales=scales, in_=values)
 
-        def gpsimd_copy(out, in_):
-            nc.gpsimd.tensor_scalar(out=out, in0=in_, scalar1=1.0, scalar2=0.0, op0=MULT, op1=ADD)
-
         offs_sb = keep.tile([P, E * LIST_COLS], U16, name="offs_sb")
         dst_sb = keep.tile([P, E * LIST_COLS], U16, name="dst_sb")
         windows = [keep.tile([P, T], F32, name=f"window{b}") for b in range(BLOCKS)]
@@ -68,17 +64,18 @@ def tile_moe_two_glu_silu_kernel(tc, xT, w1, w3, w2, gate, offs, dst, out):
             if j == 0:
                 nc.sync.dma_start(offs_sb[:], offs)
 
-        def load(w, e, name):
-            raw = kept([P, PACK, w.shape[2]], F32, f"{name}_raw{e}")
-            nc.sync.dma_start(out=raw[:], in_=w[e].rearrange("(p j) n -> p j n", j=PACK))
-            return raw
+        def load(raw, w):
+            nc.sync.dma_start(out=raw[:], in_=w.rearrange("(p j) n -> p j n", j=PACK))
 
-        w1_raw, w3_raw, w2_raw = [load(w1, 0, "w1")], [], []
+        w1_raw = [kept([P, PACK, H], F32, f"w1_raw{e}") for e in range(E)]
+        w3_raw = [at(e * RAW_BYTES, [P, PACK, H], F32, f"w3_raw{e}") for e in range(E)]
+        w2_raw = [kept([P, PACK, N], F32, f"w2_raw{e}") for e in range(E)]
+        load(w1_raw[0], w1[0])
         for e in range(E):
-            w3_raw.append(load(w3, e, "w3"))
             if e < LAST:
-                w1_raw.append(load(w1, e + 1, "w1"))
-            w2_raw.append(load(w2, e, "w2"))
+                load(w1_raw[e + 1], w1[e + 1])
+            load(w3_raw[e], w3[e])
+            load(w2_raw[e], w2[e])
             if e == 0:
                 nc.sync.dma_start(dst_sb[:], dst)
 
@@ -139,7 +136,8 @@ def tile_moe_two_glu_silu_kernel(tc, xT, w1, w3, w2, gate, offs, dst, out):
             for s in range(C // BANK_SLOTS):
                 cols = slice(s * BANK_SLOTS, (s + 1) * BANK_SLOTS)
                 bank = psum.tile([P, PACK, BANK_SLOTS], F32, name=f"{name}_bank")
-                for t, (words, scales) in enumerate(by_t):
+                for t in sorted(range(PACK), key=lambda t: (t + s * HALF) % PACK):
+                    words, scales = by_t[t]
                     nc.tensor.matmul_mx(
                         out=bank[:, t, :],
                         lhsT=words.bitcast(FP8X4),
@@ -158,106 +156,136 @@ def tile_moe_two_glu_silu_kernel(tc, xT, w1, w3, w2, gate, offs, dst, out):
         def scatter_on_scalar(e, b, y):
             nc.scalar.activation(out=windows[b][:].indirect(entries(dst_sb, e)), in_=y, func=COPY)
 
-        def halves(name, e, behind=("", "")):
-            return [kept([P, HALF, P, PACK], BF16, f"{name}_bf{e}_{h}", behind[h]) for h in range(2)]
-
-        def round_shared(bf, raw, own):
-            round_half(nc.vector.tensor_copy, bf[0], raw, 0)
-            if own < P:
-                round_half(nc.scalar.copy, bf[1], raw, 1, slice(own, P))
-            if own:
-                round_half(nc.vector.tensor_copy, bf[1], raw, 1, slice(0, own))
-
-        interleave(nc.scalar.copy, late_bf[:], rows[:])
-        slots = quantize_slots(slot_bf[0], "slot0")
-        slots.extend(quantize_slots(slot_bf[1], "slot1"))
-        w1_bf = halves("w1", 0)
-        round_shared(w1_bf, w1_raw[0], P)
-        w1_codes = quantize_half("w1_0_0", w1_bf[0]) + quantize_half("w1_0_1", w1_bf[1])
-        w1_banks = first_product("w1", w1_codes, slots[0])
         half = [P, HALF, P, PACK]
-        waiting = []
+        vector, scalar = nc.vector.tensor_copy, nc.scalar.copy
 
-        def release(blocks, ys):
-            for i, (f, b, bank) in enumerate(blocks):
-                times_gate(f, ys[:, i, :], bank)
-            for i, (f, b, bank) in enumerate(blocks):
-                scatter_on_scalar(f, b, ys[:, i, :])
-                waiting.remove((f, b, bank))
+        def rounded(name, raw, copies, behind=("", "")):
+            tiles = [kept(half, BF16, f"{name}_bf{h}", behind[h]) for h in range(2)]
+            for h in range(2):
+                round_half(copies[h], tiles[h], raw, h)
+            return tiles
 
-        for e in range(E):
-            second_at = HALF_BYTES + e * REGION
-            first_at = second_at - HALF_BYTES
-            low = at(first_at, half, BF16, f"w3_bf{e}_0")
-            if e < LAST:
-                w3_bf = [low, at(second_at, half, BF16, f"w3_bf{e}_1")]
-            else:
-                w3_bf = [low, kept(half, BF16, f"w3_bf{e}_1", f"acts{e - 1}_0")]
-            round_half(nc.vector.tensor_copy, w3_bf[0], w3_raw[e], 0)
-            round_half(nc.scalar.copy if e == LAST else nc.vector.tensor_copy, w3_bf[1], w3_raw[e], 1)
+        def codes_tile(name, behind=""):
+            return kept([P, HALF * P], U32, name, behind)
+
+        def silu(e, banks, behind_w3=None):
             acts = []
-            for s, bank in enumerate(w1_banks):
-                act = kept([P, BANK_SLOTS, PACK], F32, f"acts{e}_{s}", f"w3_raw{e}" if s == 0 and e == LAST else "")
+            for s, bank in enumerate(banks):
+                shape = [P, BANK_SLOTS, PACK]
+                if behind_w3 is None:
+                    act = kept(shape, F32, f"acts{e}_{s}")
+                else:
+                    act = at(behind_w3 * RAW_BYTES + s * HALF_BYTES, shape, F32, f"acts{e}_{s}")
                 nc.scalar.activation(out=act[:], in_=bank[:].rearrange("p t c -> p c t"), func=SILU)
                 acts.append(act)
-            if e < LAST:
-                w3_codes = quantize_half(f"w3_{e}_0", w3_bf[0]) + quantize_half(f"w3_{e}_1", w3_bf[1])
-            else:
-                high = quantize_half(f"w3_{e}_1", w3_bf[1], at(second_at, [P, HALF * P], U32, "last_w3_codes"))
-                w3_codes = quantize_half(f"w3_{e}_0", w3_bf[0]) + high
-            w3_banks = first_product("w3", w3_codes, slots[e])
-            if e == 0:
-                slots.extend(quantize_slots(late_bf, "late", at(first_at, [P, late * C], U32, "late_codes")))
-            if e < LAST:
-                low = at(first_at, half, BF16, f"w1_bf{e + 1}_0") if e else kept(half, BF16, "w1_bf1_0")
-                w1_bf = [low, kept(half, BF16, f"w1_bf{e + 1}_1", f"w3_raw{e}")]
-                round_half(nc.vector.tensor_copy if e else nc.scalar.copy, w1_bf[0], w1_raw[e + 1], 0)
-                round_half(nc.scalar.copy, w1_bf[1], w1_raw[e + 1], 1)
-            w2_bf = at(first_at if e == LAST else second_at + Y_BYTES, [P, N, PACK], BF16, f"w2_bf{e}")
-            gpsimd_copy(out=w2_bf[:], in_=w2_raw[e][:].rearrange("p j c -> p c j"))
-            if e == LAST:
-                release(sorted(waiting, key=lambda item: item[1]), kept([P, 3, C], F32, "late_y", f"acts{e - 1}_0"))
-            elif e:
-                release(waiting[:1], at(second_at, [P, 1, C], F32, f"first_y{e}"))
-            h_bf = at(second_at + REGION, [P, C, PACK], BF16, f"h_bf{e}")
-            for s, bank in enumerate(w3_banks):
-                cols = slice(s * BANK_SLOTS, (s + 1) * BANK_SLOTS)
-                nc.vector.tensor_tensor(
-                    out=h_bf[:, cols, :], in0=acts[s][:], in1=bank[:].rearrange("p t c -> p c t"), op=MULT
-                )
-            if 0 < e < LAST - 1:
-                release(waiting[:1], kept([P, 1, C], F32, f"second_y{e}", f"acts{e}_0"))
-            if e < LAST:
-                high = quantize_half(f"w1_{e + 1}_1", w1_bf[1], kept([P, HALF * P], U32, f"w1_{e + 1}_hi", f"acts{e}_1"))
-                w1_codes = quantize_half(f"w1_{e + 1}_0", w1_bf[0], kept([P, HALF * P], U32, f"w1_{e + 1}_lo", f"w2_raw{e}")) + high
-                w1_banks = first_product("w1", w1_codes, slots[e + 1])
-            w2_words = kept([P, N], U32, f"w2_codes{e}", f"w3_raw{e}" if e == LAST else "")
-            if e == LAST:
-                h_words = kept([P, C], U32, f"h_codes{e}", f"w2_raw{e}")
-            elif e:
-                h_words = at(first_at, [P, C], U32, f"h_codes{e}")
-            else:
-                h_words = kept([P, C], U32, f"h_codes{e}", "w1_bf1_0")
-            w2_scales, h_scales = kept([P, N], U8, f"w2_scales{e}"), kept([P, C], U8, f"h_scales{e}")
-            quantize(w2_words[:], w2_scales[:], w2_bf[:].rearrange("p c t -> p (c t)"))
-            quantize(h_words[:], h_scales[:], h_bf[:].rearrange("p c t -> p (c t)"))
+            return acts
+
+        def multiply(h_bf, s, acts, banks):
+            cols = slice(s * BANK_SLOTS, (s + 1) * BANK_SLOTS)
+            nc.vector.tensor_tensor(
+                out=h_bf[:, cols, :], in0=acts[s][:], in1=banks[s][:].rearrange("p t c -> p c t"), op=MULT
+            )
+
+        def quantize_whole(name, values, words):
+            scales = kept([P, C], U8, f"{name}_scales")
+            quantize(words[:], scales[:], values[:].rearrange("p c t -> p (c t)"))
+            return words, scales
+
+        def second_product(w2_codes, h_codes):
+            banks = []
             for b in range(BLOCKS):
                 bank = psum_y.tile([P, C], F32, name="y_bank")
                 nc.tensor.matmul_mx(
                     out=bank[:],
-                    lhsT=w2_words[:, b * P:(b + 1) * P].bitcast(FP8X4),
-                    lhsT_scale=w2_scales[:, b * P:(b + 1) * P],
-                    rhs=h_words[:].bitcast(FP8X4),
-                    rhs_scale=h_scales[:],
+                    lhsT=w2_codes[0][:, b * P:(b + 1) * P].bitcast(FP8X4),
+                    lhsT_scale=w2_codes[1][:, b * P:(b + 1) * P],
+                    rhs=h_codes[0][:].bitcast(FP8X4),
+                    rhs_scale=h_codes[1][:],
                     start=True,
                     stop=True,
                 )
-                waiting.append((e, b, bank))
+                banks.append(bank)
+            return banks
 
-        last_y = kept([P, BLOCKS, C], F32, "last_y")
-        for f, b, bank in waiting:
-            times_gate(f, last_y[:, b, :], bank)
-        nc.vector.tensor_copy(out=windows[0][:].indirect(entries(dst_sb, LAST)), in_=last_y[:, 0, :])
+        def release(e, b, bank, y):
+            times_gate(e, y, bank)
+            scatter_on_scalar(e, b, y)
+
+        def y_tile(e, b, behind=""):
+            return kept([P, C], F32, f"y{e}_{b}", behind)
+
+        wide = [P, N, PACK]
+        interleave(nc.scalar.copy, late_bf[:], rows[:])
+        slots = quantize_slots(slot_bf[0], "slot0")
+        slots.extend(quantize_slots(slot_bf[1], "slot1"))
+        w1_bf = rounded("w1_0", w1_raw[0], (vector, vector))
+        acts0 = silu(0, first_product("w1", quantize_half("w1_0_0", w1_bf[0]) + quantize_half("w1_0_1", w1_bf[1]), slots[0]))
+        slots.extend(quantize_slots(late_bf, "late"))
+        w1_bf = rounded("w1_1", w1_raw[1], (vector, vector))
+        w1_banks = first_product("w1", quantize_half("w1_1_0", w1_bf[0]) + quantize_half("w1_1_1", w1_bf[1]), slots[1])
+
+        def in_w3(e, at_half, shape, dtype, name):
+            return at(e * RAW_BYTES + at_half * HALF_BYTES, shape, dtype, name)
+
+        def round_w3(e, own):
+            tiles = [kept(half, BF16, f"w3_{e}_bf{h}") for h in range(2)]
+            round_half(vector, tiles[0], w3_raw[e], 0)
+            if own < P:
+                round_half(scalar, tiles[1], w3_raw[e], 1, slice(own, P))
+            round_half(vector, tiles[1], w3_raw[e], 1, slice(0, own))
+            return tiles
+
+        def w3_product(e, tiles):
+            codes = quantize_half(f"w3_{e}_0", tiles[0]) + quantize_half(f"w3_{e}_1", tiles[1])
+            return first_product("w3", codes, slots[e])
+
+        def late_w1_product(e, tiles):
+            words = in_w3(e - 1, 3, [P, 2, HALF * P], U32, f"w1_{e}_codes")
+            codes = [pair for h in range(2) for pair in quantize_half(f"w1_{e}_{h}", tiles[h], words[:, h, :])]
+            return first_product("w1", codes, slots[e])
+
+        def second_layer(e, acts, banks, w2_bf, w2_words):
+            h_bf = kept(wide, BF16, f"h_bf{e}")
+            for s in range(2):
+                multiply(h_bf, s, acts, banks)
+            w2_codes = quantize_whole(f"w2_{e}", w2_bf, w2_words)
+            return second_product(w2_codes, quantize_whole(f"h_{e}", h_bf, codes_tile(f"h_codes{e}")))
+
+        def round_w2(e, copy, behind):
+            w2_bf = kept(wide, BF16, f"w2_bf{e}", behind)
+            interleave(copy, w2_bf[:], w2_raw[e][:])
+            return w2_bf
+
+        w3_bf = round_w3(0, OWN)
+        acts1 = silu(1, w1_banks, 0)
+        banks = w3_product(0, w3_bf)
+        y0 = second_layer(0, acts0, banks, round_w2(0, vector, "w3_0_bf1"), codes_tile("w2_codes0", "acts0_0"))
+        w1_bf = rounded("w1_2", w1_raw[2], (vector, scalar), ("w3_0_bf1", ""))
+        for b in range(BLOCKS):
+            release(0, b, y0[b], y_tile(0, b)[:])
+        w1_banks = first_product("w1", quantize_half("w1_2_0", w1_bf[0]) + quantize_half("w1_2_1", w1_bf[1]), slots[2])
+        banks = w3_product(1, round_w3(1, P))
+        acts2 = silu(2, w1_banks, 1)
+        y1 = second_layer(1, acts1, banks, round_w2(1, vector, "w3_1_bf1"), in_w3(0, 0, [P, N], U32, "w2_codes1"))
+        w1_bf = rounded("w1_3", w1_raw[3], (vector, scalar), ("w3_1_bf1", ""))
+        w3_bf = round_w3(2, OWN)
+        banks = w3_product(2, w3_bf)
+        w2_bf = round_w2(2, scalar, "")
+        release(1, 0, y1[0], in_w3(2, 2, [P, C], F32, "y1_0")[:])
+        w1_banks = late_w1_product(3, w1_bf)
+        y2 = second_layer(2, acts2, banks, w2_bf, in_w3(1, 0, [P, N], U32, "w2_codes2"))
+        w3_bf = round_w3(3, OWN)
+        acts3 = silu(3, w1_banks, 3)
+        banks = w3_product(3, w3_bf)
+        ys = in_w3(3, 2, [P, 2, C], F32, "ys3")
+        release(2, 0, y2[0], ys[:, 0, :])
+        release(1, 1, y1[1], ys[:, 1, :])
+        y3 = second_layer(3, acts3, banks, round_w2(3, vector, "w3_3_bf1"), in_w3(3, 0, [P, N], U32, "w2_codes3"))
+        release(2, 1, y2[1], y_tile(2, 1, "w3_3_bf1")[:])
+        last_y = [y_tile(LAST, b) for b in range(BLOCKS)]
+        for b in range(BLOCKS):
+            times_gate(LAST, last_y[b][:], y3[b])
+        nc.vector.tensor_copy(out=windows[0][:].indirect(entries(dst_sb, LAST)), in_=last_y[0][:])
         nc.sync.dma_start(out=out[:P, :], in_=windows[0][:])
-        scatter_on_scalar(LAST, 1, last_y[:, 1, :])
+        scatter_on_scalar(LAST, 1, last_y[1][:])
         nc.sync.dma_start(out=out[P:, :], in_=windows[1][:])

@@ -15,6 +15,7 @@ FP8X4 = mybir.dt.float8_e4m3fn_x4
 COPY = mybir.ActivationFunctionType.Copy
 SILU = mybir.ActivationFunctionType.Silu
 MULT = mybir.AluOpType.mult
+ADD = mybir.AluOpType.add
 
 P = 128
 PACK = 4
@@ -256,6 +257,13 @@ def tile_moe_two_glu_silu_kernel(tc, xT, w1, w3, w2, gate, offs, dst, out):
             interleave(copy, w2_bf[:], w2_raw[e][:])
             return w2_bf
 
+        def round_w2_on_gpsimd(e, behind):
+            w2_bf = kept(wide, BF16, f"w2_bf{e}", behind)
+            nc.gpsimd.tensor_scalar(
+                out=w2_bf[:], in0=w2_raw[e][:].rearrange("p j c -> p c j"), scalar1=1.0, scalar2=0.0, op0=MULT, op1=ADD
+            )
+            return w2_bf
+
         w3_bf = round_w3(0, OWN)
         acts1 = silu(1, w1_banks, 0)
         banks = w3_product(0, w3_bf)
@@ -280,7 +288,7 @@ def tile_moe_two_glu_silu_kernel(tc, xT, w1, w3, w2, gate, offs, dst, out):
         ys = in_w3(3, 2, [P, 2, C], F32, "ys3")
         release(2, 0, y2[0], ys[:, 0, :])
         release(1, 1, y1[1], ys[:, 1, :])
-        y3 = second_layer(3, acts3, banks, round_w2(3, vector, "w3_3_bf1"), in_w3(3, 0, [P, N], U32, "w2_codes3"))
+        y3 = second_layer(3, acts3, banks, round_w2_on_gpsimd(3, "w3_3_bf1"), in_w3(3, 0, [P, N], U32, "w2_codes3"))
         release(2, 1, y2[1], y_tile(2, 1, "w3_3_bf1")[:])
         last_y = [y_tile(LAST, b) for b in range(BLOCKS)]
         for b in range(BLOCKS):

@@ -22,13 +22,15 @@ PACK = 4
 HALF = PACK // 2
 EARLY = 2
 BANK_SLOTS = 128
+BANKS = C // BANK_SLOTS
 GATE_COLS = E * C // P
 LIST_COLS = C // 16
 BLOCKS = N // P
 LAST = E - 1
-HALF_BYTES = HALF * P * PACK * 2
-RAW_BYTES = PACK * H * 4
-OWN = 32
+VECTOR_PLACES = 16
+
+W3_BYTES = PACK * H * 4
+QUARTER = W3_BYTES // 4
 
 
 def tile_moe_two_glu_silu_kernel(tc, xT, w1, w3, w2, gate, offs, dst, out):
@@ -36,14 +38,14 @@ def tile_moe_two_glu_silu_kernel(tc, xT, w1, w3, w2, gate, offs, dst, out):
     with ExitStack() as ctx:
         keep = ctx.enter_context(tc.tile_pool(name="keep", bufs=1))
         placed = ctx.enter_context(tc.tile_pool(name="placed", bufs=1))
-        psum = ctx.enter_context(tc.psum_pool(name="psum", bufs=2))
-        psum_y = ctx.enter_context(tc.psum_pool(name="psum_y", bufs=4))
+        psum = ctx.enter_context(tc.psum_pool(name="psum", bufs=BANKS))
+        psum_y = ctx.enter_context(tc.psum_pool(name="psum_y", bufs=2 * BLOCKS))
 
         def kept(shape, dtype, name, behind=""):
             return keep.tile(shape, dtype, name=name, tag=behind or name, align_bytes=64)
 
-        def at(offset, shape, dtype, name):
-            return placed.tile(shape, dtype, name=name, align_bytes=64, offset=offset)
+        def in_w3(e, quarter, shape, dtype, name):
+            return placed.tile(shape, dtype, name=name, align_bytes=64, offset=e * W3_BYTES + quarter * QUARTER)
 
         def quantize(words, scales, values):
             nc.vector.quantize_mx(out=words.bitcast(FP8X4), scales=scales, in_=values)
@@ -69,7 +71,7 @@ def tile_moe_two_glu_silu_kernel(tc, xT, w1, w3, w2, gate, offs, dst, out):
             nc.sync.dma_start(out=raw[:], in_=w.rearrange("(p j) n -> p j n", j=PACK))
 
         w1_raw = [kept([P, PACK, H], F32, f"w1_raw{e}") for e in range(E)]
-        w3_raw = [at(e * RAW_BYTES, [P, PACK, H], F32, f"w3_raw{e}") for e in range(E)]
+        w3_raw = [in_w3(e, 0, [P, PACK, H], F32, f"w3_raw{e}") for e in range(E)]
         w2_raw = [kept([P, PACK, N], F32, f"w2_raw{e}") for e in range(E)]
         load(w1_raw[0], w1[0])
         for e in range(E):
@@ -105,39 +107,66 @@ def tile_moe_two_glu_silu_kernel(tc, xT, w1, w3, w2, gate, offs, dst, out):
                 out=rows[:, j, :], in_=x_planes[j][:].indirect(entries(offs_sb, EARLY, late)), func=COPY
             )
 
+        on_vector, on_scalar = nc.vector.tensor_copy, nc.scalar.copy
+        half = [P, HALF, P, PACK]
+
         def interleave(copy, side_by_side, planes):
             copy(
                 out=side_by_side.rearrange("p (c i) j -> p c j i", i=PACK),
                 in_=planes.rearrange("p j (c i) -> p c j i", i=PACK),
             )
 
-        late_bf = kept([P, late * C, PACK], BF16, "late_bf")
-
-        def quantize_slots(values, name, words=None):
+        def quantize_columns(name, values, words=None):
             width = values.shape[1]
-            words, scales = words if words is not None else kept([P, width], U32, f"{name}_codes"), kept([P, width], U8, f"{name}_scales")
+            if words is None:
+                words = kept([P, width], U32, f"{name}_codes")
+            scales = kept([P, width], U8, f"{name}_scales")
             quantize(words[:], scales[:], values[:].rearrange("p c j -> p (c j)"))
-            return [(words[:, c:c + C], scales[:, c:c + C]) for c in range(0, width, C)]
+            return words, scales
 
-        def round_half(copy, bf, raw, h, cols=slice(0, P)):
+        def by_expert(codes):
+            words, scales = codes
+            return [(words[:, c:c + C], scales[:, c:c + C]) for c in range(0, words.shape[1], C)]
+
+        def round_half(copy, bf, raw, h, places=slice(0, P)):
             copy(
-                out=bf[:].rearrange("p t m j -> p m j t")[:, cols],
-                in_=raw[:].rearrange("p j (m t) -> p m j t", t=PACK)[:, cols, :, h * HALF:(h + 1) * HALF],
+                out=bf[:].rearrange("p t m j -> p m j t")[:, places],
+                in_=raw[:].rearrange("p j (m t) -> p m j t", t=PACK)[:, places, :, h * HALF:(h + 1) * HALF],
             )
 
-        def quantize_half(name, bf, words=None):
-            words = words if words is not None else kept([P, HALF * P], U32, f"{name}_codes")
-            scales = kept([P, HALF * P], U8, f"{name}_scales")
-            quantize(words[:], scales[:], bf[:].rearrange("p t m j -> p (t m j)"))
-            return [(words[:, c:c + P], scales[:, c:c + P]) for c in range(0, HALF * P, P)]
+        def round_w1(e, high_copy, low_behind=""):
+            halves = [kept(half, BF16, f"w1_bf{e}_0", low_behind), kept(half, BF16, f"w1_bf{e}_1")]
+            round_half(on_vector, halves[0], w1_raw[e], 0)
+            round_half(high_copy, halves[1], w1_raw[e], 1)
+            return halves
 
-        def first_product(name, by_t, slot_codes):
-            slot_words, slot_scales = slot_codes
+        def round_w3(e, vector_places):
+            halves = [kept(half, BF16, f"w3_bf{e}_{h}") for h in range(2)]
+            round_half(on_vector, halves[0], w3_raw[e], 0)
+            if vector_places < P:
+                round_half(on_scalar, halves[1], w3_raw[e], 1, slice(vector_places, P))
+            round_half(on_vector, halves[1], w3_raw[e], 1, slice(0, vector_places))
+            return halves
+
+        def round_w2(e, copy, behind=""):
+            w2_bf = kept([P, N, PACK], BF16, f"w2_bf{e}", behind)
+            interleave(copy, w2_bf[:], w2_raw[e][:])
+            return w2_bf
+
+        def first_product(name, e, halves, words_at=None):
+            by_t = []
+            for h, bf in enumerate(halves):
+                words = kept([P, HALF * P], U32, f"{name}_codes{e}_{h}") if words_at is None else words_at[:, h, :]
+                scales = kept([P, HALF * P], U8, f"{name}_scales{e}_{h}")
+                quantize(words[:], scales[:], bf[:].rearrange("p t m j -> p (t m j)"))
+                by_t.extend((words[:, c:c + P], scales[:, c:c + P]) for c in range(0, HALF * P, P))
+            slot_words, slot_scales = slots[e]
             banks = []
-            for s in range(C // BANK_SLOTS):
+            for s in range(BANKS):
                 cols = slice(s * BANK_SLOTS, (s + 1) * BANK_SLOTS)
                 bank = psum.tile([P, PACK, BANK_SLOTS], F32, name=f"{name}_bank")
-                for t in sorted(range(PACK), key=lambda t: (t + s * HALF) % PACK):
+                for step in range(PACK):
+                    t = (step + s * HALF) % PACK
                     words, scales = by_t[t]
                     nc.tensor.matmul_mx(
                         out=bank[:, t, :],
@@ -151,146 +180,92 @@ def tile_moe_two_glu_silu_kernel(tc, xT, w1, w3, w2, gate, offs, dst, out):
                 banks.append(bank)
             return banks
 
+        def silu(e, banks, behind_w3=None):
+            acts = []
+            for s, bank in enumerate(banks):
+                shape, name = [P, BANK_SLOTS, PACK], f"acts{e}_{s}"
+                act = kept(shape, F32, name) if behind_w3 is None else in_w3(behind_w3, s, shape, F32, name)
+                nc.scalar.activation(out=act[:], in_=bank[:].rearrange("p t c -> p c t"), func=SILU)
+                acts.append(act)
+            return acts
+
+        def second_layer(e, acts, banks, w2_bf, w2_words):
+            h_bf = kept([P, C, PACK], BF16, f"h_bf{e}")
+            for s, bank in enumerate(banks):
+                cols = slice(s * BANK_SLOTS, (s + 1) * BANK_SLOTS)
+                nc.vector.tensor_tensor(
+                    out=h_bf[:, cols, :], in0=acts[s][:], in1=bank[:].rearrange("p t c -> p c t"), op=MULT
+                )
+            w2_words, w2_scales = quantize_columns(f"w2_{e}", w2_bf, w2_words)
+            h_words, h_scales = quantize_columns(f"h_{e}", h_bf)
+            y_banks = []
+            for b in range(BLOCKS):
+                bank = psum_y.tile([P, C], F32, name="y_bank")
+                nc.tensor.matmul_mx(
+                    out=bank[:],
+                    lhsT=w2_words[:, b * P:(b + 1) * P].bitcast(FP8X4),
+                    lhsT_scale=w2_scales[:, b * P:(b + 1) * P],
+                    rhs=h_words[:].bitcast(FP8X4),
+                    rhs_scale=h_scales[:],
+                    start=True,
+                    stop=True,
+                )
+                y_banks.append(bank)
+            return y_banks
+
         def times_gate(e, y, bank):
             nc.vector.tensor_tensor(out=y, in0=gates[:, e * C:(e + 1) * C], in1=bank[:], op=MULT)
 
         def scatter_on_scalar(e, b, y):
             nc.scalar.activation(out=windows[b][:].indirect(entries(dst_sb, e)), in_=y, func=COPY)
 
-        half = [P, HALF, P, PACK]
-        vector, scalar = nc.vector.tensor_copy, nc.scalar.copy
-
-        def rounded(name, raw, copies, behind=("", "")):
-            tiles = [kept(half, BF16, f"{name}_bf{h}", behind[h]) for h in range(2)]
-            for h in range(2):
-                round_half(copies[h], tiles[h], raw, h)
-            return tiles
-
-        def codes_tile(name, behind=""):
-            return kept([P, HALF * P], U32, name, behind)
-
-        def silu(e, banks, behind_w3=None):
-            acts = []
-            for s, bank in enumerate(banks):
-                shape = [P, BANK_SLOTS, PACK]
-                if behind_w3 is None:
-                    act = kept(shape, F32, f"acts{e}_{s}")
-                else:
-                    act = at(behind_w3 * RAW_BYTES + s * HALF_BYTES, shape, F32, f"acts{e}_{s}")
-                nc.scalar.activation(out=act[:], in_=bank[:].rearrange("p t c -> p c t"), func=SILU)
-                acts.append(act)
-            return acts
-
-        def multiply(h_bf, s, acts, banks):
-            cols = slice(s * BANK_SLOTS, (s + 1) * BANK_SLOTS)
-            nc.vector.tensor_tensor(
-                out=h_bf[:, cols, :], in0=acts[s][:], in1=banks[s][:].rearrange("p t c -> p c t"), op=MULT
-            )
-
-        def quantize_whole(name, values, words):
-            scales = kept([P, C], U8, f"{name}_scales")
-            quantize(words[:], scales[:], values[:].rearrange("p c t -> p (c t)"))
-            return words, scales
-
-        def second_product(w2_codes, h_codes):
-            banks = []
-            for b in range(BLOCKS):
-                bank = psum_y.tile([P, C], F32, name="y_bank")
-                nc.tensor.matmul_mx(
-                    out=bank[:],
-                    lhsT=w2_codes[0][:, b * P:(b + 1) * P].bitcast(FP8X4),
-                    lhsT_scale=w2_codes[1][:, b * P:(b + 1) * P],
-                    rhs=h_codes[0][:].bitcast(FP8X4),
-                    rhs_scale=h_codes[1][:],
-                    start=True,
-                    stop=True,
-                )
-                banks.append(bank)
-            return banks
-
-        def release(e, b, bank, y):
+        def send(e, b, bank, y):
             times_gate(e, y, bank)
             scatter_on_scalar(e, b, y)
 
-        def y_tile(e, b, behind=""):
-            return kept([P, C], F32, f"y{e}_{b}", behind)
+        late_bf = kept([P, late * C, PACK], BF16, "late_bf")
+        interleave(on_scalar, late_bf[:], rows[:])
+        slots = [pair for e in range(EARLY) for pair in by_expert(quantize_columns(f"slot{e}", slot_bf[e]))]
+        acts0 = silu(0, first_product("w1", 0, round_w1(0, on_vector)))
+        slots.extend(by_expert(quantize_columns("late", late_bf)))
+        w1_banks = first_product("w1", 1, round_w1(1, on_vector))
 
-        wide = [P, N, PACK]
-        interleave(nc.scalar.copy, late_bf[:], rows[:])
-        slots = quantize_slots(slot_bf[0], "slot0")
-        slots.extend(quantize_slots(slot_bf[1], "slot1"))
-        w1_bf = rounded("w1_0", w1_raw[0], (vector, vector))
-        acts0 = silu(0, first_product("w1", quantize_half("w1_0_0", w1_bf[0]) + quantize_half("w1_0_1", w1_bf[1]), slots[0]))
-        slots.extend(quantize_slots(late_bf, "late"))
-        w1_bf = rounded("w1_1", w1_raw[1], (vector, vector))
-        w1_banks = first_product("w1", quantize_half("w1_1_0", w1_bf[0]) + quantize_half("w1_1_1", w1_bf[1]), slots[1])
-
-        def in_w3(e, at_half, shape, dtype, name):
-            return at(e * RAW_BYTES + at_half * HALF_BYTES, shape, dtype, name)
-
-        def round_w3(e, own):
-            tiles = [kept(half, BF16, f"w3_{e}_bf{h}") for h in range(2)]
-            round_half(vector, tiles[0], w3_raw[e], 0)
-            if own < P:
-                round_half(scalar, tiles[1], w3_raw[e], 1, slice(own, P))
-            round_half(vector, tiles[1], w3_raw[e], 1, slice(0, own))
-            return tiles
-
-        def w3_product(e, tiles):
-            codes = quantize_half(f"w3_{e}_0", tiles[0]) + quantize_half(f"w3_{e}_1", tiles[1])
-            return first_product("w3", codes, slots[e])
-
-        def late_w1_product(e, tiles):
-            words = in_w3(e - 1, 3, [P, 2, HALF * P], U32, f"w1_{e}_codes")
-            codes = [pair for h in range(2) for pair in quantize_half(f"w1_{e}_{h}", tiles[h], words[:, h, :])]
-            return first_product("w1", codes, slots[e])
-
-        def second_layer(e, acts, banks, w2_bf, w2_words):
-            h_bf = kept(wide, BF16, f"h_bf{e}")
-            for s in range(2):
-                multiply(h_bf, s, acts, banks)
-            w2_codes = quantize_whole(f"w2_{e}", w2_bf, w2_words)
-            return second_product(w2_codes, quantize_whole(f"h_{e}", h_bf, codes_tile(f"h_codes{e}")))
-
-        def round_w2(e, copy, behind):
-            w2_bf = kept(wide, BF16, f"w2_bf{e}", behind)
-            interleave(copy, w2_bf[:], w2_raw[e][:])
-            return w2_bf
-
-        def round_w2_on_gpsimd(e, behind):
-            w2_bf = kept(wide, BF16, f"w2_bf{e}", behind)
-            nc.gpsimd.tensor_scalar(
-                out=w2_bf[:], in0=w2_raw[e][:].rearrange("p j c -> p c j"), scalar1=1.0, scalar2=0.0, op0=MULT, op1=ADD
-            )
-            return w2_bf
-
-        w3_bf = round_w3(0, OWN)
+        w3_bf = round_w3(0, VECTOR_PLACES)
         acts1 = silu(1, w1_banks, 0)
-        banks = w3_product(0, w3_bf)
-        y0 = second_layer(0, acts0, banks, round_w2(0, vector, "w3_0_bf1"), codes_tile("w2_codes0", "acts0_0"))
-        w1_bf = rounded("w1_2", w1_raw[2], (vector, scalar), ("w3_0_bf1", ""))
+        banks = first_product("w3", 0, w3_bf)
+        w2_bf = round_w2(0, on_vector, "w3_bf0_1")
+        y0 = second_layer(0, acts0, banks, w2_bf, kept([P, N], U32, "w2_codes0", "acts0_0"))
+        w1_bf = round_w1(2, on_scalar, "w3_bf0_1")
         for b in range(BLOCKS):
-            release(0, b, y0[b], y_tile(0, b)[:])
-        w1_banks = first_product("w1", quantize_half("w1_2_0", w1_bf[0]) + quantize_half("w1_2_1", w1_bf[1]), slots[2])
-        banks = w3_product(1, round_w3(1, P))
+            send(0, b, y0[b], kept([P, C], F32, f"y0_{b}")[:])
+        w1_banks = first_product("w1", 2, w1_bf)
+
+        banks = first_product("w3", 1, round_w3(1, P))
         acts2 = silu(2, w1_banks, 1)
-        y1 = second_layer(1, acts1, banks, round_w2(1, vector, "w3_1_bf1"), in_w3(0, 0, [P, N], U32, "w2_codes1"))
-        w1_bf = rounded("w1_3", w1_raw[3], (vector, scalar), ("w3_1_bf1", ""))
-        w3_bf = round_w3(2, OWN)
-        banks = w3_product(2, w3_bf)
-        w2_bf = round_w2(2, scalar, "")
-        release(1, 0, y1[0], in_w3(2, 2, [P, C], F32, "y1_0")[:])
-        w1_banks = late_w1_product(3, w1_bf)
+        w2_bf = round_w2(1, on_vector, "w3_bf1_1")
+        y1 = second_layer(1, acts1, banks, w2_bf, in_w3(0, 0, [P, N], U32, "w2_codes1"))
+        w1_bf = round_w1(3, on_scalar, "w3_bf1_1")
+
+        banks = first_product("w3", 2, round_w3(2, VECTOR_PLACES))
+        w2_bf = round_w2(2, on_scalar)
+        send(1, 0, y1[0], in_w3(2, 2, [P, C], F32, "y1_0")[:])
+        w1_banks = first_product("w1", 3, w1_bf, in_w3(2, 3, [P, 2, HALF * P], U32, "w1_codes3"))
         y2 = second_layer(2, acts2, banks, w2_bf, in_w3(1, 0, [P, N], U32, "w2_codes2"))
-        w3_bf = round_w3(3, OWN)
-        acts3 = silu(3, w1_banks, 3)
-        banks = w3_product(3, w3_bf)
-        ys = in_w3(3, 2, [P, 2, C], F32, "ys3")
-        release(2, 0, y2[0], ys[:, 0, :])
-        release(1, 1, y1[1], ys[:, 1, :])
-        y3 = second_layer(3, acts3, banks, round_w2_on_gpsimd(3, "w3_3_bf1"), in_w3(3, 0, [P, N], U32, "w2_codes3"))
-        release(2, 1, y2[1], y_tile(2, 1, "w3_3_bf1")[:])
-        last_y = [y_tile(LAST, b) for b in range(BLOCKS)]
+
+        w3_bf = round_w3(LAST, VECTOR_PLACES)
+        acts3 = silu(LAST, w1_banks, LAST)
+        banks = first_product("w3", LAST, w3_bf)
+        waiting = in_w3(LAST, 2, [P, 2, C], F32, "waiting_y")
+        send(2, 0, y2[0], waiting[:, 0, :])
+        send(1, 1, y1[1], waiting[:, 1, :])
+        w2_bf = kept([P, N, PACK], BF16, "w2_bf3", "w3_bf3_1")
+        nc.gpsimd.tensor_scalar(
+            out=w2_bf[:], in0=w2_raw[LAST][:].rearrange("p j c -> p c j"), scalar1=1.0, scalar2=0.0, op0=MULT, op1=ADD
+        )
+        y3 = second_layer(LAST, acts3, banks, w2_bf, in_w3(LAST, 0, [P, N], U32, "w2_codes3"))
+        send(2, 1, y2[1], kept([P, C], F32, "y2_1", "w3_bf3_1")[:])
+
+        last_y = [kept([P, C], F32, f"y3_{b}") for b in range(BLOCKS)]
         for b in range(BLOCKS):
             times_gate(LAST, last_y[b][:], y3[b])
         nc.vector.tensor_copy(out=windows[0][:].indirect(entries(dst_sb, LAST)), in_=last_y[0][:])

@@ -28,6 +28,7 @@ LIST_COLS = C // 16
 BLOCKS = N // P
 LAST = E - 1
 VECTOR_PLACES = 16
+CUT = C + (E - 1) * C // 2
 
 W3_BYTES = PACK * H * 4
 QUARTER = W3_BYTES // 4
@@ -153,7 +154,7 @@ def tile_moe_two_glu_silu_kernel(tc, xT, w1, w3, w2, gate, offs, dst, out):
             interleave(copy, w2_bf[:], w2_raw[e][:])
             return w2_bf
 
-        def first_product(name, e, halves, words_at=None):
+        def first_product(name, e, halves, words_at=None, banks_of=""):
             by_t = []
             for h, bf in enumerate(halves):
                 words = kept([P, HALF * P], U32, f"{name}_codes{e}_{h}") if words_at is None else words_at[:, h, :]
@@ -164,7 +165,7 @@ def tile_moe_two_glu_silu_kernel(tc, xT, w1, w3, w2, gate, offs, dst, out):
             banks = []
             for s in range(BANKS):
                 cols = slice(s * BANK_SLOTS, (s + 1) * BANK_SLOTS)
-                bank = psum.tile([P, PACK, BANK_SLOTS], F32, name=f"{name}_bank")
+                bank = psum.tile([P, PACK, BANK_SLOTS], F32, name=f"{banks_of or name}_bank")
                 for step in range(PACK):
                     t = (step + s * HALF) % PACK
                     words, scales = by_t[t]
@@ -213,15 +214,19 @@ def tile_moe_two_glu_silu_kernel(tc, xT, w1, w3, w2, gate, offs, dst, out):
                 y_banks.append(bank)
             return y_banks
 
-        def times_gate(e, y, bank):
-            nc.vector.tensor_tensor(out=y, in0=gates[:, e * C:(e + 1) * C], in1=bank[:], op=MULT)
+        def times_gate(first, end, y, sums):
+            nc.vector.tensor_tensor(out=y, in0=gates[:, first:end], in1=sums, op=MULT)
 
         def scatter_on_scalar(e, b, y):
             nc.scalar.activation(out=windows[b][:].indirect(entries(dst_sb, e)), in_=y, func=COPY)
 
         def send(e, b, bank, y):
-            times_gate(e, y, bank)
+            times_gate(e * C, (e + 1) * C, y, bank[:])
             scatter_on_scalar(e, b, y)
+
+        def scatter_second_window(first, end, y):
+            offsets = dst_sb[:, first * LIST_COLS // C:end * LIST_COLS // C]
+            nc.scalar.activation(out=windows[1][:].indirect(offsets), in_=y, func=COPY)
 
         late_bf = kept([P, late * C, PACK], BF16, "late_bf")
         interleave(on_scalar, late_bf[:], rows[:])
@@ -249,26 +254,29 @@ def tile_moe_two_glu_silu_kernel(tc, xT, w1, w3, w2, gate, offs, dst, out):
         banks = first_product("w3", 2, round_w3(2, VECTOR_PLACES))
         w2_bf = round_w2(2, on_scalar)
         send(1, 0, y1[0], in_w3(2, 2, [P, C], F32, "y1_0")[:])
-        w1_banks = first_product("w1", 3, w1_bf, in_w3(2, 3, [P, 2, HALF * P], U32, "w1_codes3"))
+        w1_banks = first_product("w1", 3, w1_bf, in_w3(2, 3, [P, 2, HALF * P], U32, "w1_codes3"), "w3")
         y2 = second_layer(2, acts2, banks, w2_bf, in_w3(1, 0, [P, N], U32, "w2_codes2"))
 
         w3_bf = round_w3(LAST, VECTOR_PLACES)
         acts3 = silu(LAST, w1_banks, LAST)
-        banks = first_product("w3", LAST, w3_bf)
-        waiting = in_w3(LAST, 2, [P, 2, C], F32, "waiting_y")
-        send(2, 0, y2[0], waiting[:, 0, :])
-        send(1, 1, y1[1], waiting[:, 1, :])
+        banks = first_product("w3", LAST, w3_bf, None, "w1")
+        waiting = in_w3(LAST, 2, [P, CUT], F32, "waiting_y")
+        send(2, 0, y2[0], waiting[:, :C])
+        times_gate(C, 2 * C, waiting[:, C:2 * C], y1[1][:])
+        times_gate(2 * C, CUT, waiting[:, 2 * C:CUT], y2[1][:, :C // 2])
+        scatter_second_window(C, CUT, waiting[:, C:])
         w2_bf = kept([P, N, PACK], BF16, "w2_bf3", "w3_bf3_1")
         nc.gpsimd.tensor_scalar(
             out=w2_bf[:], in0=w2_raw[LAST][:].rearrange("p j c -> p c j"), scalar1=1.0, scalar2=0.0, op0=MULT, op1=ADD
         )
         y3 = second_layer(LAST, acts3, banks, w2_bf, in_w3(LAST, 0, [P, N], U32, "w2_codes3"))
-        send(2, 1, y2[1], kept([P, C], F32, "y2_1", "w3_bf3_1")[:])
 
-        last_y = [kept([P, C], F32, f"y3_{b}") for b in range(BLOCKS)]
-        for b in range(BLOCKS):
-            times_gate(LAST, last_y[b][:], y3[b])
-        nc.vector.tensor_copy(out=windows[0][:].indirect(entries(dst_sb, LAST)), in_=last_y[0][:])
+        rest = kept([P, E * C - CUT], F32, "rest_y", "w3_bf3_1")
+        times_gate(CUT, LAST * C, rest[:, :C // 2], y2[1][:, C // 2:])
+        last_y = kept([P, C], F32, "y3_0")
+        times_gate(LAST * C, E * C, last_y[:], y3[0][:])
+        times_gate(LAST * C, E * C, rest[:, C // 2:], y3[1][:])
+        nc.vector.tensor_copy(out=windows[0][:].indirect(entries(dst_sb, LAST)), in_=last_y[:])
         nc.sync.dma_start(out=out[:P, :], in_=windows[0][:])
-        scatter_on_scalar(LAST, 1, last_y[1][:])
+        scatter_second_window(CUT, E * C, rest[:])
         nc.sync.dma_start(out=out[P:, :], in_=windows[1][:])

@@ -28,6 +28,7 @@ LIST_COLS = C // 16
 BLOCKS = N // P
 LAST = E - 1
 VECTOR_PLACES = 16
+W1_PLACES = 80
 CUT = C + (E - 1) * C // 2
 
 W3_BYTES = PACK * H * 4
@@ -46,7 +47,7 @@ def tile_moe_two_glu_silu_kernel(tc, xT, w1, w3, w2, gate, offs, dst, out):
             return keep.tile(shape, dtype, name=name, tag=behind or name, align_bytes=64)
 
         def in_w3(e, quarter, shape, dtype, name):
-            return placed.tile(shape, dtype, name=name, align_bytes=64, offset=e * W3_BYTES + quarter * QUARTER)
+            return placed.tile(shape, dtype, name=name, align_bytes=64, offset=e * W3_BYTES + int(quarter * QUARTER))
 
         def quantize(words, scales, values):
             nc.vector.quantize_mx(out=words.bitcast(FP8X4), scales=scales, in_=values)
@@ -74,10 +75,8 @@ def tile_moe_two_glu_silu_kernel(tc, xT, w1, w3, w2, gate, offs, dst, out):
         w1_raw = [kept([P, PACK, H], F32, f"w1_raw{e}") for e in range(E)]
         w3_raw = [in_w3(e, 0, [P, PACK, H], F32, f"w3_raw{e}") for e in range(E)]
         w2_raw = [kept([P, PACK, N], F32, f"w2_raw{e}") for e in range(E)]
-        load(w1_raw[0], w1[0])
         for e in range(E):
-            if e < LAST:
-                load(w1_raw[e + 1], w1[e + 1])
+            load(w1_raw[e], w1[e])
             load(w3_raw[e], w3[e])
             load(w2_raw[e], w2[e])
             if e == 0:
@@ -135,39 +134,42 @@ def tile_moe_two_glu_silu_kernel(tc, xT, w1, w3, w2, gate, offs, dst, out):
                 in_=raw[:].rearrange("p j (m t) -> p m j t", t=PACK)[:, places, :, h * HALF:(h + 1) * HALF],
             )
 
-        def round_w1(e, high_copy, low_behind=""):
-            halves = [kept(half, BF16, f"w1_bf{e}_0", low_behind), kept(half, BF16, f"w1_bf{e}_1")]
-            round_half(on_vector, halves[0], w1_raw[e], 0)
-            round_half(high_copy, halves[1], w1_raw[e], 1)
-            return halves
+        def shared(bf, raw, h, vector_places):
+            round_half(on_scalar, bf, raw, h, slice(vector_places, P))
+            round_half(on_vector, bf, raw, h, slice(0, vector_places))
+
+        def on_gpsimd(side_by_side, planes):
+            nc.gpsimd.tensor_scalar(out=side_by_side, in0=planes, scalar1=1.0, scalar2=0.0, op0=MULT, op1=ADD)
+
+        def halves_of(name, e):
+            return [kept(half, BF16, f"{name}_bf{e}_{h}") for h in range(2)]
 
         def round_w3(e, vector_places):
-            halves = [kept(half, BF16, f"w3_bf{e}_{h}") for h in range(2)]
+            halves = halves_of("w3", e)
             round_half(on_vector, halves[0], w3_raw[e], 0)
-            if vector_places < P:
-                round_half(on_scalar, halves[1], w3_raw[e], 1, slice(vector_places, P))
-            round_half(on_vector, halves[1], w3_raw[e], 1, slice(0, vector_places))
+            shared(halves[1], w3_raw[e], 1, vector_places)
             return halves
 
-        def round_w2(e, copy, behind=""):
-            w2_bf = kept([P, N, PACK], BF16, f"w2_bf{e}", behind)
-            interleave(copy, w2_bf[:], w2_raw[e][:])
-            return w2_bf
-
-        def first_product(name, e, halves, words_at=None, banks_of=""):
-            by_t = []
-            for h, bf in enumerate(halves):
-                words = kept([P, HALF * P], U32, f"{name}_codes{e}_{h}") if words_at is None else words_at[:, h, :]
-                scales = kept([P, HALF * P], U8, f"{name}_scales{e}_{h}")
+        def group_codes(name, pieces, words_at=None):
+            by_t = {}
+            for first, bf in pieces:
+                width = bf.shape[1] * P
+                words = kept([P, width], U32, f"{name}_codes{first}") if words_at is None else words_at
+                scales = kept([P, width], U8, f"{name}_scales{first}")
                 quantize(words[:], scales[:], bf[:].rearrange("p t m j -> p (t m j)"))
-                by_t.extend((words[:, c:c + P], scales[:, c:c + P]) for c in range(0, HALF * P, P))
+                for c in range(0, width, P):
+                    by_t[first + c // P] = (words[:, c:c + P], scales[:, c:c + P])
+            return by_t
+
+        def first_product(name, e, pieces, words_at=None):
+            by_t = group_codes(f"{name}_{e}", pieces, words_at)
             slot_words, slot_scales = slots[e]
             banks = []
             for s in range(BANKS):
                 cols = slice(s * BANK_SLOTS, (s + 1) * BANK_SLOTS)
-                bank = psum.tile([P, PACK, BANK_SLOTS], F32, name=f"{banks_of or name}_bank")
+                bank = psum.tile([P, PACK, BANK_SLOTS], F32, name=f"{name}_bank")
                 for step in range(PACK):
-                    t = (step + s * HALF) % PACK
+                    t = (pieces[0][0] + step + s * HALF) % PACK
                     words, scales = by_t[t]
                     nc.tensor.matmul_mx(
                         out=bank[:, t, :],
@@ -181,6 +183,9 @@ def tile_moe_two_glu_silu_kernel(tc, xT, w1, w3, w2, gate, offs, dst, out):
                 banks.append(bank)
             return banks
 
+        def low_first(halves):
+            return [(0, halves[0]), (HALF, halves[1])]
+
         def silu(e, banks, behind_w3=None):
             acts = []
             for s, bank in enumerate(banks):
@@ -190,22 +195,24 @@ def tile_moe_two_glu_silu_kernel(tc, xT, w1, w3, w2, gate, offs, dst, out):
                 acts.append(act)
             return acts
 
-        def second_layer(e, acts, banks, w2_bf, w2_words):
+        def multiply(e, acts, banks):
             h_bf = kept([P, C, PACK], BF16, f"h_bf{e}")
             for s, bank in enumerate(banks):
                 cols = slice(s * BANK_SLOTS, (s + 1) * BANK_SLOTS)
                 nc.vector.tensor_tensor(
                     out=h_bf[:, cols, :], in0=acts[s][:], in1=bank[:].rearrange("p t c -> p c t"), op=MULT
                 )
-            w2_words, w2_scales = quantize_columns(f"w2_{e}", w2_bf, w2_words)
-            h_words, h_scales = quantize_columns(f"h_{e}", h_bf)
+            return h_bf
+
+        def second_product(w2_blocks, h_codes):
+            h_words, h_scales = h_codes
             y_banks = []
-            for b in range(BLOCKS):
+            for words, scales in w2_blocks:
                 bank = psum_y.tile([P, C], F32, name="y_bank")
                 nc.tensor.matmul_mx(
                     out=bank[:],
-                    lhsT=w2_words[:, b * P:(b + 1) * P].bitcast(FP8X4),
-                    lhsT_scale=w2_scales[:, b * P:(b + 1) * P],
+                    lhsT=words.bitcast(FP8X4),
+                    lhsT_scale=scales,
                     rhs=h_words[:].bitcast(FP8X4),
                     rhs_scale=h_scales[:],
                     start=True,
@@ -213,6 +220,19 @@ def tile_moe_two_glu_silu_kernel(tc, xT, w1, w3, w2, gate, offs, dst, out):
                 )
                 y_banks.append(bank)
             return y_banks
+
+        def by_block(codes):
+            words, scales = codes
+            return [(words[:, c:c + P], scales[:, c:c + P]) for c in range(0, N, P)]
+
+        def second_layer(e, h_bf, w2_bf, w2_words=None):
+            w2_codes = quantize_columns(f"w2_{e}", w2_bf, w2_words)
+            return second_product(by_block(w2_codes), quantize_columns(f"h_{e}", h_bf))
+
+        def w2_on_gpsimd(e):
+            w2_bf = kept([P, N, PACK], BF16, f"w2_bf{e}", f"w3_bf{e}_1")
+            on_gpsimd(w2_bf[:], w2_raw[e][:].rearrange("p j c -> p c j"))
+            return w2_bf
 
         def times_gate(first, end, y, sums):
             nc.vector.tensor_tensor(out=y, in0=gates[:, first:end], in1=sums, op=MULT)
@@ -231,45 +251,62 @@ def tile_moe_two_glu_silu_kernel(tc, xT, w1, w3, w2, gate, offs, dst, out):
         late_bf = kept([P, late * C, PACK], BF16, "late_bf")
         interleave(on_scalar, late_bf[:], rows[:])
         slots = [pair for e in range(EARLY) for pair in by_expert(quantize_columns(f"slot{e}", slot_bf[e]))]
-        acts0 = silu(0, first_product("w1", 0, round_w1(0, on_vector)))
-        slots.extend(by_expert(quantize_columns("late", late_bf)))
-        w1_banks = first_product("w1", 1, round_w1(1, on_vector))
+        w1_bf = halves_of("w1", 0)
+        for h in range(2):
+            round_half(on_vector, w1_bf[h], w1_raw[0], h)
+        acts = silu(0, first_product("w1", 0, low_first(w1_bf)))
 
-        w3_bf = round_w3(0, VECTOR_PLACES)
-        acts1 = silu(1, w1_banks, 0)
-        banks = first_product("w3", 0, w3_bf)
-        w2_bf = round_w2(0, on_vector, "w3_bf0_1")
-        y0 = second_layer(0, acts0, banks, w2_bf, kept([P, N], U32, "w2_codes0", "acts0_0"))
-        w1_bf = round_w1(2, on_scalar, "w3_bf0_1")
+        w3_bf = halves_of("w3", 0)
+        for h in range(2):
+            round_half(on_vector, w3_bf[h], w3_raw[0], h)
+        banks = first_product("w3", 0, low_first(w3_bf))
+        slots.extend(by_expert(quantize_columns("late", late_bf, in_w3(0, 0, [P, late * C], U32, "late_codes"))))
+        w2_bf = kept([P, N, PACK], BF16, "w2_bf0")
+        interleave(on_scalar, w2_bf[:], w2_raw[0][:])
+        y0 = second_layer(0, multiply(0, acts, banks), w2_bf, kept([P, N], U32, "w2_codes0", "acts0_0"))
+        w1_bf = halves_of("w1", 1)
+        round_half(on_scalar, w1_bf[1], w1_raw[1], 1)
+        shared(w1_bf[0], w1_raw[1], 0, P // 2)
+        w1_banks = first_product("w1", 1, low_first(w1_bf)[::-1])
+
+        w3_bf = round_w3(1, VECTOR_PLACES)
+        acts = silu(1, w1_banks, 1)
+        banks = first_product("w3", 1, low_first(w3_bf))
+        w2_bf = w2_on_gpsimd(1)
+        y_sb = in_w3(1, 2, [P, BLOCKS, C], F32, "y0")
         for b in range(BLOCKS):
-            send(0, b, y0[b], kept([P, C], F32, f"y0_{b}")[:])
-        w1_banks = first_product("w1", 2, w1_bf)
+            send(0, b, y0[b], y_sb[:, b, :])
+        y1 = second_layer(1, multiply(1, acts, banks), w2_bf, in_w3(1, 0, [P, N], U32, "w2_codes1"))
+        w1_bf = [kept(half, BF16, "w1_bf2_0", "w3_bf1_1"), kept(half, BF16, "w1_bf2_1", "h_bf1")]
+        for h in range(2):
+            round_half(on_vector, w1_bf[h], w1_raw[2], h)
+        w1_banks = first_product("w1", 2, low_first(w1_bf))
 
-        banks = first_product("w3", 1, round_w3(1, P))
-        acts2 = silu(2, w1_banks, 1)
-        w2_bf = round_w2(1, on_vector, "w3_bf1_1")
-        y1 = second_layer(1, acts1, banks, w2_bf, in_w3(0, 0, [P, N], U32, "w2_codes1"))
-        w1_bf = round_w1(3, on_scalar, "w3_bf1_1")
-
-        banks = first_product("w3", 2, round_w3(2, VECTOR_PLACES))
-        w2_bf = round_w2(2, on_scalar)
+        w3_bf = round_w3(2, VECTOR_PLACES)
+        acts = silu(2, w1_banks, 2)
+        banks = first_product("w3", 2, low_first(w3_bf))
+        w2_bf = w2_on_gpsimd(2)
         send(1, 0, y1[0], in_w3(2, 2, [P, C], F32, "y1_0")[:])
-        w1_banks = first_product("w1", 3, w1_bf, in_w3(2, 3, [P, 2, HALF * P], U32, "w1_codes3"), "w3")
-        y2 = second_layer(2, acts2, banks, w2_bf, in_w3(1, 0, [P, N], U32, "w2_codes2"))
+        h_bf = multiply(2, acts, banks)
+        w1_whole = in_w3(2, 0, [P, PACK, P, PACK], BF16, "w1_bf3")
+        for copy, places in ((on_scalar, slice(W1_PLACES, P)), (on_vector, slice(0, W1_PLACES))):
+            copy(
+                out=w1_whole[:].rearrange("p t m j -> p m j t")[:, places],
+                in_=w1_raw[LAST][:].rearrange("p j (m t) -> p m j t", t=PACK)[:, places],
+            )
+        y2 = second_layer(2, h_bf, w2_bf)
+        w1_banks = first_product("w1", LAST, [(0, w1_whole)])
 
         w3_bf = round_w3(LAST, VECTOR_PLACES)
-        acts3 = silu(LAST, w1_banks, LAST)
-        banks = first_product("w3", LAST, w3_bf, None, "w1")
+        acts = silu(LAST, w1_banks, LAST)
+        banks = first_product("w3", LAST, low_first(w3_bf))
+        w2_bf = w2_on_gpsimd(LAST)
         waiting = in_w3(LAST, 2, [P, CUT], F32, "waiting_y")
         send(2, 0, y2[0], waiting[:, :C])
         times_gate(C, 2 * C, waiting[:, C:2 * C], y1[1][:])
         times_gate(2 * C, CUT, waiting[:, 2 * C:CUT], y2[1][:, :C // 2])
         scatter_second_window(C, CUT, waiting[:, C:])
-        w2_bf = kept([P, N, PACK], BF16, "w2_bf3", "w3_bf3_1")
-        nc.gpsimd.tensor_scalar(
-            out=w2_bf[:], in0=w2_raw[LAST][:].rearrange("p j c -> p c j"), scalar1=1.0, scalar2=0.0, op0=MULT, op1=ADD
-        )
-        y3 = second_layer(LAST, acts3, banks, w2_bf, in_w3(LAST, 0, [P, N], U32, "w2_codes3"))
+        y3 = second_layer(LAST, multiply(LAST, acts, banks), w2_bf, in_w3(LAST, 0, [P, N], U32, "w2_codes3"))
 
         rest = kept([P, E * C - CUT], F32, "rest_y", "w3_bf3_1")
         times_gate(CUT, LAST * C, rest[:, :C // 2], y2[1][:, C // 2:])

@@ -78,9 +78,9 @@ def tile_moe_two_glu_silu_kernel(tc, xT, w1, w3, w2, gate, offs, dst, out):
         for e in range(E):
             load(w1_raw[e], w1[e])
             load(w3_raw[e], w3[e])
-            load(w2_raw[e], w2[e])
-            if e == 0:
+            if e == 1:
                 nc.sync.dma_start(dst_sb[:], dst)
+            load(w2_raw[e], w2[e])
 
         make_identity(nc, identity[:])
         for window in windows:
@@ -150,11 +150,20 @@ def tile_moe_two_glu_silu_kernel(tc, xT, w1, w3, w2, gate, offs, dst, out):
             shared(halves[1], w3_raw[e], 1, vector_places)
             return halves
 
-        def group_codes(name, pieces, words_at=None):
+        def round_by_halves(e):
+            halves = halves_of("w3", e)
+            round_half(on_scalar, halves[1], w3_raw[e], 1)
+            round_half(on_vector, halves[0], w3_raw[e], 0)
+            return halves
+
+        def group_codes(name, pieces, last_words=None):
             by_t = {}
             for first, bf in pieces:
                 width = bf.shape[1] * P
-                words = kept([P, width], U32, f"{name}_codes{first}") if words_at is None else words_at
+                if last_words is not None and first == pieces[-1][0]:
+                    words = last_words
+                else:
+                    words = kept([P, width], U32, f"{name}_codes{first}")
                 scales = kept([P, width], U8, f"{name}_scales{first}")
                 quantize(words[:], scales[:], bf[:].rearrange("p t m j -> p (t m j)"))
                 for c in range(0, width, P):
@@ -229,8 +238,8 @@ def tile_moe_two_glu_silu_kernel(tc, xT, w1, w3, w2, gate, offs, dst, out):
             w2_codes = quantize_columns(f"w2_{e}", w2_bf, w2_words)
             return second_product(by_block(w2_codes), quantize_columns(f"h_{e}", h_bf))
 
-        def w2_on_gpsimd(e):
-            w2_bf = kept([P, N, PACK], BF16, f"w2_bf{e}", f"w3_bf{e}_1")
+        def w2_on_gpsimd(e, later_half=1):
+            w2_bf = kept([P, N, PACK], BF16, f"w2_bf{e}", f"w3_bf{e}_{later_half}")
             on_gpsimd(w2_bf[:], w2_raw[e][:].rearrange("p j c -> p c j"))
             return w2_bf
 
@@ -266,7 +275,7 @@ def tile_moe_two_glu_silu_kernel(tc, xT, w1, w3, w2, gate, offs, dst, out):
         y0 = second_layer(0, multiply(0, acts, banks), w2_bf, kept([P, N], U32, "w2_codes0", "acts0_0"))
         w1_bf = halves_of("w1", 1)
         round_half(on_scalar, w1_bf[1], w1_raw[1], 1)
-        shared(w1_bf[0], w1_raw[1], 0, P // 2)
+        shared(w1_bf[0], w1_raw[1], 0, W1_PLACES)
         w1_banks = first_product("w1", 1, low_first(w1_bf)[::-1])
 
         w3_bf = round_w3(1, VECTOR_PLACES)
@@ -282,10 +291,10 @@ def tile_moe_two_glu_silu_kernel(tc, xT, w1, w3, w2, gate, offs, dst, out):
             round_half(on_vector, w1_bf[h], w1_raw[2], h)
         w1_banks = first_product("w1", 2, low_first(w1_bf))
 
-        w3_bf = round_w3(2, VECTOR_PLACES)
+        w3_bf = round_by_halves(2)
         acts = silu(2, w1_banks, 2)
-        banks = first_product("w3", 2, low_first(w3_bf))
-        w2_bf = w2_on_gpsimd(2)
+        banks = first_product("w3", 2, low_first(w3_bf)[::-1], in_w3(2, 3, [P, HALF * P], U32, "w3_low_codes2"))
+        w2_bf = w2_on_gpsimd(2, 0)
         send(1, 0, y1[0], in_w3(2, 2, [P, C], F32, "y1_0")[:])
         h_bf = multiply(2, acts, banks)
         w1_whole = in_w3(2, 0, [P, PACK, P, PACK], BF16, "w1_bf3")
@@ -297,10 +306,10 @@ def tile_moe_two_glu_silu_kernel(tc, xT, w1, w3, w2, gate, offs, dst, out):
         y2 = second_layer(2, h_bf, w2_bf)
         w1_banks = first_product("w1", LAST, [(0, w1_whole)])
 
-        w3_bf = round_w3(LAST, VECTOR_PLACES)
+        w3_bf = round_by_halves(LAST)
         acts = silu(LAST, w1_banks, LAST)
-        banks = first_product("w3", LAST, low_first(w3_bf))
-        w2_bf = w2_on_gpsimd(LAST)
+        banks = first_product("w3", LAST, low_first(w3_bf)[::-1], in_w3(LAST, 3.5, [P, HALF * P], U32, "w3_low_codes3"))
+        w2_bf = w2_on_gpsimd(LAST, 0)
         waiting = in_w3(LAST, 2, [P, CUT], F32, "waiting_y")
         send(2, 0, y2[0], waiting[:, :C])
         times_gate(C, 2 * C, waiting[:, C:2 * C], y1[1][:])
@@ -308,7 +317,7 @@ def tile_moe_two_glu_silu_kernel(tc, xT, w1, w3, w2, gate, offs, dst, out):
         scatter_second_window(C, CUT, waiting[:, C:])
         y3 = second_layer(LAST, multiply(LAST, acts, banks), w2_bf, in_w3(LAST, 0, [P, N], U32, "w2_codes3"))
 
-        rest = kept([P, E * C - CUT], F32, "rest_y", "w3_bf3_1")
+        rest = kept([P, E * C - CUT], F32, "rest_y", "w3_bf3_0")
         times_gate(CUT, LAST * C, rest[:, :C // 2], y2[1][:, C // 2:])
         last_y = kept([P, C], F32, "y3_0")
         times_gate(LAST * C, E * C, last_y[:], y3[0][:])

@@ -27,7 +27,7 @@ GATE_COLS = E * C // P
 LIST_COLS = C // 16
 BLOCKS = N // P
 LAST = E - 1
-VECTOR_PLACES = 16
+VECTOR_PLACES = 32
 W1_PLACES = 80
 CUT = C + (E - 1) * C // 2
 
@@ -150,9 +150,9 @@ def tile_moe_two_glu_silu_kernel(tc, xT, w1, w3, w2, gate, offs, dst, out):
             shared(halves[1], w3_raw[e], 1, vector_places)
             return halves
 
-        def round_by_halves(e):
+        def round_by_halves(e, vector_places):
             halves = halves_of("w3", e)
-            round_half(on_scalar, halves[1], w3_raw[e], 1)
+            shared(halves[1], w3_raw[e], 1, vector_places)
             round_half(on_vector, halves[0], w3_raw[e], 0)
             return halves
 
@@ -259,7 +259,7 @@ def tile_moe_two_glu_silu_kernel(tc, xT, w1, w3, w2, gate, offs, dst, out):
 
         late_bf = kept([P, late * C, PACK], BF16, "late_bf")
         interleave(on_scalar, late_bf[:], rows[:])
-        slots = [pair for e in range(EARLY) for pair in by_expert(quantize_columns(f"slot{e}", slot_bf[e]))]
+        slots = by_expert(quantize_columns("slot0", slot_bf[0]))
         w1_bf = halves_of("w1", 0)
         for h in range(2):
             round_half(on_vector, w1_bf[h], w1_raw[0], h)
@@ -269,7 +269,9 @@ def tile_moe_two_glu_silu_kernel(tc, xT, w1, w3, w2, gate, offs, dst, out):
         for h in range(2):
             round_half(on_vector, w3_bf[h], w3_raw[0], h)
         banks = first_product("w3", 0, low_first(w3_bf))
-        slots.extend(by_expert(quantize_columns("late", late_bf, in_w3(0, 0, [P, late * C], U32, "late_codes"))))
+        late_slots = by_expert(quantize_columns("late", late_bf, in_w3(0, 0, [P, late * C], U32, "late_codes")))
+        slots.extend(by_expert(quantize_columns("slot1", slot_bf[1], in_w3(0, 1, [P, C], U32, "slot1_codes"))))
+        slots.extend(late_slots)
         w2_bf = kept([P, N, PACK], BF16, "w2_bf0")
         interleave(on_scalar, w2_bf[:], w2_raw[0][:])
         y0 = second_layer(0, multiply(0, acts, banks), w2_bf, kept([P, N], U32, "w2_codes0", "acts0_0"))
@@ -291,7 +293,7 @@ def tile_moe_two_glu_silu_kernel(tc, xT, w1, w3, w2, gate, offs, dst, out):
             round_half(on_vector, w1_bf[h], w1_raw[2], h)
         w1_banks = first_product("w1", 2, low_first(w1_bf))
 
-        w3_bf = round_by_halves(2)
+        w3_bf = round_by_halves(2, 16)
         acts = silu(2, w1_banks, 2)
         banks = first_product("w3", 2, low_first(w3_bf)[::-1], in_w3(2, 3, [P, HALF * P], U32, "w3_low_codes2"))
         w2_bf = w2_on_gpsimd(2, 0)
@@ -306,7 +308,7 @@ def tile_moe_two_glu_silu_kernel(tc, xT, w1, w3, w2, gate, offs, dst, out):
         y2 = second_layer(2, h_bf, w2_bf)
         w1_banks = first_product("w1", LAST, [(0, w1_whole)])
 
-        w3_bf = round_by_halves(LAST)
+        w3_bf = round_by_halves(LAST, VECTOR_PLACES)
         acts = silu(LAST, w1_banks, LAST)
         banks = first_product("w3", LAST, low_first(w3_bf)[::-1], in_w3(LAST, 3.5, [P, HALF * P], U32, "w3_low_codes3"))
         w2_bf = w2_on_gpsimd(LAST, 0)
@@ -315,7 +317,24 @@ def tile_moe_two_glu_silu_kernel(tc, xT, w1, w3, w2, gate, offs, dst, out):
         times_gate(C, 2 * C, waiting[:, C:2 * C], y1[1][:])
         times_gate(2 * C, CUT, waiting[:, 2 * C:CUT], y2[1][:, :C // 2])
         scatter_second_window(C, CUT, waiting[:, C:])
-        y3 = second_layer(LAST, multiply(LAST, acts, banks), w2_bf, in_w3(LAST, 0, [P, N], U32, "w2_codes3"))
+        h_bf = multiply(LAST, acts, banks)
+        h_codes = [quantize_columns("h_3_0", h_bf[:, :BANK_SLOTS, :], in_w3(LAST, 0.5, [P, BANK_SLOTS], U32, "h_codes3"))]
+        w2_blocks = by_block(quantize_columns("w2_3", w2_bf, in_w3(LAST, 0, [P, N], U32, "w2_codes3")))
+        h_codes.append(quantize_columns("h_3_1", h_bf[:, BANK_SLOTS:, :]))
+        y3 = []
+        for words, scales in w2_blocks:
+            bank = psum_y.tile([P, C], F32, name="y_bank")
+            for s, (h_words, h_scales) in enumerate(h_codes):
+                nc.tensor.matmul_mx(
+                    out=bank[:, s * BANK_SLOTS:(s + 1) * BANK_SLOTS],
+                    lhsT=words.bitcast(FP8X4),
+                    lhsT_scale=scales,
+                    rhs=h_words[:].bitcast(FP8X4),
+                    rhs_scale=h_scales[:],
+                    start=True,
+                    stop=True,
+                )
+            y3.append(bank)
 
         rest = kept([P, E * C - CUT], F32, "rest_y", "w3_bf3_0")
         times_gate(CUT, LAST * C, rest[:, :C // 2], y2[1][:, C // 2:])

@@ -27,12 +27,14 @@ GATE_COLS = E * C // P
 LIST_COLS = C // 16
 BLOCKS = N // P
 LAST = E - 1
-VECTOR_PLACES = 32
+DMA_ALIGN = 256
+W3_PLACES = 32
+W3_PLACES_LATE = 16
 W1_PLACES = 80
 CUT = C + (E - 1) * C // 2
 
 W3_BYTES = PACK * H * 4
-QUARTER = W3_BYTES // 4
+EIGHTH = W3_BYTES // 8
 
 
 def tile_moe_two_glu_silu_kernel(tc, xT, w1, w3, w2, gate, offs, dst, out):
@@ -46,15 +48,18 @@ def tile_moe_two_glu_silu_kernel(tc, xT, w1, w3, w2, gate, offs, dst, out):
         def kept(shape, dtype, name, behind=""):
             return keep.tile(shape, dtype, name=name, tag=behind or name, align_bytes=64)
 
-        def in_w3(e, quarter, shape, dtype, name):
-            return placed.tile(shape, dtype, name=name, align_bytes=64, offset=e * W3_BYTES + int(quarter * QUARTER))
+        def moved(shape, name):
+            return keep.tile(shape, F32, name=name, align_bytes=DMA_ALIGN)
+
+        def in_w3(e, eighth, shape, dtype, name):
+            return placed.tile(shape, dtype, name=name, align_bytes=DMA_ALIGN, offset=e * W3_BYTES + eighth * EIGHTH)
 
         def quantize(words, scales, values):
             nc.vector.quantize_mx(out=words.bitcast(FP8X4), scales=scales, in_=values)
 
         offs_sb = keep.tile([P, E * LIST_COLS], U16, name="offs_sb")
         dst_sb = keep.tile([P, E * LIST_COLS], U16, name="dst_sb")
-        windows = [keep.tile([P, T], F32, name=f"window{b}") for b in range(BLOCKS)]
+        windows = [moved([P, T], f"window{b}") for b in range(BLOCKS)]
         gates = keep.tile([P, E * C], F32, name="gates")
         gate_cols = keep.tile([P, GATE_COLS], F32, name="gate_cols")
         identity = keep.tile([P, P], F32, name="identity")
@@ -63,7 +68,7 @@ def tile_moe_two_glu_silu_kernel(tc, xT, w1, w3, w2, gate, offs, dst, out):
         x_rows = xT.rearrange("(p j) t -> p j t", j=PACK)
         x_planes = []
         for j in range(PACK):
-            plane = kept([P, T], F32, f"x_plane{j}")
+            plane = moved([P, T], f"x_plane{j}")
             nc.sync.dma_start(out=plane[:], in_=x_rows[:, j, :])
             x_planes.append(plane)
             if j == 0:
@@ -72,9 +77,9 @@ def tile_moe_two_glu_silu_kernel(tc, xT, w1, w3, w2, gate, offs, dst, out):
         def load(raw, w):
             nc.sync.dma_start(out=raw[:], in_=w.rearrange("(p j) n -> p j n", j=PACK))
 
-        w1_raw = [kept([P, PACK, H], F32, f"w1_raw{e}") for e in range(E)]
+        w1_raw = [moved([P, PACK, H], f"w1_raw{e}") for e in range(E)]
         w3_raw = [in_w3(e, 0, [P, PACK, H], F32, f"w3_raw{e}") for e in range(E)]
-        w2_raw = [kept([P, PACK, N], F32, f"w2_raw{e}") for e in range(E)]
+        w2_raw = [moved([P, PACK, N], f"w2_raw{e}") for e in range(E)]
         for e in range(E):
             load(w1_raw[e], w1[e])
             load(w3_raw[e], w3[e])
@@ -134,44 +139,35 @@ def tile_moe_two_glu_silu_kernel(tc, xT, w1, w3, w2, gate, offs, dst, out):
                 in_=raw[:].rearrange("p j (m t) -> p m j t", t=PACK)[:, places, :, h * HALF:(h + 1) * HALF],
             )
 
-        def shared(bf, raw, h, vector_places):
+        def round_shared(bf, raw, h, vector_places):
             round_half(on_scalar, bf, raw, h, slice(vector_places, P))
             round_half(on_vector, bf, raw, h, slice(0, vector_places))
-
-        def on_gpsimd(side_by_side, planes):
-            nc.gpsimd.tensor_scalar(out=side_by_side, in0=planes, scalar1=1.0, scalar2=0.0, op0=MULT, op1=ADD)
 
         def halves_of(name, e):
             return [kept(half, BF16, f"{name}_bf{e}_{h}") for h in range(2)]
 
-        def round_w3(e, vector_places):
-            halves = halves_of("w3", e)
-            round_half(on_vector, halves[0], w3_raw[e], 0)
-            shared(halves[1], w3_raw[e], 1, vector_places)
-            return halves
+        def round_on_vector(halves, raw):
+            for h, bf in enumerate(halves):
+                round_half(on_vector, bf, raw, h)
 
-        def round_by_halves(e, vector_places):
-            halves = halves_of("w3", e)
-            shared(halves[1], w3_raw[e], 1, vector_places)
-            round_half(on_vector, halves[0], w3_raw[e], 0)
-            return halves
+        def low_first(halves):
+            return [(0, halves[0]), (HALF, halves[1])]
 
-        def group_codes(name, pieces, last_words=None):
+        def high_first(halves):
+            return [(HALF, halves[1]), (0, halves[0])]
+
+        def first_product(name, e, pieces, last_words=None):
             by_t = {}
             for first, bf in pieces:
                 width = bf.shape[1] * P
                 if last_words is not None and first == pieces[-1][0]:
                     words = last_words
                 else:
-                    words = kept([P, width], U32, f"{name}_codes{first}")
-                scales = kept([P, width], U8, f"{name}_scales{first}")
+                    words = kept([P, width], U32, f"{name}_{e}_codes{first}")
+                scales = kept([P, width], U8, f"{name}_{e}_scales{first}")
                 quantize(words[:], scales[:], bf[:].rearrange("p t m j -> p (t m j)"))
                 for c in range(0, width, P):
                     by_t[first + c // P] = (words[:, c:c + P], scales[:, c:c + P])
-            return by_t
-
-        def first_product(name, e, pieces, words_at=None):
-            by_t = group_codes(f"{name}_{e}", pieces, words_at)
             slot_words, slot_scales = slots[e]
             banks = []
             for s in range(BANKS):
@@ -192,14 +188,11 @@ def tile_moe_two_glu_silu_kernel(tc, xT, w1, w3, w2, gate, offs, dst, out):
                 banks.append(bank)
             return banks
 
-        def low_first(halves):
-            return [(0, halves[0]), (HALF, halves[1])]
-
         def silu(e, banks, behind_w3=None):
             acts = []
             for s, bank in enumerate(banks):
                 shape, name = [P, BANK_SLOTS, PACK], f"acts{e}_{s}"
-                act = kept(shape, F32, name) if behind_w3 is None else in_w3(behind_w3, s, shape, F32, name)
+                act = kept(shape, F32, name) if behind_w3 is None else in_w3(behind_w3, 2 * s, shape, F32, name)
                 nc.scalar.activation(out=act[:], in_=bank[:].rearrange("p t c -> p c t"), func=SILU)
                 acts.append(act)
             return acts
@@ -213,45 +206,41 @@ def tile_moe_two_glu_silu_kernel(tc, xT, w1, w3, w2, gate, offs, dst, out):
                 )
             return h_bf
 
-        def second_product(w2_blocks, h_codes):
-            h_words, h_scales = h_codes
+        def second_product(w2_codes, h_pieces):
+            w2_words, w2_scales = w2_codes
             y_banks = []
-            for words, scales in w2_blocks:
+            for b in range(BLOCKS):
                 bank = psum_y.tile([P, C], F32, name="y_bank")
-                nc.tensor.matmul_mx(
-                    out=bank[:],
-                    lhsT=words.bitcast(FP8X4),
-                    lhsT_scale=scales,
-                    rhs=h_words[:].bitcast(FP8X4),
-                    rhs_scale=h_scales[:],
-                    start=True,
-                    stop=True,
-                )
+                width = C // len(h_pieces)
+                for s, (h_words, h_scales) in enumerate(h_pieces):
+                    nc.tensor.matmul_mx(
+                        out=bank[:, s * width:(s + 1) * width],
+                        lhsT=w2_words[:, b * P:(b + 1) * P].bitcast(FP8X4),
+                        lhsT_scale=w2_scales[:, b * P:(b + 1) * P],
+                        rhs=h_words[:].bitcast(FP8X4),
+                        rhs_scale=h_scales[:],
+                        start=True,
+                        stop=True,
+                    )
                 y_banks.append(bank)
             return y_banks
 
-        def by_block(codes):
-            words, scales = codes
-            return [(words[:, c:c + P], scales[:, c:c + P]) for c in range(0, N, P)]
-
         def second_layer(e, h_bf, w2_bf, w2_words=None):
             w2_codes = quantize_columns(f"w2_{e}", w2_bf, w2_words)
-            return second_product(by_block(w2_codes), quantize_columns(f"h_{e}", h_bf))
+            return second_product(w2_codes, [quantize_columns(f"h_{e}", h_bf)])
 
-        def w2_on_gpsimd(e, later_half=1):
-            w2_bf = kept([P, N, PACK], BF16, f"w2_bf{e}", f"w3_bf{e}_{later_half}")
-            on_gpsimd(w2_bf[:], w2_raw[e][:].rearrange("p j c -> p c j"))
+        def round_w2_on_gpsimd(e, behind):
+            w2_bf = kept([P, N, PACK], BF16, f"w2_bf{e}", behind)
+            planes = w2_raw[e][:].rearrange("p j c -> p c j")
+            nc.gpsimd.tensor_scalar(out=w2_bf[:], in0=planes, scalar1=1.0, scalar2=0.0, op0=MULT, op1=ADD)
             return w2_bf
 
         def times_gate(first, end, y, sums):
             nc.vector.tensor_tensor(out=y, in0=gates[:, first:end], in1=sums, op=MULT)
 
-        def scatter_on_scalar(e, b, y):
-            nc.scalar.activation(out=windows[b][:].indirect(entries(dst_sb, e)), in_=y, func=COPY)
-
         def send(e, b, bank, y):
             times_gate(e * C, (e + 1) * C, y, bank[:])
-            scatter_on_scalar(e, b, y)
+            nc.scalar.activation(out=windows[b][:].indirect(entries(dst_sb, e)), in_=y, func=COPY)
 
         def scatter_second_window(first, end, y):
             offsets = dst_sb[:, first * LIST_COLS // C:end * LIST_COLS // C]
@@ -261,43 +250,44 @@ def tile_moe_two_glu_silu_kernel(tc, xT, w1, w3, w2, gate, offs, dst, out):
         interleave(on_scalar, late_bf[:], rows[:])
         slots = by_expert(quantize_columns("slot0", slot_bf[0]))
         w1_bf = halves_of("w1", 0)
-        for h in range(2):
-            round_half(on_vector, w1_bf[h], w1_raw[0], h)
+        round_on_vector(w1_bf, w1_raw[0])
         acts = silu(0, first_product("w1", 0, low_first(w1_bf)))
 
         w3_bf = halves_of("w3", 0)
-        for h in range(2):
-            round_half(on_vector, w3_bf[h], w3_raw[0], h)
+        round_on_vector(w3_bf, w3_raw[0])
         banks = first_product("w3", 0, low_first(w3_bf))
         late_slots = by_expert(quantize_columns("late", late_bf, in_w3(0, 0, [P, late * C], U32, "late_codes")))
-        slots.extend(by_expert(quantize_columns("slot1", slot_bf[1], in_w3(0, 1, [P, C], U32, "slot1_codes"))))
+        slots.extend(by_expert(quantize_columns("slot1", slot_bf[1], in_w3(0, 2, [P, C], U32, "slot1_codes"))))
         slots.extend(late_slots)
         w2_bf = kept([P, N, PACK], BF16, "w2_bf0")
         interleave(on_scalar, w2_bf[:], w2_raw[0][:])
         y0 = second_layer(0, multiply(0, acts, banks), w2_bf, kept([P, N], U32, "w2_codes0", "acts0_0"))
         w1_bf = halves_of("w1", 1)
         round_half(on_scalar, w1_bf[1], w1_raw[1], 1)
-        shared(w1_bf[0], w1_raw[1], 0, W1_PLACES)
-        w1_banks = first_product("w1", 1, low_first(w1_bf)[::-1])
+        round_shared(w1_bf[0], w1_raw[1], 0, W1_PLACES)
+        w1_banks = first_product("w1", 1, high_first(w1_bf))
 
-        w3_bf = round_w3(1, VECTOR_PLACES)
+        w3_bf = halves_of("w3", 1)
+        round_half(on_vector, w3_bf[0], w3_raw[1], 0)
+        round_shared(w3_bf[1], w3_raw[1], 1, W3_PLACES)
         acts = silu(1, w1_banks, 1)
         banks = first_product("w3", 1, low_first(w3_bf))
-        w2_bf = w2_on_gpsimd(1)
-        y_sb = in_w3(1, 2, [P, BLOCKS, C], F32, "y0")
+        w2_bf = round_w2_on_gpsimd(1, "w3_bf1_1")
+        y_sb = in_w3(1, 4, [P, BLOCKS, C], F32, "y0")
         for b in range(BLOCKS):
             send(0, b, y0[b], y_sb[:, b, :])
         y1 = second_layer(1, multiply(1, acts, banks), w2_bf, in_w3(1, 0, [P, N], U32, "w2_codes1"))
         w1_bf = [kept(half, BF16, "w1_bf2_0", "w3_bf1_1"), kept(half, BF16, "w1_bf2_1", "h_bf1")]
-        for h in range(2):
-            round_half(on_vector, w1_bf[h], w1_raw[2], h)
+        round_on_vector(w1_bf, w1_raw[2])
         w1_banks = first_product("w1", 2, low_first(w1_bf))
 
-        w3_bf = round_by_halves(2, 16)
+        w3_bf = halves_of("w3", 2)
+        round_shared(w3_bf[1], w3_raw[2], 1, W3_PLACES_LATE)
+        round_half(on_vector, w3_bf[0], w3_raw[2], 0)
         acts = silu(2, w1_banks, 2)
-        banks = first_product("w3", 2, low_first(w3_bf)[::-1], in_w3(2, 3, [P, HALF * P], U32, "w3_low_codes2"))
-        w2_bf = w2_on_gpsimd(2, 0)
-        send(1, 0, y1[0], in_w3(2, 2, [P, C], F32, "y1_0")[:])
+        banks = first_product("w3", 2, high_first(w3_bf), in_w3(2, 6, [P, HALF * P], U32, "w3_low_codes2"))
+        w2_bf = round_w2_on_gpsimd(2, "w3_bf2_0")
+        send(1, 0, y1[0], in_w3(2, 4, [P, C], F32, "y1_0")[:])
         h_bf = multiply(2, acts, banks)
         w1_whole = in_w3(2, 0, [P, PACK, P, PACK], BF16, "w1_bf3")
         for copy, places in ((on_scalar, slice(W1_PLACES, P)), (on_vector, slice(0, W1_PLACES))):
@@ -308,33 +298,21 @@ def tile_moe_two_glu_silu_kernel(tc, xT, w1, w3, w2, gate, offs, dst, out):
         y2 = second_layer(2, h_bf, w2_bf)
         w1_banks = first_product("w1", LAST, [(0, w1_whole)])
 
-        w3_bf = round_by_halves(LAST, VECTOR_PLACES)
+        w3_bf = halves_of("w3", LAST)
+        round_shared(w3_bf[1], w3_raw[LAST], 1, W3_PLACES)
+        round_half(on_vector, w3_bf[0], w3_raw[LAST], 0)
         acts = silu(LAST, w1_banks, LAST)
-        banks = first_product("w3", LAST, low_first(w3_bf)[::-1], in_w3(LAST, 3.5, [P, HALF * P], U32, "w3_low_codes3"))
-        w2_bf = w2_on_gpsimd(LAST, 0)
-        waiting = in_w3(LAST, 2, [P, CUT], F32, "waiting_y")
+        banks = first_product("w3", LAST, high_first(w3_bf), in_w3(LAST, 7, [P, HALF * P], U32, "w3_low_codes3"))
+        w2_bf = round_w2_on_gpsimd(LAST, "w3_bf3_0")
+        waiting = in_w3(LAST, 4, [P, CUT], F32, "waiting_y")
         send(2, 0, y2[0], waiting[:, :C])
         times_gate(C, 2 * C, waiting[:, C:2 * C], y1[1][:])
         times_gate(2 * C, CUT, waiting[:, 2 * C:CUT], y2[1][:, :C // 2])
         scatter_second_window(C, CUT, waiting[:, C:])
         h_bf = multiply(LAST, acts, banks)
-        h_codes = [quantize_columns("h_3_0", h_bf[:, :BANK_SLOTS, :], in_w3(LAST, 0.5, [P, BANK_SLOTS], U32, "h_codes3"))]
-        w2_blocks = by_block(quantize_columns("w2_3", w2_bf, in_w3(LAST, 0, [P, N], U32, "w2_codes3")))
-        h_codes.append(quantize_columns("h_3_1", h_bf[:, BANK_SLOTS:, :]))
-        y3 = []
-        for words, scales in w2_blocks:
-            bank = psum_y.tile([P, C], F32, name="y_bank")
-            for s, (h_words, h_scales) in enumerate(h_codes):
-                nc.tensor.matmul_mx(
-                    out=bank[:, s * BANK_SLOTS:(s + 1) * BANK_SLOTS],
-                    lhsT=words.bitcast(FP8X4),
-                    lhsT_scale=scales,
-                    rhs=h_words[:].bitcast(FP8X4),
-                    rhs_scale=h_scales[:],
-                    start=True,
-                    stop=True,
-                )
-            y3.append(bank)
+        h_first = quantize_columns("h_3_0", h_bf[:, :BANK_SLOTS, :], in_w3(LAST, 1, [P, BANK_SLOTS], U32, "h_codes3"))
+        w2_codes = quantize_columns("w2_3", w2_bf, in_w3(LAST, 0, [P, N], U32, "w2_codes3"))
+        y3 = second_product(w2_codes, [h_first, quantize_columns("h_3_1", h_bf[:, BANK_SLOTS:, :])])
 
         rest = kept([P, E * C - CUT], F32, "rest_y", "w3_bf3_0")
         times_gate(CUT, LAST * C, rest[:, :C // 2], y2[1][:, C // 2:])

@@ -29,8 +29,10 @@ BLOCKS = N // P
 LAST = E - 1
 DMA_ALIGN = 256
 W3_PLACES = 32
-W3_PLACES_LATE = 16
-W1_PLACES = 80
+W3_PLACES_LATE = 32
+W3_PLACES_LAST = 32
+W1_PLACES = 96
+W1_LAST = 32
 CUT = C + (E - 1) * C // 2
 
 W3_BYTES = PACK * H * 4
@@ -272,12 +274,12 @@ def tile_moe_two_glu_silu_kernel(tc, xT, w1, w3, w2, gate, offs, dst, out):
         round_shared(w3_bf[1], w3_raw[1], 1, W3_PLACES)
         acts = silu(1, w1_banks, 1)
         banks = first_product("w3", 1, low_first(w3_bf))
-        w2_bf = round_w2_on_gpsimd(1, "w3_bf1_1")
+        w2_bf = round_w2_on_gpsimd(1, "w3_bf1_0")
         y_sb = in_w3(1, 4, [P, BLOCKS, C], F32, "y0")
         for b in range(BLOCKS):
             send(0, b, y0[b], y_sb[:, b, :])
         y1 = second_layer(1, multiply(1, acts, banks), w2_bf, in_w3(1, 0, [P, N], U32, "w2_codes1"))
-        w1_bf = [kept(half, BF16, "w1_bf2_0", "w3_bf1_1"), kept(half, BF16, "w1_bf2_1", "h_bf1")]
+        w1_bf = [kept(half, BF16, "w1_bf2_0", "w3_bf1_0"), kept(half, BF16, "w1_bf2_1", "h_bf1")]
         round_on_vector(w1_bf, w1_raw[2])
         w1_banks = first_product("w1", 2, low_first(w1_bf))
 
@@ -286,24 +288,21 @@ def tile_moe_two_glu_silu_kernel(tc, xT, w1, w3, w2, gate, offs, dst, out):
         round_half(on_vector, w3_bf[0], w3_raw[2], 0)
         acts = silu(2, w1_banks, 2)
         banks = first_product("w3", 2, high_first(w3_bf), in_w3(2, 6, [P, HALF * P], U32, "w3_low_codes2"))
-        w2_bf = round_w2_on_gpsimd(2, "w3_bf2_0")
+        w2_bf = round_w2_on_gpsimd(2, "w3_bf2_1")
         send(1, 0, y1[0], in_w3(2, 4, [P, C], F32, "y1_0")[:])
         h_bf = multiply(2, acts, banks)
-        w1_whole = in_w3(2, 0, [P, PACK, P, PACK], BF16, "w1_bf3")
-        for copy, places in ((on_scalar, slice(W1_PLACES, P)), (on_vector, slice(0, W1_PLACES))):
-            copy(
-                out=w1_whole[:].rearrange("p t m j -> p m j t")[:, places],
-                in_=w1_raw[LAST][:].rearrange("p j (m t) -> p m j t", t=PACK)[:, places],
-            )
-        y2 = second_layer(2, h_bf, w2_bf)
-        w1_banks = first_product("w1", LAST, [(0, w1_whole)])
+        y2 = second_layer(2, h_bf, w2_bf, in_w3(2, 0, [P, N], U32, "w2_codes2"))
+        w1_bf = [kept(half, BF16, "w1_bf3_0", "w3_bf2_1"), in_w3(2, 2, half, BF16, "w1_bf3_1")]
+        round_half(on_vector, w1_bf[0], w1_raw[LAST], 0)
+        round_shared(w1_bf[1], w1_raw[LAST], 1, W1_LAST)
+        w1_banks = first_product("w1", LAST, low_first(w1_bf))
 
         w3_bf = halves_of("w3", LAST)
-        round_shared(w3_bf[1], w3_raw[LAST], 1, W3_PLACES)
+        round_shared(w3_bf[1], w3_raw[LAST], 1, W3_PLACES_LAST)
         round_half(on_vector, w3_bf[0], w3_raw[LAST], 0)
         acts = silu(LAST, w1_banks, LAST)
         banks = first_product("w3", LAST, high_first(w3_bf), in_w3(LAST, 7, [P, HALF * P], U32, "w3_low_codes3"))
-        w2_bf = round_w2_on_gpsimd(LAST, "w3_bf3_0")
+        w2_bf = round_w2_on_gpsimd(LAST, "w3_bf3_1")
         waiting = in_w3(LAST, 4, [P, CUT], F32, "waiting_y")
         send(2, 0, y2[0], waiting[:, :C])
         times_gate(C, 2 * C, waiting[:, C:2 * C], y1[1][:])
@@ -314,7 +313,7 @@ def tile_moe_two_glu_silu_kernel(tc, xT, w1, w3, w2, gate, offs, dst, out):
         w2_codes = quantize_columns("w2_3", w2_bf, in_w3(LAST, 0, [P, N], U32, "w2_codes3"))
         y3 = second_product(w2_codes, [h_first, quantize_columns("h_3_1", h_bf[:, BANK_SLOTS:, :])])
 
-        rest = kept([P, E * C - CUT], F32, "rest_y", "w3_bf3_0")
+        rest = kept([P, E * C - CUT], F32, "rest_y", "w3_bf3_1")
         times_gate(CUT, LAST * C, rest[:, :C // 2], y2[1][:, C // 2:])
         last_y = kept([P, C], F32, "y3_0")
         times_gate(LAST * C, E * C, last_y[:], y3[0][:])

@@ -29,10 +29,11 @@ BLOCKS = N // P
 LAST = E - 1
 DMA_ALIGN = 256
 W3_PLACES = 32
-W3_PLACES_LATE = 32
-W3_PLACES_LAST = 32
+S2 = 56
+S3 = 72
+TAILP = 128
 W1_PLACES = 96
-W1_LAST = 32
+W1_LAST = 64
 CUT = C + (E - 1) * C // 2
 
 W3_BYTES = PACK * H * 4
@@ -53,8 +54,9 @@ def tile_moe_two_glu_silu_kernel(tc, xT, w1, w3, w2, gate, offs, dst, out):
         def moved(shape, name):
             return keep.tile(shape, F32, name=name, align_bytes=DMA_ALIGN)
 
-        def in_w3(e, eighth, shape, dtype, name):
-            return placed.tile(shape, dtype, name=name, align_bytes=DMA_ALIGN, offset=e * W3_BYTES + eighth * EIGHTH)
+        def in_w3(e, eighth, shape, dtype, name, skip=0):
+            offset = e * W3_BYTES + eighth * EIGHTH + skip
+            return placed.tile(shape, dtype, name=name, align_bytes=DMA_ALIGN, offset=offset)
 
         def quantize(words, scales, values):
             nc.vector.quantize_mx(out=words.bitcast(FP8X4), scales=scales, in_=values)
@@ -80,16 +82,30 @@ def tile_moe_two_glu_silu_kernel(tc, xT, w1, w3, w2, gate, offs, dst, out):
             nc.sync.dma_start(out=raw[:], in_=w.rearrange("(p j) n -> p j n", j=PACK))
 
         w1_raw = [moved([P, PACK, H], f"w1_raw{e}") for e in range(E)]
-        w3_raw = [in_w3(e, 0, [P, PACK, H], F32, f"w3_raw{e}") for e in range(E)]
+        w3_raw = [in_w3(e, 0, [P, PACK, H], F32, f"w3_raw{e}") for e in range(2)]
+        scalar_places = {2: S2, 3: S3}
+        w3_parts = {}
+        for e, n in scalar_places.items():
+            w3_parts[e] = [
+                in_w3(e, 0, [P, PACK, n * PACK], F32, f"w3_part{e}_0"),
+                in_w3(e, 0, [P, PACK, H - n * PACK], F32, f"w3_part{e}_1", n * PACK * PACK * 4),
+            ]
         w2_raw = [moved([P, PACK, N], f"w2_raw{e}") for e in range(E)]
         for e in range(E):
             load(w1_raw[e], w1[e])
-            load(w3_raw[e], w3[e])
+            if e in w3_parts:
+                cut = scalar_places[e] * PACK
+                load(w3_parts[e][0], w3[e][:, :cut])
+                load(w3_parts[e][1], w3[e][:, cut:])
+            else:
+                load(w3_raw[e], w3[e])
             if e == 1:
                 nc.sync.dma_start(dst_sb[:], dst)
             load(w2_raw[e], w2[e])
 
         make_identity(nc, identity[:])
+        ones = keep.tile([P, 1], F32, name="ones")
+        nc.vector.memset(ones[:], 1.0)
         for window in windows:
             nc.vector.memset(window[:], 0.0)
         for m0 in range(0, GATE_COLS, PACK):
@@ -248,6 +264,41 @@ def tile_moe_two_glu_silu_kernel(tc, xT, w1, w3, w2, gate, offs, dst, out):
             offsets = dst_sb[:, first * LIST_COLS // C:end * LIST_COLS // C]
             nc.scalar.activation(out=windows[1][:].indirect(offsets), in_=y, func=COPY)
 
+        def round_parts(e, halves):
+            n = scalar_places[e]
+            for copy, part, places in ((on_scalar, 0, slice(0, n)), (on_vector, 1, slice(n, P))):
+                for h in (1, 0):
+                    copy(
+                        out=halves[h][:].rearrange("p t m j -> p m j t")[:, places],
+                        in_=w3_parts[e][part][:].rearrange("p j (m t) -> p m j t", t=PACK)[
+                            :, :, :, h * HALF:(h + 1) * HALF
+                        ],
+                    )
+
+        def round_on_gpsimd(bf, raw):
+            planes = raw[:].rearrange("p j c -> p c j")
+            nc.gpsimd.tensor_scalar(out=bf[:], in0=planes, scalar1=1.0, scalar2=0.0, op0=MULT, op1=ADD)
+            return bf
+
+        def spare(eighth, shape, dtype, name):
+            return in_w3(E, eighth, shape, dtype, name)
+
+        def matmul(bank, w2_codes, h_codes):
+            nc.tensor.matmul_mx(
+                out=bank,
+                lhsT=w2_codes[0][:].bitcast(FP8X4),
+                lhsT_scale=w2_codes[1][:],
+                rhs=h_codes[0][:].bitcast(FP8X4),
+                rhs_scale=h_codes[1][:],
+                start=True,
+                stop=True,
+            )
+
+        def block_product(w2_codes, h_codes):
+            bank = psum_y.tile([P, C], F32, name="y_bank")
+            matmul(bank[:], w2_codes, h_codes)
+            return bank
+
         late_bf = kept([P, late * C, PACK], BF16, "late_bf")
         interleave(on_scalar, late_bf[:], rows[:])
         slots = by_expert(quantize_columns("slot0", slot_bf[0]))
@@ -274,51 +325,71 @@ def tile_moe_two_glu_silu_kernel(tc, xT, w1, w3, w2, gate, offs, dst, out):
         round_shared(w3_bf[1], w3_raw[1], 1, W3_PLACES)
         acts = silu(1, w1_banks, 1)
         banks = first_product("w3", 1, low_first(w3_bf))
-        w2_bf = round_w2_on_gpsimd(1, "w3_bf1_0")
+        w2_bf = round_w2_on_gpsimd(1, "w3_bf1_1")
         y_sb = in_w3(1, 4, [P, BLOCKS, C], F32, "y0")
         for b in range(BLOCKS):
             send(0, b, y0[b], y_sb[:, b, :])
-        y1 = second_layer(1, multiply(1, acts, banks), w2_bf, in_w3(1, 0, [P, N], U32, "w2_codes1"))
-        w1_bf = [kept(half, BF16, "w1_bf2_0", "w3_bf1_0"), kept(half, BF16, "w1_bf2_1", "h_bf1")]
+        h_bf = multiply(1, acts, banks)
+        w1_bf = [spare(8 + 2 * h, half, BF16, f"w1_bf2_{h}") for h in range(2)]
         round_on_vector(w1_bf, w1_raw[2])
         w1_banks = first_product("w1", 2, low_first(w1_bf))
+        h_codes = quantize_columns("h_1", h_bf, spare(8, [P, C], U32, "h_codes1"))
+        y1 = [block_product(quantize_columns("w2_1_0", w2_bf[:, :P, :], spare(9, [P, P], U32, "w2_codes1_0")), h_codes)]
+        w2_before = w2_bf
 
-        w3_bf = halves_of("w3", 2)
-        round_shared(w3_bf[1], w3_raw[2], 1, W3_PLACES_LATE)
-        round_half(on_vector, w3_bf[0], w3_raw[2], 0)
-        acts = silu(2, w1_banks, 2)
-        banks = first_product("w3", 2, high_first(w3_bf), in_w3(2, 6, [P, HALF * P], U32, "w3_low_codes2"))
-        w2_bf = round_w2_on_gpsimd(2, "w3_bf2_1")
-        send(1, 0, y1[0], in_w3(2, 4, [P, C], F32, "y1_0")[:])
+        w3_bf = [spare(2 * h, half, BF16, f"w3_bf2_{h}") for h in range(2)]
+        round_parts(2, w3_bf)
+        acts = silu(2, w1_banks)
+        banks = first_product("w3", 2, high_first(w3_bf))
+        y1.append(block_product(quantize_columns("w2_1_1", w2_before[:, P:, :], spare(2, [P, P], U32, "w2_codes1_1")), h_codes))
+        w2_bf = round_on_gpsimd(spare(0, [P, N, PACK], BF16, "w2_bf2"), w2_raw[2])
+        send(1, 0, y1[0], in_w3(2, 7, [P, C], F32, "y1_0")[:])
         h_bf = multiply(2, acts, banks)
-        y2 = second_layer(2, h_bf, w2_bf, in_w3(2, 0, [P, N], U32, "w2_codes2"))
-        w1_bf = [kept(half, BF16, "w1_bf3_0", "w3_bf2_1"), in_w3(2, 2, half, BF16, "w1_bf3_1")]
+        w1_bf = [spare(12 + 2 * h, half, BF16, f"w1_bf3_{h}") for h in range(2)]
         round_half(on_vector, w1_bf[0], w1_raw[LAST], 0)
         round_shared(w1_bf[1], w1_raw[LAST], 1, W1_LAST)
         w1_banks = first_product("w1", LAST, low_first(w1_bf))
+        h_codes = quantize_columns("h_2", h_bf, spare(12, [P, C], U32, "h_codes2"))
+        y2 = [block_product(quantize_columns("w2_2_0", w2_bf[:, :P, :], spare(13, [P, P], U32, "w2_codes2_0")), h_codes)]
+        w2_before = w2_bf
 
-        w3_bf = halves_of("w3", LAST)
-        round_shared(w3_bf[1], w3_raw[LAST], 1, W3_PLACES_LAST)
-        round_half(on_vector, w3_bf[0], w3_raw[LAST], 0)
-        acts = silu(LAST, w1_banks, LAST)
-        banks = first_product("w3", LAST, high_first(w3_bf), in_w3(LAST, 7, [P, HALF * P], U32, "w3_low_codes3"))
-        w2_bf = round_w2_on_gpsimd(LAST, "w3_bf3_1")
-        waiting = in_w3(LAST, 4, [P, CUT], F32, "waiting_y")
-        send(2, 0, y2[0], waiting[:, :C])
-        times_gate(C, 2 * C, waiting[:, C:2 * C], y1[1][:])
-        times_gate(2 * C, CUT, waiting[:, 2 * C:CUT], y2[1][:, :C // 2])
-        scatter_second_window(C, CUT, waiting[:, C:])
-        h_bf = multiply(LAST, acts, banks)
-        h_first = quantize_columns("h_3_0", h_bf[:, :BANK_SLOTS, :], in_w3(LAST, 1, [P, BANK_SLOTS], U32, "h_codes3"))
-        w2_codes = quantize_columns("w2_3", w2_bf, in_w3(LAST, 0, [P, N], U32, "w2_codes3"))
-        y3 = second_product(w2_codes, [h_first, quantize_columns("h_3_1", h_bf[:, BANK_SLOTS:, :])])
+        w3_bf = [spare(4 + 2 * h, half, BF16, f"w3_bf3_{h}") for h in range(2)]
+        round_parts(LAST, w3_bf)
+        acts = silu(LAST, w1_banks)
+        banks = first_product("w3", LAST, high_first(w3_bf))
+        y2.append(block_product(quantize_columns("w2_2_1", w2_before[:, P:, :], spare(6, [P, P], U32, "w2_codes2_1")), h_codes))
+        w2_bf = round_on_gpsimd(spare(4, [P, N, PACK], BF16, "w2_bf3"), w2_raw[LAST])
+        send(2, 0, y2[0], in_w3(LAST, 7, [P, C], F32, "y2_0")[:])
+        send(1, 1, y1[1], spare(7, [P, C], F32, "y1_1")[:])
 
-        rest = kept([P, E * C - CUT], F32, "rest_y", "w3_bf3_1")
-        times_gate(CUT, LAST * C, rest[:, :C // 2], y2[1][:, C // 2:])
+        cuts = [0, BANK_SLOTS, C - TAILP, C] if TAILP < BANK_SLOTS else [0, BANK_SLOTS, C]
+        spans = list(zip(cuts, cuts[1:]))
+        h_bf = [kept([P, end - first, PACK], BF16, f"h_bf3_{first}") for first, end in spans]
+        for piece, (first, end) in zip(h_bf, spans):
+            s, cols = first // BANK_SLOTS, slice(first % BANK_SLOTS, (end - 1) % BANK_SLOTS + 1)
+            nc.vector.tensor_tensor(
+                out=piece[:], in0=acts[s][:, cols, :], in1=banks[s][:].rearrange("p t c -> p c t")[:, cols, :], op=MULT
+            )
+        h_codes = [quantize_columns("h_3_0", h_bf[0], kept([P, BANK_SLOTS], U32, "h_codes3", "acts3_0"))]
+        first_codes = quantize_columns("w2_3_0", w2_bf[:, :P, :], kept([P, P], U32, "w2_codes3_0"))
+        h_codes.extend(quantize_columns(f"h_3_{s}", h_bf[s]) for s in range(1, len(spans)))
+        early = psum_y.tile([P, C - TAILP], F32, name="y_bank")
+        for codes, (first, end) in list(zip(h_codes, spans))[:-1]:
+            matmul(early[:, first:end], first_codes, codes)
+        late_bank = psum_y.tile([P, TAILP], F32, name="y_bank")
+        matmul(late_bank[:], first_codes, h_codes[-1])
+        second_codes = quantize_columns("w2_3_1", w2_bf[:, P:, :], kept([P, P], U32, "w2_codes3_1", "h_bf3_0"))
+        second = psum_y.tile([P, C], F32, name="y_bank")
+        for codes, (first, end) in zip(h_codes, spans):
+            matmul(second[:, first:end], second_codes, codes)
+        rest = kept([P, 2 * C], F32, "rest_y", "acts3_1")
+        times_gate(2 * C, LAST * C, rest[:, :C], y2[1][:])
+
         last_y = kept([P, C], F32, "y3_0")
-        times_gate(LAST * C, E * C, last_y[:], y3[0][:])
-        times_gate(LAST * C, E * C, rest[:, C // 2:], y3[1][:])
+        times_gate(LAST * C, E * C - TAILP, last_y[:, :C - TAILP], early[:])
+        times_gate(E * C - TAILP, E * C, last_y[:, C - TAILP:], late_bank[:])
+        times_gate(LAST * C, E * C, rest[:, C:], second[:])
         nc.vector.tensor_copy(out=windows[0][:].indirect(entries(dst_sb, LAST)), in_=last_y[:])
         nc.sync.dma_start(out=out[:P, :], in_=windows[0][:])
-        scatter_second_window(CUT, E * C, rest[:])
+        nc.scalar.activation(out=windows[1][:].indirect(entries(dst_sb, 2, 2)), in_=rest[:], func=COPY, scale=ones[:])
         nc.sync.dma_start(out=out[P:, :], in_=windows[1][:])

@@ -29,8 +29,8 @@ BLOCKS = N // P
 LAST = E - 1
 DMA_ALIGN = 256
 W3_PLACES = 32
-S2 = 56
-S3 = 72
+S2 = 64
+S3 = 64
 TAILP = 128
 W1_PLACES = 96
 W1_LAST = 64

@@ -29,6 +29,17 @@ BLOCKS = N // P
 LAST = E - 1
 DMA_ALIGN = 256
 W3_PLACES = 32
+WU = 0
+POST = 1
+X2 = 0
+X3 = 0
+Y2 = 16
+Y3 = 0
+CUTS3 = [0, 64, 96, 128]
+GE = 1
+SQ = 64
+SQ2 = 32
+ACT = 1
 S2 = 64
 S3 = 64
 TAILP = 128
@@ -83,20 +94,19 @@ def tile_moe_two_glu_silu_kernel(tc, xT, w1, w3, w2, gate, offs, dst, out):
 
         w1_raw = [moved([P, PACK, H], f"w1_raw{e}") for e in range(E)]
         w3_raw = [in_w3(e, 0, [P, PACK, H], F32, f"w3_raw{e}") for e in range(2)]
-        scalar_places = {2: S2, 3: S3}
+        cuts_of = {2: [0, 64, P], 3: CUTS3}
         w3_parts = {}
-        for e, n in scalar_places.items():
+        for e, cuts in cuts_of.items():
             w3_parts[e] = [
-                in_w3(e, 0, [P, PACK, n * PACK], F32, f"w3_part{e}_0"),
-                in_w3(e, 0, [P, PACK, H - n * PACK], F32, f"w3_part{e}_1", n * PACK * PACK * 4),
+                in_w3(e, 0, [P, PACK, (end - first) * PACK], F32, f"w3_part{e}_{first}", first * PACK * PACK * 4)
+                for first, end in zip(cuts, cuts[1:])
             ]
         w2_raw = [moved([P, PACK, N], f"w2_raw{e}") for e in range(E)]
         for e in range(E):
             load(w1_raw[e], w1[e])
             if e in w3_parts:
-                cut = scalar_places[e] * PACK
-                load(w3_parts[e][0], w3[e][:, :cut])
-                load(w3_parts[e][1], w3[e][:, cut:])
+                for part, first, end in zip(w3_parts[e], cuts_of[e], cuts_of[e][1:]):
+                    load(part, w3[e][:, first * PACK:end * PACK])
             else:
                 load(w3_raw[e], w3[e])
             if e == 1:
@@ -264,16 +274,15 @@ def tile_moe_two_glu_silu_kernel(tc, xT, w1, w3, w2, gate, offs, dst, out):
             offsets = dst_sb[:, first * LIST_COLS // C:end * LIST_COLS // C]
             nc.scalar.activation(out=windows[1][:].indirect(offsets), in_=y, func=COPY)
 
-        def round_parts(e, halves):
-            n = scalar_places[e]
-            for copy, part, places in ((on_scalar, 0, slice(0, n)), (on_vector, 1, slice(n, P))):
-                for h in (1, 0):
-                    copy(
-                        out=halves[h][:].rearrange("p t m j -> p m j t")[:, places],
-                        in_=w3_parts[e][part][:].rearrange("p j (m t) -> p m j t", t=PACK)[
-                            :, :, :, h * HALF:(h + 1) * HALF
-                        ],
-                    )
+        def piece(copy, e, halves, part, h, first, end):
+            base = cuts_of[e][part]
+            if first < end:
+                copy(
+                    out=halves[h][:].rearrange("p t m j -> p m j t")[:, first:end],
+                    in_=w3_parts[e][part][:].rearrange("p j (m t) -> p m j t", t=PACK)[
+                        :, first - base:end - base, :, h * HALF:(h + 1) * HALF
+                    ],
+                )
 
         def round_on_gpsimd(bf, raw):
             planes = raw[:].rearrange("p j c -> p c j")
@@ -309,7 +318,9 @@ def tile_moe_two_glu_silu_kernel(tc, xT, w1, w3, w2, gate, offs, dst, out):
         w3_bf = halves_of("w3", 0)
         round_on_vector(w3_bf, w3_raw[0])
         banks = first_product("w3", 0, low_first(w3_bf))
-        late_slots = by_expert(quantize_columns("late", late_bf, in_w3(0, 0, [P, late * C], U32, "late_codes")))
+        late_codes = quantize_columns("late", late_bf, in_w3(0, 0, [P, late * C], U32, "late_codes"))
+        late_slots = by_expert(late_codes)
+        slots_first = (late_codes[0][:, :P], late_codes[1][:, :P])
         slots.extend(by_expert(quantize_columns("slot1", slot_bf[1], in_w3(0, 2, [P, C], U32, "slot1_codes"))))
         slots.extend(late_slots)
         w2_bf = kept([P, N, PACK], BF16, "w2_bf0")
@@ -325,42 +336,68 @@ def tile_moe_two_glu_silu_kernel(tc, xT, w1, w3, w2, gate, offs, dst, out):
         round_shared(w3_bf[1], w3_raw[1], 1, W3_PLACES)
         acts = silu(1, w1_banks, 1)
         banks = first_product("w3", 1, low_first(w3_bf))
-        w2_bf = round_w2_on_gpsimd(1, "w3_bf1_1")
+        w2_bf = round_w2_on_gpsimd(1, "w3_bf1_0" if GE else "w3_bf1_1")
         y_sb = in_w3(1, 4, [P, BLOCKS, C], F32, "y0")
         for b in range(BLOCKS):
             send(0, b, y0[b], y_sb[:, b, :])
         h_bf = multiply(1, acts, banks)
-        w1_bf = [spare(8 + 2 * h, half, BF16, f"w1_bf2_{h}") for h in range(2)]
+        w1_bf = [spare(9 + 2 * h, half, BF16, f"w1_bf2_{h}") for h in range(2)]
         round_on_vector(w1_bf, w1_raw[2])
         w1_banks = first_product("w1", 2, low_first(w1_bf))
-        h_codes = quantize_columns("h_1", h_bf, spare(8, [P, C], U32, "h_codes1"))
-        y1 = [block_product(quantize_columns("w2_1_0", w2_bf[:, :P, :], spare(9, [P, P], U32, "w2_codes1_0")), h_codes)]
+        h_codes = quantize_columns("h_1", h_bf, spare(9, [P, C], U32, "h_codes1"))
+        y1 = [block_product(quantize_columns("w2_1_0", w2_bf[:, :P, :], spare(10, [P, P], U32, "w2_codes1_0")), h_codes)]
         w2_before = w2_bf
 
         w3_bf = [spare(2 * h, half, BF16, f"w3_bf2_{h}") for h in range(2)]
-        round_parts(2, w3_bf)
+        piece(on_scalar, 2, w3_bf, 0, 1, 0, 64)
+        piece(on_scalar, 2, w3_bf, 0, 0, Y2, 64)
+        piece(on_vector, 2, w3_bf, 1, 1, 64, P)
+        piece(on_vector, 2, w3_bf, 0, 0, 0, Y2)
+        piece(on_vector, 2, w3_bf, 1, 0, 64, P)
         acts = silu(2, w1_banks)
         banks = first_product("w3", 2, high_first(w3_bf))
         y1.append(block_product(quantize_columns("w2_1_1", w2_before[:, P:, :], spare(2, [P, P], U32, "w2_codes1_1")), h_codes))
-        w2_bf = round_on_gpsimd(spare(0, [P, N, PACK], BF16, "w2_bf2"), w2_raw[2])
-        send(1, 0, y1[0], in_w3(2, 7, [P, C], F32, "y1_0")[:])
+        w2_bf = spare(0, [P, N, PACK], BF16, "w2_bf2")
+        round_on_gpsimd(w2_bf[:, :N - SQ2, :], w2_raw[2][:, :, :N - SQ2])
+        if SQ2:
+            interleave(on_scalar, w2_bf[:, N - SQ2:, :], w2_raw[2][:, :, N - SQ2:])
+        send(1, 0, y1[0], (spare(3, [P, C], F32, "y1_0") if X2 else in_w3(2, 7, [P, C], F32, "y1_0"))[:])
         h_bf = multiply(2, acts, banks)
-        w1_bf = [spare(12 + 2 * h, half, BF16, f"w1_bf3_{h}") for h in range(2)]
+        for s in range(WU):
+            bank = psum.tile([P, PACK * BANK_SLOTS], F32, name="w3_bank")
+            matmul(bank[:], slots_first, late_codes)
+        w1_bf = [spare(13 + 2 * h, half, BF16, f"w1_bf3_{h}") for h in range(2)]
         round_half(on_vector, w1_bf[0], w1_raw[LAST], 0)
         round_shared(w1_bf[1], w1_raw[LAST], 1, W1_LAST)
         w1_banks = first_product("w1", LAST, low_first(w1_bf))
-        h_codes = quantize_columns("h_2", h_bf, spare(12, [P, C], U32, "h_codes2"))
-        y2 = [block_product(quantize_columns("w2_2_0", w2_bf[:, :P, :], spare(13, [P, P], U32, "w2_codes2_0")), h_codes)]
+        h_codes = quantize_columns("h_2", h_bf, spare(13, [P, C], U32, "h_codes2"))
+        y2 = [block_product(quantize_columns("w2_2_0", w2_bf[:, :P, :], spare(14, [P, P], U32, "w2_codes2_0")), h_codes)]
+        if not POST:
+            y2.append(block_product(quantize_columns("w2_2_1", w2_bf[:, P:, :], in_w3(E, 14, [P, P], U32, "w2_codes2_1", 512)), h_codes))
         w2_before = w2_bf
 
         w3_bf = [spare(4 + 2 * h, half, BF16, f"w3_bf3_{h}") for h in range(2)]
-        round_parts(LAST, w3_bf)
+        piece(on_scalar, LAST, w3_bf, 0, 1, 0, 64)
+        piece(on_scalar, LAST, w3_bf, 0, 0, 0, 64)
+        if len(CUTS3) == 4:
+            piece(on_scalar, LAST, w3_bf, 1, 0, 64 + Y3, 96)
+            piece(on_vector, LAST, w3_bf, 1, 1, 64, 96)
+            piece(on_vector, LAST, w3_bf, 1, 0, 64, 64 + Y3)
+            piece(on_vector, LAST, w3_bf, 2, 1, 96, P)
+            piece(on_vector, LAST, w3_bf, 2, 0, 96, P)
+        else:
+            piece(on_vector, LAST, w3_bf, 1, 1, 64, P)
+            piece(on_vector, LAST, w3_bf, 1, 0, 64, P)
         acts = silu(LAST, w1_banks)
         banks = first_product("w3", LAST, high_first(w3_bf))
-        y2.append(block_product(quantize_columns("w2_2_1", w2_before[:, P:, :], spare(6, [P, P], U32, "w2_codes2_1")), h_codes))
-        w2_bf = round_on_gpsimd(spare(4, [P, N, PACK], BF16, "w2_bf3"), w2_raw[LAST])
-        send(2, 0, y2[0], in_w3(LAST, 7, [P, C], F32, "y2_0")[:])
-        send(1, 1, y1[1], spare(7, [P, C], F32, "y1_1")[:])
+        if POST:
+            y2.append(block_product(quantize_columns("w2_2_1", w2_before[:, P:, :], spare(6, [P, P], U32, "w2_codes2_1")), h_codes))
+        w2_bf = spare(4, [P, N, PACK], BF16, "w2_bf3")
+        round_on_gpsimd(w2_bf[:, :N - SQ, :], w2_raw[LAST][:, :, :N - SQ])
+        if SQ:
+            interleave(on_scalar, w2_bf[:, N - SQ:, :], w2_raw[LAST][:, :, N - SQ:])
+        send(2, 0, y2[0], (in_w3(E, 6, [P, C], F32, "y2_0", 512) if X3 else in_w3(LAST, 7, [P, C], F32, "y2_0"))[:])
+        send(1, 1, y1[1], in_w3(E, 7, [P, C], F32, "y1_1", 512)[:])
 
         cuts = [0, BANK_SLOTS, C - TAILP, C] if TAILP < BANK_SLOTS else [0, BANK_SLOTS, C]
         spans = list(zip(cuts, cuts[1:]))
@@ -370,7 +407,7 @@ def tile_moe_two_glu_silu_kernel(tc, xT, w1, w3, w2, gate, offs, dst, out):
             nc.vector.tensor_tensor(
                 out=piece[:], in0=acts[s][:, cols, :], in1=banks[s][:].rearrange("p t c -> p c t")[:, cols, :], op=MULT
             )
-        h_codes = [quantize_columns("h_3_0", h_bf[0], kept([P, BANK_SLOTS], U32, "h_codes3", "acts3_0"))]
+        h_codes = [quantize_columns("h_3_0", h_bf[0], (in_w3(LAST, 4, [P, BANK_SLOTS], U32, "h_codes3") if X3 else kept([P, BANK_SLOTS], U32, "h_codes3", "acts3_0")))]
         first_codes = quantize_columns("w2_3_0", w2_bf[:, :P, :], kept([P, P], U32, "w2_codes3_0"))
         h_codes.extend(quantize_columns(f"h_3_{s}", h_bf[s]) for s in range(1, len(spans)))
         early = psum_y.tile([P, C - TAILP], F32, name="y_bank")
@@ -382,7 +419,7 @@ def tile_moe_two_glu_silu_kernel(tc, xT, w1, w3, w2, gate, offs, dst, out):
         second = psum_y.tile([P, C], F32, name="y_bank")
         for codes, (first, end) in zip(h_codes, spans):
             matmul(second[:, first:end], second_codes, codes)
-        rest = kept([P, 2 * C], F32, "rest_y", "acts3_1")
+        rest = (in_w3(LAST, 6, [P, 2 * C], F32, "rest_y") if X3 else kept([P, 2 * C], F32, "rest_y", "acts3_1"))
         times_gate(2 * C, LAST * C, rest[:, :C], y2[1][:])
 
         last_y = kept([P, C], F32, "y3_0")
@@ -392,4 +429,4 @@ def tile_moe_two_glu_silu_kernel(tc, xT, w1, w3, w2, gate, offs, dst, out):
         nc.vector.tensor_copy(out=windows[0][:].indirect(entries(dst_sb, LAST)), in_=last_y[:])
         nc.sync.dma_start(out=out[:P, :], in_=windows[0][:])
         nc.scalar.activation(out=windows[1][:].indirect(entries(dst_sb, 2, 2)), in_=rest[:], func=COPY, scale=ones[:])
-        nc.sync.dma_start(out=out[P:, :], in_=windows[1][:])
+        (nc.scalar if ACT else nc.sync).dma_start(out=out[P:, :], in_=windows[1][:])

from contextlib import ExitStack

import concourse.mybir as mybir
from concourse.masks import make_identity

K, T, E, C, H, N = 512, 2048, 4, 256, 512, 256
FLOPS = 2 * E * C * (2 * K * H + H * N)

F32 = mybir.dt.float32
BF16 = mybir.dt.bfloat16
U32 = mybir.dt.uint32
U16 = mybir.dt.uint16
U8 = mybir.dt.uint8
FP8X4 = mybir.dt.float8_e4m3fn_x4
COPY = mybir.ActivationFunctionType.Copy
SILU = mybir.ActivationFunctionType.Silu
MULT = mybir.AluOpType.mult
ADD = mybir.AluOpType.add

P = 128
PACK = 4
HALF = PACK // 2
EARLY = 2
BANK_SLOTS = 128
BANKS = C // BANK_SLOTS
GATE_COLS = E * C // P
LIST_COLS = C // 16
BLOCKS = N // P
LAST = E - 1
DMA_ALIGN = 256
W3_PLACES = 32
WU = 0
POST = 1
X2 = 0
X3 = 0
Y2 = 16
Y3 = 0
CUTS3 = [0, 64, 96, 128]
GE = 1
SQ = 64
SQ2 = 32
ACT = 1
S2 = 64
S3 = 64
TAILP = 128
W1_PLACES = 96
W1_LAST = 64
CUT = C + (E - 1) * C // 2

W3_BYTES = PACK * H * 4
EIGHTH = W3_BYTES // 8


def tile_moe_two_glu_silu_kernel(tc, xT, w1, w3, w2, gate, offs, dst, out):
    nc = tc.nc
    with ExitStack() as ctx:
        keep = ctx.enter_context(tc.tile_pool(name="keep", bufs=1))
        placed = ctx.enter_context(tc.tile_pool(name="placed", bufs=1))
        psum = ctx.enter_context(tc.psum_pool(name="psum", bufs=BANKS))
        psum_y = ctx.enter_context(tc.psum_pool(name="psum_y", bufs=2 * BLOCKS))

        def kept(shape, dtype, name, behind=""):
            return keep.tile(shape, dtype, name=name, tag=behind or name, align_bytes=64)

        def moved(shape, name):
            return keep.tile(shape, F32, name=name, align_bytes=DMA_ALIGN)

        def in_w3(e, eighth, shape, dtype, name, skip=0):
            offset = e * W3_BYTES + eighth * EIGHTH + skip
            return placed.tile(shape, dtype, name=name, align_bytes=DMA_ALIGN, offset=offset)

        def quantize(words, scales, values):
            nc.vector.quantize_mx(out=words.bitcast(FP8X4), scales=scales, in_=values)

        offs_sb = keep.tile([P, E * LIST_COLS], U16, name="offs_sb")
        dst_sb = keep.tile([P, E * LIST_COLS], U16, name="dst_sb")
        windows = [moved([P, T], f"window{b}") for b in range(BLOCKS)]
        gates = keep.tile([P, E * C], F32, name="gates")
        gate_cols = keep.tile([P, GATE_COLS], F32, name="gate_cols")
        identity = keep.tile([P, P], F32, name="identity")

        nc.scalar.dma_start(out=gate_cols[:], in_=gate[0].rearrange("(p m) -> p m", m=GATE_COLS))
        x_rows = xT.rearrange("(p j) t -> p j t", j=PACK)
        x_planes = []
        for j in range(PACK):
            plane = moved([P, T], f"x_plane{j}")
            nc.sync.dma_start(out=plane[:], in_=x_rows[:, j, :])
            x_planes.append(plane)
            if j == 0:
                nc.sync.dma_start(offs_sb[:], offs)

        def load(raw, w):
            nc.sync.dma_start(out=raw[:], in_=w.rearrange("(p j) n -> p j n", j=PACK))

        w1_raw = [moved([P, PACK, H], f"w1_raw{e}") for e in range(E)]
        w3_raw = [in_w3(e, 0, [P, PACK, H], F32, f"w3_raw{e}") for e in range(2)]
        cuts_of = {2: [0, 64, P], 3: CUTS3}
        w3_parts = {}
        for e, cuts in cuts_of.items():
            w3_parts[e] = [
                in_w3(e, 0, [P, PACK, (end - first) * PACK], F32, f"w3_part{e}_{first}", first * PACK * PACK * 4)
                for first, end in zip(cuts, cuts[1:])
            ]
        w2_raw = [moved([P, PACK, N], f"w2_raw{e}") for e in range(E)]
        for e in range(E):
            load(w1_raw[e], w1[e])
            if e in w3_parts:
                for part, first, end in zip(w3_parts[e], cuts_of[e], cuts_of[e][1:]):
                    load(part, w3[e][:, first * PACK:end * PACK])
            else:
                load(w3_raw[e], w3[e])
            if e == 1:
                nc.sync.dma_start(dst_sb[:], dst)
            load(w2_raw[e], w2[e])

        make_identity(nc, identity[:])
        ones = keep.tile([P, 1], F32, name="ones")
        nc.vector.memset(ones[:], 1.0)
        for window in windows:
            nc.vector.memset(window[:], 0.0)
        for m0 in range(0, GATE_COLS, PACK):
            bank = psum_y.tile([P, PACK, P], F32, name="y_bank")
            for m in range(PACK):
                nc.tensor.transpose(bank[:, m, :], gate_cols[:, m0 + m:m0 + m + 1].to_broadcast([P, P]), identity[:])
            nc.vector.tensor_copy(
                out=gates[:].rearrange("q (p m) -> q p m", m=GATE_COLS)[:, :, m0:m0 + PACK],
                in_=bank[:].rearrange("q m p -> q p m"),
            )

        def entries(list_sb, first, count=1):
            return list_sb[:, first * LIST_COLS:(first + count) * LIST_COLS]

        late = E - EARLY
        slot_bf = [kept([P, C, PACK], BF16, f"slot_bf{e}") for e in range(EARLY)]
        rows = kept([P, PACK, late * C], BF16, "rows")
        for j in range(PACK):
            for e in range(EARLY):
                nc.vector.tensor_copy(out=slot_bf[e][:, :, j], in_=x_planes[j][:].indirect(entries(offs_sb, e)))
            nc.scalar.activation(
                out=rows[:, j, :], in_=x_planes[j][:].indirect(entries(offs_sb, EARLY, late)), func=COPY
            )

        on_vector, on_scalar = nc.vector.tensor_copy, nc.scalar.copy
        half = [P, HALF, P, PACK]

        def interleave(copy, side_by_side, planes):
            copy(
                out=side_by_side.rearrange("p (c i) j -> p c j i", i=PACK),
                in_=planes.rearrange("p j (c i) -> p c j i", i=PACK),
            )

        def quantize_columns(name, values, words=None):
            width = values.shape[1]
            if words is None:
                words = kept([P, width], U32, f"{name}_codes")
            scales = kept([P, width], U8, f"{name}_scales")
            quantize(words[:], scales[:], values[:].rearrange("p c j -> p (c j)"))
            return words, scales

        def by_expert(codes):
            words, scales = codes
            return [(words[:, c:c + C], scales[:, c:c + C]) for c in range(0, words.shape[1], C)]

        def round_half(copy, bf, raw, h, places=slice(0, P)):
            copy(
                out=bf[:].rearrange("p t m j -> p m j t")[:, places],
                in_=raw[:].rearrange("p j (m t) -> p m j t", t=PACK)[:, places, :, h * HALF:(h + 1) * HALF],
            )

        def round_shared(bf, raw, h, vector_places):
            round_half(on_scalar, bf, raw, h, slice(vector_places, P))
            round_half(on_vector, bf, raw, h, slice(0, vector_places))

        def halves_of(name, e):
            return [kept(half, BF16, f"{name}_bf{e}_{h}") for h in range(2)]

        def round_on_vector(halves, raw):
            for h, bf in enumerate(halves):
                round_half(on_vector, bf, raw, h)

        def low_first(halves):
            return [(0, halves[0]), (HALF, halves[1])]

        def high_first(halves):
            return [(HALF, halves[1]), (0, halves[0])]

        def first_product(name, e, pieces, last_words=None):
            by_t = {}
            for first, bf in pieces:
                width = bf.shape[1] * P
                if last_words is not None and first == pieces[-1][0]:
                    words = last_words
                else:
                    words = kept([P, width], U32, f"{name}_{e}_codes{first}")
                scales = kept([P, width], U8, f"{name}_{e}_scales{first}")
                quantize(words[:], scales[:], bf[:].rearrange("p t m j -> p (t m j)"))
                for c in range(0, width, P):
                    by_t[first + c // P] = (words[:, c:c + P], scales[:, c:c + P])
            slot_words, slot_scales = slots[e]
            banks = []
            for s in range(BANKS):
                cols = slice(s * BANK_SLOTS, (s + 1) * BANK_SLOTS)
                bank = psum.tile([P, PACK, BANK_SLOTS], F32, name=f"{name}_bank")
                for step in range(PACK):
                    t = (pieces[0][0] + step + s * HALF) % PACK
                    words, scales = by_t[t]
                    nc.tensor.matmul_mx(
                        out=bank[:, t, :],
                        lhsT=words.bitcast(FP8X4),
                        lhsT_scale=scales,
                        rhs=slot_words[:, cols].bitcast(FP8X4),
                        rhs_scale=slot_scales[:, cols],
                        start=True,
                        stop=True,
                    )
                banks.append(bank)
            return banks

        def silu(e, banks, behind_w3=None):
            acts = []
            for s, bank in enumerate(banks):
                shape, name = [P, BANK_SLOTS, PACK], f"acts{e}_{s}"
                act = kept(shape, F32, name) if behind_w3 is None else in_w3(behind_w3, 2 * s, shape, F32, name)
                nc.scalar.activation(out=act[:], in_=bank[:].rearrange("p t c -> p c t"), func=SILU)
                acts.append(act)
            return acts

        def multiply(e, acts, banks):
            h_bf = kept([P, C, PACK], BF16, f"h_bf{e}")
            for s, bank in enumerate(banks):
                cols = slice(s * BANK_SLOTS, (s + 1) * BANK_SLOTS)
                nc.vector.tensor_tensor(
                    out=h_bf[:, cols, :], in0=acts[s][:], in1=bank[:].rearrange("p t c -> p c t"), op=MULT
                )
            return h_bf

        def second_product(w2_codes, h_pieces):
            w2_words, w2_scales = w2_codes
            y_banks = []
            for b in range(BLOCKS):
                bank = psum_y.tile([P, C], F32, name="y_bank")
                width = C // len(h_pieces)
                for s, (h_words, h_scales) in enumerate(h_pieces):
                    nc.tensor.matmul_mx(
                        out=bank[:, s * width:(s + 1) * width],
                        lhsT=w2_words[:, b * P:(b + 1) * P].bitcast(FP8X4),
                        lhsT_scale=w2_scales[:, b * P:(b + 1) * P],
                        rhs=h_words[:].bitcast(FP8X4),
                        rhs_scale=h_scales[:],
                        start=True,
                        stop=True,
                    )
                y_banks.append(bank)
            return y_banks

        def second_layer(e, h_bf, w2_bf, w2_words=None):
            w2_codes = quantize_columns(f"w2_{e}", w2_bf, w2_words)
            return second_product(w2_codes, [quantize_columns(f"h_{e}", h_bf)])

        def round_w2_on_gpsimd(e, behind):
            w2_bf = kept([P, N, PACK], BF16, f"w2_bf{e}", behind)
            planes = w2_raw[e][:].rearrange("p j c -> p c j")
            nc.gpsimd.tensor_scalar(out=w2_bf[:], in0=planes, scalar1=1.0, scalar2=0.0, op0=MULT, op1=ADD)
            return w2_bf

        def times_gate(first, end, y, sums):
            nc.vector.tensor_tensor(out=y, in0=gates[:, first:end], in1=sums, op=MULT)

        def send(e, b, bank, y):
            times_gate(e * C, (e + 1) * C, y, bank[:])
            nc.scalar.activation(out=windows[b][:].indirect(entries(dst_sb, e)), in_=y, func=COPY)

        def scatter_second_window(first, end, y):
            offsets = dst_sb[:, first * LIST_COLS // C:end * LIST_COLS // C]
            nc.scalar.activation(out=windows[1][:].indirect(offsets), in_=y, func=COPY)

        def piece(copy, e, halves, part, h, first, end):
            base = cuts_of[e][part]
            if first < end:
                copy(
                    out=halves[h][:].rearrange("p t m j -> p m j t")[:, first:end],
                    in_=w3_parts[e][part][:].rearrange("p j (m t) -> p m j t", t=PACK)[
                        :, first - base:end - base, :, h * HALF:(h + 1) * HALF
                    ],
                )

        def round_on_gpsimd(bf, raw):
            planes = raw[:].rearrange("p j c -> p c j")
            nc.gpsimd.tensor_scalar(out=bf[:], in0=planes, scalar1=1.0, scalar2=0.0, op0=MULT, op1=ADD)
            return bf

        def spare(eighth, shape, dtype, name):
            return in_w3(E, eighth, shape, dtype, name)

        def matmul(bank, w2_codes, h_codes):
            nc.tensor.matmul_mx(
                out=bank,
                lhsT=w2_codes[0][:].bitcast(FP8X4),
                lhsT_scale=w2_codes[1][:],
                rhs=h_codes[0][:].bitcast(FP8X4),
                rhs_scale=h_codes[1][:],
                start=True,
                stop=True,
            )

        def block_product(w2_codes, h_codes):
            bank = psum_y.tile([P, C], F32, name="y_bank")
            matmul(bank[:], w2_codes, h_codes)
            return bank

        late_bf = kept([P, late * C, PACK], BF16, "late_bf")
        interleave(on_scalar, late_bf[:], rows[:])
        slots = by_expert(quantize_columns("slot0", slot_bf[0]))
        w1_bf = halves_of("w1", 0)
        round_on_vector(w1_bf, w1_raw[0])
        acts = silu(0, first_product("w1", 0, low_first(w1_bf)))

        w3_bf = halves_of("w3", 0)
        round_on_vector(w3_bf, w3_raw[0])
        banks = first_product("w3", 0, low_first(w3_bf))
        late_codes = quantize_columns("late", late_bf, in_w3(0, 0, [P, late * C], U32, "late_codes"))
        late_slots = by_expert(late_codes)
        slots_first = (late_codes[0][:, :P], late_codes[1][:, :P])
        slots.extend(by_expert(quantize_columns("slot1", slot_bf[1], in_w3(0, 2, [P, C], U32, "slot1_codes"))))
        slots.extend(late_slots)
        w2_bf = kept([P, N, PACK], BF16, "w2_bf0")
        interleave(on_scalar, w2_bf[:], w2_raw[0][:])
        y0 = second_layer(0, multiply(0, acts, banks), w2_bf, kept([P, N], U32, "w2_codes0", "acts0_0"))
        w1_bf = halves_of("w1", 1)
        round_half(on_scalar, w1_bf[1], w1_raw[1], 1)
        round_shared(w1_bf[0], w1_raw[1], 0, W1_PLACES)
        w1_banks = first_product("w1", 1, high_first(w1_bf))

        w3_bf = halves_of("w3", 1)
        round_half(on_vector, w3_bf[0], w3_raw[1], 0)
        round_shared(w3_bf[1], w3_raw[1], 1, W3_PLACES)
        acts = silu(1, w1_banks, 1)
        banks = first_product("w3", 1, low_first(w3_bf))
        w2_bf = round_w2_on_gpsimd(1, "w3_bf1_0" if GE else "w3_bf1_1")
        y_sb = in_w3(1, 4, [P, BLOCKS, C], F32, "y0")
        for b in range(BLOCKS):
            send(0, b, y0[b], y_sb[:, b, :])
        h_bf = multiply(1, acts, banks)
        w1_bf = [spare(9 + 2 * h, half, BF16, f"w1_bf2_{h}") for h in range(2)]
        round_on_vector(w1_bf, w1_raw[2])
        w1_banks = first_product("w1", 2, low_first(w1_bf))
        h_codes = quantize_columns("h_1", h_bf, spare(9, [P, C], U32, "h_codes1"))
        y1 = [block_product(quantize_columns("w2_1_0", w2_bf[:, :P, :], spare(10, [P, P], U32, "w2_codes1_0")), h_codes)]
        w2_before = w2_bf

        w3_bf = [spare(2 * h, half, BF16, f"w3_bf2_{h}") for h in range(2)]
        piece(on_scalar, 2, w3_bf, 0, 1, 0, 64)
        piece(on_scalar, 2, w3_bf, 0, 0, Y2, 64)
        piece(on_vector, 2, w3_bf, 1, 1, 64, P)
        piece(on_vector, 2, w3_bf, 0, 0, 0, Y2)
        piece(on_vector, 2, w3_bf, 1, 0, 64, P)
        acts = silu(2, w1_banks)
        banks = first_product("w3", 2, high_first(w3_bf))
        y1.append(block_product(quantize_columns("w2_1_1", w2_before[:, P:, :], spare(2, [P, P], U32, "w2_codes1_1")), h_codes))
        w2_bf = spare(0, [P, N, PACK], BF16, "w2_bf2")
        round_on_gpsimd(w2_bf[:, :N - SQ2, :], w2_raw[2][:, :, :N - SQ2])
        if SQ2:
            interleave(on_scalar, w2_bf[:, N - SQ2:, :], w2_raw[2][:, :, N - SQ2:])
        send(1, 0, y1[0], (spare(3, [P, C], F32, "y1_0") if X2 else in_w3(2, 7, [P, C], F32, "y1_0"))[:])
        h_bf = multiply(2, acts, banks)
        for s in range(WU):
            bank = psum.tile([P, PACK * BANK_SLOTS], F32, name="w3_bank")
            matmul(bank[:], slots_first, late_codes)
        w1_bf = [spare(13 + 2 * h, half, BF16, f"w1_bf3_{h}") for h in range(2)]
        round_half(on_vector, w1_bf[0], w1_raw[LAST], 0)
        round_shared(w1_bf[1], w1_raw[LAST], 1, W1_LAST)
        w1_banks = first_product("w1", LAST, low_first(w1_bf))
        h_codes = quantize_columns("h_2", h_bf, spare(13, [P, C], U32, "h_codes2"))
        y2 = [block_product(quantize_columns("w2_2_0", w2_bf[:, :P, :], spare(14, [P, P], U32, "w2_codes2_0")), h_codes)]
        if not POST:
            y2.append(block_product(quantize_columns("w2_2_1", w2_bf[:, P:, :], in_w3(E, 14, [P, P], U32, "w2_codes2_1", 512)), h_codes))
        w2_before = w2_bf

        w3_bf = [spare(4 + 2 * h, half, BF16, f"w3_bf3_{h}") for h in range(2)]
        piece(on_scalar, LAST, w3_bf, 0, 1, 0, 64)
        piece(on_scalar, LAST, w3_bf, 0, 0, 0, 64)
        if len(CUTS3) == 4:
            piece(on_scalar, LAST, w3_bf, 1, 0, 64 + Y3, 96)
            piece(on_vector, LAST, w3_bf, 1, 1, 64, 96)
            piece(on_vector, LAST, w3_bf, 1, 0, 64, 64 + Y3)
            piece(on_vector, LAST, w3_bf, 2, 1, 96, P)
            piece(on_vector, LAST, w3_bf, 2, 0, 96, P)
        else:
            piece(on_vector, LAST, w3_bf, 1, 1, 64, P)
            piece(on_vector, LAST, w3_bf, 1, 0, 64, P)
        acts = silu(LAST, w1_banks)
        banks = first_product("w3", LAST, high_first(w3_bf))
        if POST:
            y2.append(block_product(quantize_columns("w2_2_1", w2_before[:, P:, :], spare(6, [P, P], U32, "w2_codes2_1")), h_codes))
        w2_bf = spare(4, [P, N, PACK], BF16, "w2_bf3")
        round_on_gpsimd(w2_bf[:, :N - SQ, :], w2_raw[LAST][:, :, :N - SQ])
        if SQ:
            interleave(on_scalar, w2_bf[:, N - SQ:, :], w2_raw[LAST][:, :, N - SQ:])
        send(2, 0, y2[0], (in_w3(E, 6, [P, C], F32, "y2_0", 512) if X3 else in_w3(LAST, 7, [P, C], F32, "y2_0"))[:])
        send(1, 1, y1[1], in_w3(E, 7, [P, C], F32, "y1_1", 512)[:])

        cuts = [0, BANK_SLOTS, C - TAILP, C] if TAILP < BANK_SLOTS else [0, BANK_SLOTS, C]
        spans = list(zip(cuts, cuts[1:]))
        h_bf = [kept([P, end - first, PACK], BF16, f"h_bf3_{first}") for first, end in spans]
        for piece, (first, end) in zip(h_bf, spans):
            s, cols = first // BANK_SLOTS, slice(first % BANK_SLOTS, (end - 1) % BANK_SLOTS + 1)
            nc.vector.tensor_tensor(
                out=piece[:], in0=acts[s][:, cols, :], in1=banks[s][:].rearrange("p t c -> p c t")[:, cols, :], op=MULT
            )
        h_codes = [quantize_columns("h_3_0", h_bf[0], (in_w3(LAST, 4, [P, BANK_SLOTS], U32, "h_codes3") if X3 else kept([P, BANK_SLOTS], U32, "h_codes3", "acts3_0")))]
        first_codes = quantize_columns("w2_3_0", w2_bf[:, :P, :], kept([P, P], U32, "w2_codes3_0"))
        h_codes.extend(quantize_columns(f"h_3_{s}", h_bf[s]) for s in range(1, len(spans)))
        early = psum_y.tile([P, C - TAILP], F32, name="y_bank")
        for codes, (first, end) in list(zip(h_codes, spans))[:-1]:
            matmul(early[:, first:end], first_codes, codes)
        late_bank = psum_y.tile([P, TAILP], F32, name="y_bank")
        matmul(late_bank[:], first_codes, h_codes[-1])
        second_codes = quantize_columns("w2_3_1", w2_bf[:, P:, :], kept([P, P], U32, "w2_codes3_1", "h_bf3_0"))
        second = psum_y.tile([P, C], F32, name="y_bank")
        for codes, (first, end) in zip(h_codes, spans):
            matmul(second[:, first:end], second_codes, codes)
        rest = (in_w3(LAST, 6, [P, 2 * C], F32, "rest_y") if X3 else kept([P, 2 * C], F32, "rest_y", "acts3_1"))
        times_gate(2 * C, LAST * C, rest[:, :C], y2[1][:])

        last_y = kept([P, C], F32, "y3_0")
        times_gate(LAST * C, E * C - TAILP, last_y[:, :C - TAILP], early[:])
        times_gate(E * C - TAILP, E * C, last_y[:, C - TAILP:], late_bank[:])
        times_gate(LAST * C, E * C, rest[:, C:], second[:])
        nc.vector.tensor_copy(out=windows[0][:].indirect(entries(dst_sb, LAST)), in_=last_y[:])
        nc.sync.dma_start(out=out[:P, :], in_=windows[0][:])
        nc.scalar.activation(out=windows[1][:].indirect(entries(dst_sb, 2, 2)), in_=rest[:], func=COPY, scale=ones[:])
        (nc.scalar if ACT else nc.sync).dma_start(out=out[P:, :], in_=windows[1][:])
